import numpy as np, ml_dtypes
CORES = [2,6,10,14,18,22,26,30]
N = 8
import mx_ref
BF = ml_dtypes.bfloat16
def pick(q, e):
    c = np.concatenate([q[0].reshape(128, -1, 4), np.zeros((128, 1, 4), np.uint8)], axis=1); s = np.concatenate([q[1], np.ones((16, 1), np.uint8)], axis=1)
    return (np.ascontiguousarray(c[:, e].reshape(128, -1)), np.ascontiguousarray(s[:, e]))
def join(*qs):
    return (np.concatenate([q[0] for q in qs], axis=1), np.concatenate([q[1] for q in qs], axis=1))
def put(q, e, v):
    c, s = q[0].reshape(128, -1, 4).copy(), q[1].copy(); c[:, e] = v[0].reshape(128, -1, 4); s[:, e] = v[1]
    return (c.reshape(128, -1), s)
def pk(c, s):
    return (np.ascontiguousarray(c), mx_ref.live(s))
def emit(q):
    return q[0], q[1]
def decode(q):
    o = []
    for b in range(4):
        e = np.zeros((128, 128, 4), np.float32); e[np.arange(128), np.arange(128), b] = 1
        o.append(mx_ref.matmul(mx_ref.quantize(e.reshape(128, 512).astype(BF)), q))
    return np.stack(o, axis=2).reshape(128, -1)
def f(rng, *shape):
    return mx_ref.flush((rng.standard_normal(shape, dtype=np.float32) * np.exp2(rng.integers(-2, 3, shape[:-1] + (1,)))).astype(BF))
def wide(rng, *shape, cols=0):
    v = rng.standard_normal(shape, dtype=np.float32) * np.exp2(rng.integers(-12, 13, shape)).astype(np.float32)
    if cols: v *= np.repeat(np.exp2(rng.integers(-cols, cols + 1, shape[:-2] + (1, shape[-1] // 4))) * (rng.random(shape[:-2] + (1, shape[-1] // 4)) > 0.0625), 4, axis=-1).astype(np.float32)
    return mx_ref.flush(v.astype(BF))
P, CAP, M, S = 24, 12, 64, 48
def big(v):
    v = np.array(v, np.float32)
    v[np.abs(v) < np.float32(2.0 ** -16)] = 0
    return v.astype(BF)
def setup_inputs(rng):
    u = big(f(rng, N, 128, 512))
    u[:, :, 8:] = 0
    return {"r0": big(f(rng, N, 128, 4 * P)), "r1": big(f(rng, N, 128, 16 * P)), "r2": big(f(rng, N, 128, 64 * P)), "u": u, "w": f(rng, N, 128, 512)}
def setup_inputs_far(rng):
    d = setup_inputs(rng)
    low = rng.permutation(N) < N // 2
    i = np.arange(128)
    side = np.where(i < 48, -1, np.where(i < 80, 0, 1))
    o, c = rng.permutation(N), rng.permutation(N // 2 * P)[:M // 8]
    kind = np.full((N, P), -1)
    kind[o[:N // 2], rng.integers(0, P, N // 2)] = 0
    kind[o[N // 2 + c // P], c % P] = 1
    on = (side[None, :, None] == 0) | (side[None, :, None] == kind[:, None, :])
    for k, m in (("r0", on), ("r1", np.repeat(on | (kind != 0)[:, None, :], 4, axis=2))):
        v = (1.5 + 0.5 * rng.random((N, 128, m.shape[2], 4))) * 2.0 ** 26
        d[k] = big((v * m[:, :, :, None]).reshape(N, 128, -1))
    g = np.where(low[:, None], -1, side[None, :])
    d["u"][:, :, :4] = big((1.875 + 0.125 * rng.random((N, 128, 4))) * 2.0 ** 29 * g[:, :, None])
    h = d["u"][:, :, 4:8].astype(np.float32) * (side == 0)[None, :, None]
    d["u"][:, :, 4:8] = big(np.where(low[:, None, None], (1.875 + 0.125 * rng.random((N, 128, 4))) * 2.0 ** 26, h))
    return d
def setup_inputs_near(rng):
    d = setup_inputs(rng)
    t = N * np.arange(P)[None, :] + rng.permutation(N)[:, None]
    a, b, u = np.zeros((N, 128, P, 4), np.float32), np.zeros((N, 128, 4 * P, 4), np.float32), np.zeros((N, 128, 512), np.float32)
    a[:, :64] = rng.integers(4, 8, (64, 4))[None, :, None, :]
    for i in range(3): a[:, 64, :, i] = t // 8 ** i % 8
    b[:, 64, :, 3] = np.arange(4 * P) % 4
    a[:, 72:] = f(rng, N, 56, 4 * P).astype(np.float32).reshape(N, 56, P, 4)
    b[:, 72:] = f(rng, N, 56, 16 * P).astype(np.float32).reshape(N, 56, 4 * P, 4)
    u[:, :64, :4] = 1024 * rng.integers(4, 8, (N, 64, 4))
    u[:, 64, :4] = np.array([4, 32, 256, 1])[None, :] * (1 - 2 * (np.arange(N) % 2))[:, None]
    u[:, 72:, 4:8] = f(rng, N, 56, 4).astype(np.float32)
    return {**d, "r0": big(a.reshape(N, 128, -1)), "r1": big(b.reshape(N, 128, -1)), "u": big(u)}
def setup_inputs_pile(rng):
    d = setup_inputs(rng)
    of = np.arange(128) // (128 // N)
    a, b = np.zeros((N, N)), np.full((N, N), 4.0)
    for r in range(N):
        o = rng.permutation(N)
        o = o[o != r]
        o = np.concatenate([[r], o]) if r % 2 == 0 else np.concatenate([o, [r]])
        a[r, o] = 2.0 ** (10 - 2 * np.arange(N))
        b[r, o[(M - 1) // P]] = 2.0 ** 14
    d["r0"] = big((1 + rng.random((N, 128, 4 * P))) * a[of].T[:, :, None])
    d["r1"] = big((1 + rng.random((N, 128, 16 * P))) * b[of].T[:, :, None])
    d["u"][:, :, :4] = big((1 + rng.random((N, 128, 4))) * (of[None, :] == np.arange(N)[:, None])[:, :, None])
    return d
def setup_inputs_spread(rng):
    d = setup_inputs(rng)
    a = wide(rng, N, 128, 4 * P, cols=6).astype(np.float32).reshape(N, 128, P, 4)
    b = wide(rng, N, 128, 16 * P, cols=6).astype(np.float32).reshape(N, 128, 4 * P, 4)
    c = wide(rng, N, 128, 64 * P, cols=6).astype(np.float32).reshape(N, 128, 16 * P, 4)
    for q in range(N):
        n = rng.permutation(P)[:2]
        x = (1 + rng.random((128, 1, 4))) * 2.0 ** 26 * rng.choice([-1.0, 1.0], (128, 1, 4))
        a[q][:, n] = np.concatenate([x, -x], axis=1)
        b[q][:, 4 * n] = -a[q][:, n]
        b[q][:, 4 * n + 1] = 0
        c[q][:, 4 * (4 * n + 1)] = -a[q][:, n]
    return {**d, "r0": big(a.reshape(N, 128, -1)), "r1": big(b.reshape(N, 128, -1)), "r2": big(c.reshape(N, 128, -1))}
def setup_inputs_ties(rng):
    d = setup_inputs(rng)
    x = np.abs(big(f(rng, 128, 4)).astype(np.float32))
    a = np.ones((N, P), np.float32)
    for q in range(N): a[q, 1 + rng.permutation(P - 1)[:M // 2 // N]] = 2
    b = np.where(np.arange(4)[None, None, :] == rng.integers(0, 4, (N, P))[:, :, None], 3 - a[:, :, None], 0.125).reshape(N, 4 * P)
    d["r0"] = big((x[None, :, None, :] * a[:, None, :, None]).reshape(N, 128, -1))
    d["r1"] = big((x[None, :, None, :] * b[:, None, :, None]).reshape(N, 128, -1))
    d["u"][:, :, :4] = np.abs(d["u"][:, :, :4].astype(np.float32)).astype(BF)
    return d
def check_inputs(d):
    b = []
    def bad(v, lo, hi):
        v = np.abs(v.astype(np.float32))
        return not (np.isfinite(v).all() and ((v == 0) | (v >= lo) & (v <= hi)).all())
    for k in ("u", "w"):
        if bad(d[k], 2.0 ** -30, 2.0 ** 30): b.append("a value of " + k)
    for k in ("r0", "r1", "r2"):
        if bad(d[k], 2.0 ** -16, 2.0 ** 27): b.append("a value of " + k)
    if bad(d["u"][:, :, 4:8], 2.0 ** -16, 2.0 ** 27): b.append("a value of column 1 of u")
    if (d["u"][:, :, 8:].astype(np.float32) != 0).any(): b.append("u has numbers behind its first 2 columns")
    return b
def take(s, own):
    s = s + np.float32(0.0)
    at = np.flatnonzero(own >= 0)
    best = at[np.argsort(-s[at], kind="stable")][:M]
    got = np.full((N, CAP), -1)
    for q in range(N):
        k = best[own[best] == q][:CAP]
        got[q, :k.size] = k
    return got
def held(q, e):
    return decode(pick(q, np.concatenate([e, np.full(-len(e) % 4, -1)]))).reshape(128, -1, 4)[:, :len(e)]
def reference(r0, r1, r2, u, w):
    y, nm = np.zeros((N, 128, 2 * N * S), np.float32), np.full((N, 1, 2 * N * S), -1, np.float32)
    oc, osc = np.zeros((N, 128, 4 * N * S), np.uint8), np.zeros((N, 16, N * S), np.uint8)
    roots = join(*[mx_ref.quantize(np.ascontiguousarray(r0[q])) for q in range(N)])
    res = [join(*[mx_ref.quantize(np.ascontiguousarray(a[q])) for q in range(N)]) for a in (r1, r2)]
    to = np.arange(N * S) // S
    for r in range(N):
        uq, wq = mx_ref.quantize(np.ascontiguousarray(u[r])), mx_ref.quantize(np.ascontiguousarray(w[r]))
        shift = held(uq, np.arange(1, 2))[:, 0]
        pool, own, num = roots, np.repeat(np.arange(N), P), np.tile(np.arange(P), N)
        for t in range(2):
            parent = np.repeat(take(mx_ref.matmul(uq, pool)[0], own).reshape(-1), 4)
            on = np.flatnonzero(parent >= 0)
            new = np.full(N * S, -1)
            new[on] = 4 * num[parent[on]] + on % 4
            e, back = np.unique(parent[on], return_inverse=True)
            v = np.zeros((128, N * S, 4), np.float32)
            v[:, on] = (held(pool, e)[:, back] + held(res[t], 4 ** (t + 1) * P * to[on] + new[on])) + shift[:, None, :]
            pool, own, num = mx_ref.quantize(np.ascontiguousarray(v.reshape(128, -1).astype(BF))), np.where(parent >= 0, to, -1), new
            i = t * N * S
            y[r, :, i:i + N * S] = mx_ref.matmul(wq, pool)
            nm[r, 0, i:i + N * S] = num
        oc[r], osc[r] = emit(pool)
    return {"y": y, "oc": oc, "osc": osc, "nm": nm}

@@ -1,0 +1,604 @@
+from concourse.bass import DstId, RemoteDMATransfer
+from concourse.mybir import dt, AluOpType, AxisListType, ActivationFunctionType
+
+Op, Act = AluOpType, ActivationFunctionType
+N, P, CAP, M, S = 8, 24, 12, 64, 48
+B0 = P + 2
+Z0 = 6
+NL = Z0 + N * B0
+NO = (N - 1) * B0
+NP = N * S
+EPS, BIG, UP = 1e-37, 1e29, 2.0 ** 72
+RELAY = 0
+PARTS = ((4, 8), (0, 4))
+
+F, BF, I32, U16, C, SC = "float32", "bfloat16", "int32", "uint16", "float8_e4m3fn_x4", "uint8"
+SCRATCH = {}
+
+
+def _sb(dtype, **kw):
+    for name, n in kw.items():
+        SCRATCH[name] = ("sbuf", [128, n], dtype)
+
+
+_sb(BF, T0=512, T1=512, T2=4 * NP, TW=512, TE=2048, H=3 * NP, X1=4 * NP, X2=4 * NP, ID=128,
+    R32=64, R48=144, TH0=64, TH1=144, THG=NO, THA=NP, IR=NP, D0=64, CM0=64, SN0=64, SG=NO, CG=NO, JK=NO,
+    D1=144, CM1=144, SN1=144, VS=NP, VM=NP, TM=NP, DA=NP, CA=NP)
+for _n, _w in dict(Q0=128, Q1=128, Q2=NP, QW=128, QE=512, LC=NL, WQ=128, WM=128, V0=128, C1=NP, PV=NP, PE=NP,
+                   C2=NP, L1=NP, L2=NP + 16, OC=NP, RL=NP // 2).items():
+    _sb(C, **{_n + "c": _w})
+    _sb(SC, **{_n + "s": _w})
+_sb(F, J=128, CF=10, A0=NP, DH=32, AF=192, MG=64, ML=64, IRB=NP, Z=NP, AM=NP, YS=2 * NP, NM=64, NN=64, NT=64)
+_sb(I32, PI=1, CI=10, FA=64, LI=48, U=48, DI=48, PJ=2)
+_sb(U16, OU=88, OL0=2, OL1=4, L0=24, L0b=26, LV=24, LE=24, OP=2, OG=2, OZ=2, OI=4, LP=24, LQ=24, O96=6, LT=24)
+for _k in range(8):
+    SCRATCH["P%d" % _k] = ("psum", [128, 512], F)
+PIECE = {}
+for _b, _d in (("K", dict(JM=256, DM=256, R16=256, CD=16, OF=64, RW=256, RM=256, RS=256, TB0=64, TT0=64, TE0=64, TB1=144,
+                          PY0=32, PYB=48, PYC=48, LM0=32, LM1=32, TA8=8, TA9=8, TAa=8, M64=64, ADJ=8, AD2=16, ILB=24,
+                          IL=32, PLZ=24, I96=96, ILT=24)),
+               ("WA", dict(M0=32, BS0=32, SR0=32, AS=32, SS=32, MS=16, NS=8, CN0=8, FL0=32, FT0=32, VL=48, PEN=48, CC=8,
+                           G0=96, GT0=96, A1=48, M1=48, BS1=48, PA=48, PB=48, SR1=48, G1=96, GT1=96)),
+               ("WB", dict(DF=48, NA=24, NB=24, V1=24, PM=64, PC=8, GI=16, SI=8, CN1=8, FL1=32, FT1=32, FS1=32,
+                           C1A=16, TK=32, LZ=24, F96=96))):
+    _at = 0
+    for _n, _w in _d.items():
+        PIECE[_n] = (_b, _at, _w)
+        _at += _w
+    _sb(F, **{_b: _at})
+
+POOL = {"v": 48, "a": 36, "p": 20, "g": 18, "d": 20}
+SEMAPHORES = ["e1", "p1", "p2", "ms", "rc", "rs", "sent"] + ["x%s%d" % (q, i) for q, n in POOL.items() for i in range(n)]
+
+
+def _mask(engines):
+    m = 0
+    for e in engines:
+        m |= 1 << e
+    return m
+
+
+def _deal(engines, sizes):
+    out, at = [], 0
+    for s in sizes:
+        out.append(engines[at:at + s])
+        at += s
+    return out
+
+
+def _plan(T, topo):
+    cores = list(T.cores)
+    plan = {}
+    for r, c in enumerate(cores):
+        off = [q for q in range(N) if topo.chip(cores[q]) != topo.chip(c)]
+        plane = [q for q in off if topo.same_plane(topo.chip(c), topo.chip(cores[q]))]
+        far = [q for q in off if q not in plane]
+        far.sort(key=lambda q: (topo.mates(topo.chip(c), topo.chip(cores[q])), topo.die(cores[q]) == topo.die(c)))
+        plane.sort(key=lambda q: topo.die(cores[q]) == topo.die(c))
+        peer = [q for q in range(N) if q != r and q not in off]
+        free = [h for h in topo.cores_of(c) if topo.die(h) == topo.die(c) and h not in cores]
+        ha = [h for h in free if all(topo.may_write(h, cores[q]) for q in far)][0]
+        hb, hc = [h for h in free if h != ha]
+        serve = {0: {}, 1: {ha: (4, 5, 6, 7), hb: (2, 3, 1)}, 2: {hb: (2,), hc: (3,)}}[RELAY]
+        plan[r] = dict(slots=[r] + peer + plane + far, ha=ha, hb=hb, hc=hc, serve=serve)
+    return plan
+
+
+def _engines(topo, src, off_dst, on_dst):
+    off = topo.engines(src, off_dst)
+    return off, [e for e in topo.engines(src, on_dst) if e not in off]
+
+
+OFF = (4, 5, 6, 7, 2, 3)
+ENG_MS = (0, 2, 2, 2, 1, 1, 1, 1)
+ENG_D = ((0, 2, 2, 2, 1, 1, 1, 1), (0, 2, 1, 1, 2, 2, 1, 1))
+ENG_P1 = {0: ENG_D, 1: ((0, 4, 4, 4, 2, 2, 2, 2),) * 2, 2: ((0, 2, 8, 8, 2, 2, 2, 2),) * 2}[RELAY]
+ENG_P2 = ((0, 2, 2, 2, 2, 2, 2, 2), (0, 2, 4, 4, 2, 2, 2, 2)) if len(PARTS) == 2 else ENG_D
+
+
+def _dst(topo, c):
+    rid, pid, _ = topo.addr(c)
+    return DstId(rid=rid, pnc=pid)
+
+
+def _u8(v):
+    return v.bitcast(dt.uint8)
+
+
+def _u32(v):
+    return v.bitcast(dt.uint32)
+
+
+def _same(v):
+    return v
+
+
+def _helper(g, core, T, topo, plan):
+    cores = list(T.cores)
+    for r in range(N):
+        ks = plan[r]["serve"].get(core)
+        if ks is None:
+            continue
+        slots = plan[r]["slots"]
+        off, on = _engines(topo, core, cores[slots[ks[0]]], cores[r])
+        eng = _deal(off + on, [ENG_P1[0][k] for k in ks])
+        total = 0
+        for sem, src, dst, cast in (("rc", T.RLc, T.L1c, _u8), ("rs", T.RLs, T.L1s, _same)):
+            g.wait_ge(T.sem[sem], 8 if RELAY == 1 else 2)
+            at = [S * (k % 4) if RELAY == 1 else 0 for k in ks]
+            g.remote_dma_fused([RemoteDMATransfer(
+                dst_ids=[_dst(topo, cores[slots[k]])], dma_engine_mask=_mask(e), remote_sem=T.sem.p1,
+                srcs=[cast(src[:, a:a + S])], dsts=[cast(dst[:, S * r:S * (r + 1)])])
+                for k, a, e in zip(ks, at, eng)], local_sem=T.sem.sent)
+            total += sum(len(e) for e in eng)
+        g.wait_ge(T.sem.sent, total)
+
+
+def rank_program(g, core, T, topo):
+    plan = _plan(T, topo)
+    me = T.rank_of(core)
+    if me is None:
+        _helper(g, core, T, topo, plan)
+        return
+    cores = list(T.cores)
+    slots = plan[me]["slots"]
+    slot_at = [plan[q]["slots"].index(me) for q in range(N)]
+    off, on = _engines(topo, core, cores[slots[7]], cores[slots[1]])
+    V, A, PE, SY = g.vector, g.scalar, g.tensor, g.sync
+    queues = {"v": V, "a": A, "p": PE, "g": g, "s": SY}
+
+    def W(name, a=0, b=None, step=1):
+        buf, at, n = PIECE[name]
+        return T[buf][:, at + a:at + (n if b is None else b):step]
+
+    def Wc(name, j=0):
+        return W(name, j, j + 1)
+
+    ops, writer, readers = [], {}, {}
+
+    def op(q, fn, r="", w="", arrive=(), dma=False, acc=False):
+        i, deps = len(ops), set()
+        for key in r.split():
+            deps.update(writer.get(key, ()))
+            if key[0] == "P" and key[1:].isdigit():
+                deps.update(d for d in readers.get(key, ()) if ops[d]["q"] != q)
+        for key in w.split():
+            if not acc:
+                deps.update(writer.get(key, ()))
+            deps.update(readers.get(key, ()))
+        for key in r.split():
+            readers.setdefault(key, []).append(i)
+        for key in w.split():
+            writer[key] = [i]
+            readers[key] = []
+        ops.append(dict(q=q, fn=fn, deps=sorted(deps, reverse=True), arrive=arrive, dma=dma))
+
+    def ts(out, in0, s1, s2, o0, o1, r, w):
+        if s2 is None:
+            op("v", lambda: V.tensor_scalar(out, in0, s1, None, o0), r, w)
+        else:
+            op("v", lambda: V.tensor_scalar(out, in0, s1, s2, o0, o1), r, w)
+
+    def tt(out, in0, in1, o, r, w, arrive=()):
+        op("v", lambda: V.tensor_tensor(out, in0, in1, o), r, w, arrive)
+
+    def cp(out, in_, r, w, arrive=()):
+        op("v", lambda: V.tensor_copy(out, in_), r, w, arrive)
+
+    def ms(ap, val, w, r=""):
+        op("v", lambda: V.memset(ap, val), r, w)
+
+    def scan(out, reset, data, r, w):
+        op("v", lambda: V.tensor_tensor_scan(out, reset, data, 0.0, Op.mult, Op.add), r, w)
+
+    def red(out, in_, r, w, negate=False):
+        op("v", lambda: V.tensor_reduce(out, in_, AxisListType.X, Op.add, negate=negate), r, w)
+
+    def tr(out, in_, r, w):
+        op("v", lambda: V.transpose(out, in_), r, w)
+
+    def act(out, in_, r, w, func=Act.Identity, arrive=(), **kw):
+        op("a", lambda: A.activation(out, in_, func, **kw), r, w, arrive)
+
+    def quant(name, a, b, tile, r, w):
+        op("v", lambda: V.quantize_mx(T[name + "c"][:, a:b], T[name + "s"][:, a:b], tile[:, 4 * a:4 * b]), r, w)
+
+    def mm(bank, lhs, la, rhs, a, b, r, start=True, stop=True, arrive=()):
+        op("p", lambda: PE.matmul_mx(T[bank][:, 0:b - a], T[lhs + "c"][:, la:la + 128], T[lhs + "s"][:, la:la + 128],
+                                     T[rhs + "c"][:, a:b], T[rhs + "s"][:, a:b], start, stop),
+           r, bank, arrive, acc=not start)
+
+    def pick(dst, a, b, src, offs, r, w, arrive=()):
+        cp(_u32(T[dst + "c"][:, a:b]), _u32(T[src + "c"][:]).indirect(offs), r, w + "c", arrive)
+        act(T[dst + "s"][:, a:b], T[src + "s"][:].indirect(offs), r.replace("c ", "s "), w + "s", Act.Copy, arrive)
+
+    def dma(q, out, in_, r, w, arrive=()):
+        op(q, lambda: queues[q].dma_start(out, in_), r, w, arrive, dma=True)
+
+    def iota(out, pattern, w, r=""):
+        op("g", lambda: g.iota(out, pattern, 0, 0, allow_small_or_imprecise_dtypes=True), r, w)
+
+    sent = [0]
+
+    def remote(transfers, r):
+        sent[0] += sum(len(t[2]) for t in transfers)
+        op("g", lambda: g.remote_dma_fused([RemoteDMATransfer(
+            dst_ids=[_dst(topo, c) for c, _ in d], dma_engine_mask=_mask(e), remote_sem=T.sem[sem],
+            srcs=[s], dsts=[x for _, x in d]) for s, d, e, sem in transfers], local_sem=T.sem.sent), r, "")
+
+    def direct(src, dst, cast, w, ks, sizes, sem, first=0):
+        far = [k for k in OFF if k in ks]
+        eng = dict(zip(far, _deal(off[len(off) - sum(sizes[k] for k in far):], [sizes[k] for k in far])))
+        eng[1] = on[first:first + sizes[1]]
+        return [(cast(src[:, w * k:w * (k + 1)]), [(cores[slots[k]], cast(dst[:, w * me:w * (me + 1)]))], eng[k], sem)
+                for k in ks if k]
+
+    def spread(buf, base, w, key):
+        def mv(po, pi, n, a, b, r, wr):
+            cp(buf[po:po + n, base + a:base + b], buf[pi:pi + n, base + a:base + b], r, wr)
+        mv(0, 32, 32, w, 2 * w, key, key + ".a")
+        mv(32, 0, 32, 0, w, key, key + ".b")
+        mv(64, 96, 32, 3 * w, 4 * w, key, key + ".c")
+        mv(96, 64, 32, 2 * w, 3 * w, key, key + ".d")
+        mv(64, 0, 64, 0, 2 * w, "%s %s.a %s.b" % (key, key, key), key + ".e")
+        mv(0, 64, 64, 2 * w, 4 * w, "%s %s.c %s.d" % (key, key, key), key + ".f")
+        return " ".join(key + x for x in ("", ".a", ".b", ".c", ".d", ".e", ".f"))
+
+    def col(buf, j):
+        return buf[:, j:j + 1]
+
+    def arrivals(sem, *sizes):
+        return ((sem, sum(s[slot_at[q]] for s in sizes for q in range(N))),)
+
+    ca, cg, cs, ck, ch, cg4, ca1, cpp, ca7 = (col(T.CF, j) for j in range(9))
+    oWQ, oWM, oV0, oG = T.OU[:, 0:8], T.OU[:, 8:16], T.OU[:, 16:24], T.OU[:, 24:30]
+    oA1, oPN, oC1, oJ4 = T.OU[:, 32:35], T.OU[:, 36:39], T.OU[:, 30:31], T.OU[:, 64:67]
+    oH = T.OU[:, 40:64]
+    oF, oMG, oUN, oTK = T.OU[:, 72:74], T.OU[:, 76:80], T.OU[:, 80:83], T.OU[:, 84:86]
+
+    dma("s", T.T0[:, 4 * Z0:4 * (Z0 + P)], T.r0[:], "", "T0a")
+    dma("a", T.T0[:, 4 * (Z0 + P):128], T.u[:, 0:8], "", "T0b")
+    dma("s", T.T1[:, 0:16 * P], T.r1[:], "", "T1a")
+    dma("s", T.T2[:], T.r2[:], "", "T2")
+    op("g", lambda: g.iota(T.PI[:], [[0, 1]], 0, 1), "", "PI")
+    iota(T.J[:], [[1, 128]], "J")
+    iota(W("JM"), [[0, 16], [1, 16]], "JM")
+    iota(W("TB0"), [[-16, 2], [1, 32]], "TB0")
+    iota(W("PY0"), [[2048, 32]], "PY0")
+    ms(T.T0[:, 0:4 * Z0], 0.0, "T0d")
+    ms(T.T0[:, 128:512], 0.0, "T0c")
+    ms(T.T1[:, 16 * P:512], 0.0, "T1b")
+    ms(T.TE[:], 0.0, "TE")
+    ms(W("OF"), 0.0, "OF")
+    ms(W("RW"), 0.0, "RW")
+    for j, (s1, s2) in enumerate(((0, 15), (4, 7), (2, 3), (0, 3))):
+        ts(col(T.CI, j), T.PI[:], s1, s2, Op.logical_shift_right, Op.bitwise_and, "PI", "CI%d" % j)
+    quant("Q0", 0, 128, T.T0, "T0a T0b T0c T0d", "Q0")
+    for j, (s1, s2) in enumerate(((4, 1), (4, 3), (0, 1), (0, 127), (0, 7)), 4):
+        ts(col(T.CI, j), T.PI[:], s1, s2, Op.logical_shift_right, Op.bitwise_and, "PI", "CI%d" % j)
+    cp(T.CF[:, 0:9], T.CI[:, 0:9], " ".join("CI%d" % j for j in range(9)), "CF")
+
+    for j, (src, dst, cast) in enumerate(((T.Q0c, T.LCc, _u8), (T.Q0s, T.LCs, _same))):
+        land = [(cores[q], cast(dst[:, Z0 + B0 * slot_at[q]:Z0 + B0 * (slot_at[q] + 1)])) for q in slots]
+        remote([(cast(src[:, Z0:Z0 + B0]), [land[k] for k in OFF], off, "e1"),
+                (cast(src[:, Z0:Z0 + B0]), land[1:2], on[j:j + 1], "e1")], "Q0")
+    E1 = (("e1", 2 * (6 * len(off) + 1)),)
+    dma("s", T.TW[:], T.w[:], "", "TW", E1)
+
+    iota(W("RW", 0, 48), [[0, 8], [16, 2], [32, 3]], "RW0", "RW")
+    for k in range(2):
+        op("g", lambda k=k: g.iota(W("RW", 64 + 3 * k, 128, 8), [[3, 8]], 32 * k, 0, allow_small_or_imprecise_dtypes=True),
+           "RW", "RX%d" % k)
+    iota(W("RW", 128, 176), [[3, 2], [8, 8], [1, 3]], "RW2", "RW")
+    iota(W("RW", 192, 240), [[1, 16], [0, 3]], "RW3", "RW")
+    iota(W("OF", 40, 64), [[1, 8], [0, 3]], "OFh", "OF")
+    iota(W("TB1"), [[-16, 3], [1, 48]], "TB1")
+    iota(W("PYB"), [[4, 12], [513, 4]], "PYB")
+    iota(W("ILB"), [[0, 8], [4, 3]], "ILB")
+    iota(W("I96"), [[1, 12], [0, 8]], "I96")
+    iota(W("ILT"), [[1, 8], [32, 3]], "ILT")
+    iota(T.IR[:], [[0, 8], [1, 12], [0, 4]], "IR")
+
+    ts(T.ID[:], T.J[:], cpp, None, Op.is_equal, None, "J CF", "ID")
+    act(W("OF", 0, 8), T.J[:, 0:8], "J OF", "OF0", scale=float(B0), bias=float(Z0 + P))
+    act(W("OF", 8, 16), T.J[:, 0:8], "J OF", "OF1", scale=0.0, bias=float(Z0 + P))
+    act(W("OF", 24, 30, 2), T.J[:, 0:3], "J OF CF", "OF3", scale=4.0, bias=cs)
+    act(W("OF", 25, 30, 2), T.J[:, 0:3], "J OF CF", "OF4", scale=4.0, bias=cs)
+    act(W("OF", 30, 31), ca1, "OF CF", "OF5", scale=16.0, bias=15.0)
+    for b in range(4):
+        cp(T.TE[:, 512 * b + b:512 * (b + 1):4], T.ID[:], "ID TE", "TE%d" % b)
+    ts(Wc("CD", 0), cg4, 48.0, ca, Op.mult, Op.add, "CF", "CD0")
+    ts(Wc("CD", 1), ch, 16.0, cs, Op.mult, Op.add, "CF", "CD1")
+    ts(Wc("CD", 14), cs, float(Z0), None, Op.add, None, "CF", "CD14")
+    ts(Wc("CD", 2), cg, 48.0, None, Op.mult, None, "CF", "CD2")
+    ts(Wc("CD", 3), ca, 8.0, None, Op.is_ge, None, "CF", "CD3")
+    ts(Wc("CD", 4), ca, float(CAP), None, Op.is_lt, None, "CF", "CD4")
+    ts(Wc("CD", 5), ca, -1.0, float(M), Op.mult, Op.add, "CF", "CD5")
+    ts(Wc("CD", 6), ck, 3.0, None, Op.is_lt, None, "CF", "CD6")
+    ts(Wc("CD", 7), ck, 4.0, cs, Op.mult, Op.add, "CF", "CD7")
+    ts(T.OI[:], T.J[:, 0:4], 16.0, ca, Op.mult, Op.add, "J CF", "OI")
+    ts(T.OZ[:], T.J[:, 0:2], 0.0, None, Op.mult, None, "J", "OZ")
+    ts(T.OU[:, 64:68], T.J[:, 0:4], 4.0, cs, Op.mult, Op.add, "J CF", "OUd")
+    act(W("OF", 16, 24), T.J[:, 0:8], "J OF CD14", "OF2", scale=4.0, bias=Wc("CD", 14))
+    act(W("OF", 32, 35), T.J[:, 0:3], "J OF CD0", "OF6", scale=16.0, bias=Wc("CD", 0))
+    act(W("OF", 36, 39), T.J[:, 0:3], "J OF CD1", "OF7", scale=4.0, bias=Wc("CD", 1))
+    act(Wc("CD", 8), cg, "CF", "CD8", scale=8.0, bias=ck)
+    act(Wc("CD", 9), ck, "CF", "CD9", bias=1.0)
+    act(Wc("CD", 10), ca, "CF", "CD10", bias=-float(NP))
+    act(Wc("CD", 11), Wc("CD", 7), "CD7", "CD11", scale=-1.0, bias=float(M))
+    act(Wc("CD", 13), cs, "CF", "CD13", Act.Copy, scale=8.0)
+    quant("QE", 0, 512, T.TE, "TE TE0 TE1 TE2 TE3", "QE")
+    cp(T.OU[:, 0:32], W("OF", 0, 32), "OF OF0 OF1 OF2 OF3 OF4 OF5", "OUa")
+    pick("LC", 0, 32, "Q0", T.OI[:, 0:2], "Q0 OI", "LC")
+    pick("L2", NP, NP + 16, "Q0", T.OZ[:, 0:1], "Q0 OZ", "Lz")
+    quant("Q1", 0, 128, T.T1, "T1a T1b", "Q1")
+    pick("V0", 0, 128, "Q0", oV0, "Q0 OUa", "V0")
+    for b in range(4):
+        mm("P%d" % b, "QE", 128 * b, "V0", 0, 128, "QE V0c V0s", True, False)
+        mm("P%d" % b, "QE", 128 * b, "Q1", 0, 128, "QE Q1", False, True)
+    ts(W("DM"), W("JM"), ca, None, Op.is_equal, None, "JM CF", "DM")
+    ts(W("R16"), W("JM"), 0.0, None, Op.is_gt, None, "JM", "R16")
+    ts(W("TT0"), W("TB0"), ca, -2 * BIG, Op.is_lt, Op.mult, "TB0 CF", "TT0")
+    ts(W("TE0"), W("TB0"), ca, -EPS, Op.is_lt, Op.mult, "TB0 CF", "TE0")
+    for s in range(2):
+        ts(T.R32[:, 32 * s:32 * s + 32], T.J[:, 0:32], 0.0, None, Op.is_gt, None, "J", "R32%d" % s)
+    for s in range(3):
+        ts(T.R48[:, 48 * s:48 * s + 48], T.J[:, 0:48], 0.0, None, Op.is_gt, None, "J", "R48%d" % s)
+    ms(T.THG[:], 2.0, "THG")
+    ts(W("TT0"), W("TT0"), BIG, None, Op.add, None, "TT0", "TT0")
+    pick("WM", 0, 128, "Q0", oWM, "Q0 OUa", "WM")
+    ts(W("TT0", 0, P), W("TT0", 0, P), 0.0, None, Op.mult, None, "TT0", "TT1")
+    ts(W("TT0", 32, 32 + P), W("TT0", 32, 32 + P), Wc("CD", 3), None, Op.mult, None, "TT0 CD3", "TT2")
+    for k in range(1, N):
+        ms(T.THG[:, B0 * (k - 1):B0 * (k - 1) + P], -0.5 if slots[k] < me else 0.0, "THG%d" % k, "THG")
+    THG = "THG " + " ".join("THG%d" % k for k in range(1, N))
+    tt(T.TH0[:], W("TT0"), W("TE0"), Op.add, "TT0 TT1 TT2 TE0", "TH0")
+    for b in range(4):
+        act(T.A0[:, 96 * b:96 * (b + 1)], T["P%d" % b][:, 0:96], "P%d" % b, "A0%d" % b, Act.Copy)
+    ts(W("LM0"), T.J[:, 0:32], 0.0, Wc("CD", 5), Op.mult, Op.add, "J CD5", "LM0")
+    ms(T.NM[:], 0.0, "NM")
+    cp(T.OG[:, 0:1], cg, "CF", "OG")
+    ts(W("LM0"), W("LM0"), Wc("CD", 4), None, Op.mult, None, "LM0 CD4", "LM0")
+    ms(W("IL", 24, 32), 0.0, "ILp")
+    quant("Q2", 0, NP, T.T2, "T2", "Q2")
+    for k in range(2):
+        for c in (1, 2):
+            act(W("RW", 64 + 3 * k + c, 128, 8), W("RW", 64 + 3 * k, 128, 8), "RX%d" % k, "RY%d%d" % (k, c), bias=float(c))
+    tt(W("RM"), W("RW"), W("DM"), Op.mult, "RW RW0 RX0 RX1 RY01 RY02 RY11 RY12 RW2 RW3 DM", "RM")
+    ts(T.O96[:], T.J[:, 0:6], 0.0, ca7, Op.mult, Op.add, "J CF", "O96")
+    scan(W("RS"), W("R16"), W("RM"), "R16 RM", "RS")
+    cp(T.OU[:, 32:64], W("OF", 32, 64), "OF OF6 OF7 OFh", "OUb")
+    cp(T.OU[:, 72:88], W("RS", 15, 256, 16), "RS", "OUc")
+    ts(T.TH1[:], W("TB1"), ca, -EPS, Op.is_lt, Op.mult, "TB1 CF", "TH1")
+    act(W("PYC"), W("PYB"), "PYB CD2", "PYC", bias=Wc("CD", 2))
+
+    pick("WQ", 0, 128, "LC", oWQ, "LCc OUa", "WQ", E1)
+    for b in range(2):
+        mm("P%d" % b, "QE", 128 * b, "LC", 0, NL, "QE LCc LCs", arrive=E1)
+    mm("P4", "WQ", 0, "LC", 0, NL, "WQc WQs")
+    for b in range(2, 4):
+        mm("P%d" % b, "QE", 128 * b, "LC", 0, NL, "QE")
+    tt(W("M0"), T.P4[:, Z0:Z0 + 32], W("DM", 0, 32), Op.mult, "P4 DM", "M0")
+    cp(W("AS"), T.P4[:, Z0:Z0 + 32], "P4", "AS")
+    scan(W("BS0"), W("R16", 0, 32), W("M0"), "R16 M0", "BS0")
+    for s in range(2):
+        ts(T.D0[:, 32 * s:32 * s + 32], W("AS"), Wc("BS0", 16 * s + 15), None, Op.subtract, None, "AS BS0", "D0%d" % s)
+    tt(T.CM0[:], T.D0[:], T.TH0[:], Op.is_gt, "D00 D01 TH0", "CM0")
+    scan(T.SN0[:], T.R32[:], T.CM0[:], "R320 R321 CM0", "SN0")
+    cp(T.OL0[:], T.SN0[:, 31:64:32], "SN0", "OL0")
+    cp(W("SR0").indirect(T.OL0[:]), W("PY0"), "OL0 PY0", "SR0")
+    cp(W("SS").indirect(T.OL0[:]), W("AS"), "OL0 AS", "SS")
+    cp(W("G0"), W("SR0").indirect(oG), "SR0 OUa", "G0")
+    tt(W("MS"), W("SS", 0, 16), W("DM", 0, 16), Op.mult, "SS DM", "MS")
+    tr(W("GT0"), W("G0"), "G0", "GT0")
+    red(Wc("NS"), W("MS"), "MS", "NS", True)
+    cp(T.FA[:, 0:32], W("GT0").indirect(oF), "GT0 OUc", "F0")
+    for b in range(4):
+        act(T.DH[:, 8 * b:8 * b + 8], T["P%d" % b][:, Z0 + P + 1:NL:B0], "P%d" % b, "DH%d" % b, Act.Copy)
+    for b in range(3):
+        act(T.H[:, NP * b:NP * (b + 1)], T.DH[:, 8 * b:8 * b + 8].indirect(oH), "DH%d OUb" % b, "H%d" % b, Act.Copy)
+    act(T.SG[:], T.P4[:, 32:NL], "P4 NS", "SG", Act.Sign, bias=Wc("NS"))
+    F0 = spread(T.FA, 0, 6, "F0")
+    ts(T.L0[:], T.FA[:, 0:24], 1.0 / 512, ck, Op.mult, Op.add, F0 + " CF", "L0")
+    ts(T.L0b[:, 1:25], T.FA[:, 0:24], 1.0 / 512, ck, Op.mult, Op.add, F0 + " CF", "L0b")
+    keys = []
+    for b, n in ((0, 8), (1, 8), (2, 6)):
+        keys.append("X1%d" % b)
+        tt(T.X1[:, b:4 * S * n:4], T.A0[:, 96 * b:96 * (b + 1)].indirect(T.L0[:, 0:3 * n]), T.H[:, NP * b:NP * b + S * n],
+           Op.add, "A0%d L0 H%d" % (b, b), keys[-1])
+        if b == 0:
+            tt(T.CG[:], T.SG[:], T.THG[:], Op.is_gt, "SG " + THG, "CG")
+        if b == 1:
+            ts(W("FL0"), W("LM0"), Wc("CN0"), None, Op.is_gt, None, "LM0 CN0", "FL0")
+        if b == 0:
+            for i, (bb, k) in enumerate([(3, k) for k in range(N)] + [(2, 6), (2, 7)]):
+                lst = T.L0b[:, 3 * k + 1:3 * k + 4] if k % 2 else T.L0[:, 3 * k:3 * k + 3]
+                keys.append("X1%d%d" % (bb, k))
+                act(T.X1[:, 4 * S * k + bb:4 * S * (k + 1):4], T.A0[:, 96 * bb:96 * (bb + 1)].indirect(lst),
+                    "A0%d L0 DH%d" % (bb, bb) + (" L0b" if k % 2 else ""), keys[-1], bias=col(T.DH, 8 * bb + k))
+                if i == 5:
+                    act(T.JK[:], T.CG[:], "CG", "CN0", Act.Copy, accum_out=Wc("CN0"))
+    tr(W("FT0"), W("FL0"), "FL0", "FT0")
+    quant("C1", 0, 192, T.X1, " ".join(keys), "C0")
+    quant("C1", 192, NP, T.X1, " ".join(keys), "C1")
+    mm("P5", "WQ", 0, "C1", 0, 192, "C0")
+    mm("P6", "WQ", 0, "C1", 192, NP, "C1")
+
+    for j, (src, rl, dst, cast, sem) in enumerate(((T.C1c, T.RLc, T.L1c, _u8, "rc"), (T.C1s, T.RLs, T.L1s, _same, "rs"))):
+        if RELAY == 1:
+            eng = _deal(off + on, (4, 4, 4, 4))
+            remote([(cast(src[:, 96 * i:96 * (i + 1)]),
+                     [(plan[me]["hb" if i < 2 else "ha"], cast(rl[:, 96 * (i % 2):96 * (i % 2 + 1)]))], eng[3 - i], sem)
+                    for i in range(4)], "C0 C1")
+        elif RELAY == 2:
+            remote(direct(src, dst, cast, S, (1, 4, 5, 6, 7), ENG_P1[j], "p1")
+                   + [(cast(src[:, S * k:S * (k + 1)]), [(plan[me][h], cast(rl[:, 0:S]))], on[2 * k - 2:2 * k], sem)
+                      for k, h in ((2, "hb"), (3, "hc"))], "C0 C1")
+        else:
+            remote(direct(src, dst, cast, S, range(N), ENG_P1[j], "p1"), "C0 C1")
+    P1 = arrivals("p1", *ENG_P1)
+
+    ts(W("VL"), W("FT0").indirect(oPN), 16384.0, None, Op.mult, None, "FT0 OUb", "VL")
+    tt(W("PA"), W("SR0").indirect(oJ4), W("PYC"), Op.add, "SR0 OUd PYC", "PA")
+    ts(W("PEN"), W("VL"), -16384.0, BIG / 16384, Op.add, Op.mult, "VL", "PEN")
+    act(T.AF[0:64, :], T.P5[0:64, 0:192], "P5", "AFa", Act.Copy)
+    cp(T.AF[64:128, :], T.P6[64:128, 0:192], "P6", "AFb")
+    act(W("IL", 0, 24), W("ILB"), "ILB CF", "IL", bias=cs)
+    act(W("PLZ"), T.J[:, 0:24], "J CD10", "PLZ", scale=16.0, bias=Wc("CD", 10))
+    act(T.IRB[:], T.IR[:], "IR", "IRB", scale=65536.0 * UP, bias=65535.5 * UP)
+    for q in range(N):
+        act(Wc("ADJ", q), Wc("CD", 6), "CD6", "ADJ%d" % q, Act.Copy, scale=float(S * (q - slot_at[q])))
+    act(W("AD2"), W("ADJ").indirect(T.OG[:, 0:1]), "OG " + " ".join("ADJ%d" % q for q in range(N)), "AD2", Act.Copy)
+    red(Wc("CC"), W("VL"), "VL", "CC")
+    tt(W("A1"), T.AF[:].indirect(oA1), W("PEN"), Op.add, "AFa AFb OUb PEN", "A1")
+    ts(W("PB"), W("PA"), Wc("CC"), None, Op.add, None, "PA CC", "PB")
+    tt(W("M1"), W("A1"), W("DM", 0, 48), Op.mult, "A1 DM", "M1")
+    scan(W("BS1"), W("R16", 0, 48), W("M1"), "R16 M1", "BS1")
+    for s in range(3):
+        ts(T.D1[:, 48 * s:48 * s + 48], W("A1"), Wc("BS1", 16 * s + 15), None, Op.subtract, None, "A1 BS1", "D1%d" % s)
+    tt(T.CM1[:], T.D1[:], T.TH1[:], Op.is_gt, "D10 D11 D12 TH1", "CM1")
+    scan(T.SN1[:], T.R48[:], T.CM1[:], "R480 R481 R482 CM1", "SN1")
+    cp(T.OL1[:, 0:3], T.SN1[:, 47:144:48], "SN1", "OL1")
+    cp(W("SR1").indirect(T.OL1[:, 0:3]), W("PB"), "OL1 PB", "SR1")
+    cp(W("G1"), W("SR1").indirect(oG), "SR1 OUa", "G1")
+    tr(W("GT1"), W("G1"), "G1", "GT1")
+    cp(T.FA[:, 32:64], W("GT1").indirect(oF), "GT1 OUc", "F1")
+    F1 = spread(T.FA, 32, 6, "F1")
+    ts(T.LI[:, 0:24], T.FA[:, 32:56], 511, None, Op.bitwise_and, None, F1, "LIa")
+    ts(T.LI[:, 24:48], T.FA[:, 32:56], 9, 127, Op.logical_shift_right, Op.bitwise_and, F1, "LIb")
+    ts(T.MG[:], T.FA[:].indirect(oMG), UP, None, Op.mult, None, F0 + " " + F1 + " OUc", "MG")
+    cp(T.LV[:], T.LI[:, 0:24], "LIa", "LV")
+    ts(T.LE[:], T.LI[:, 24:48], 4.0, ck, Op.mult, Op.add, "LIb CF", "LE")
+    remote(direct(T.MG, T.ML, _same, 8, range(N), ENG_MS, "ms"), "MG")
+    MS = arrivals("ms", ENG_MS)
+    for i, (k0, k1) in enumerate(PARTS):
+        pick("PV", S * k0, S * k1, "C1", T.LV[:, 3 * k0:3 * k1], "C0 C1 LV", "PV%d" % i)
+        pick("PE", S * k0, S * k1, "Q2", T.LE[:, 3 * k0:3 * k1], "Q2 LE", "PE%d" % i)
+    order = (3, 0, 1, 2)
+    for i, (k0, k1) in enumerate(PARTS):
+        a, b = S * k0, S * k1
+        for j in order:
+            mm("P%d" % (4 * i + j), "QE", 128 * j, "PV", a, b, "QE PV%dc PV%ds" % (i, i), True, False)
+        for j in order:
+            mm("P%d" % (4 * i + j), "QE", 128 * j, "PE", a, b, "QE PE%dc PE%ds" % (i, i), False, True)
+    for i, (k0, k1) in enumerate(PARTS):
+        a, b = S * k0, S * k1
+        keys = []
+        for k in range(k0, k1):
+            keys.append("X23%d" % k)
+            act(T.X2[:, 4 * S * k + 3:4 * S * (k + 1):4], T["P%d" % (4 * i + 3)][:, S * (k - k0):S * (k - k0 + 1)],
+                "P%d DH3" % (4 * i + 3), keys[-1], bias=col(T.DH, 24 + k))
+        for j in range(3):
+            keys.append("X2%d%d" % (j, i))
+            tt(T.X2[:, 4 * a + j:4 * b:4], T["P%d" % (4 * i + j)][:, 0:b - a], T.H[:, NP * j + a:NP * j + b], Op.add,
+               "P%d H%d" % (4 * i + j, j), keys[-1])
+        quant("C2", a, b, T.X2, " ".join(keys), "C2%d" % i)
+        for j, (src, dst, cast) in enumerate(((T.C2c, T.L2c, _u8), (T.C2s, T.L2s, _same))):
+            remote(direct(src, dst, cast, S, range(k0, k1), ENG_P2[j], "p2", 2 * j * (RELAY > 0)), "C2%d" % i)
+    P2 = arrivals("p2", *ENG_P2)
+
+    cp(T.ML[:, 8 * me:8 * me + 8], T.MG[:, 0:8], "MG", "ML")
+    pick("L1", S * me, S * (me + 1), "C1", T.OI[:, 0:3], "C0 OI", "L1")
+    quant("QW", 0, 128, T.TW, "TW", "QW")
+    ms(W("M64", 0, 3), 0.0, "M4a")
+    ts(W("M64", 3, 64), T.J[:, 0:61], Wc("CD", 8), Wc("CD", 6), Op.is_equal, Op.mult, "J CD8 CD6", "M64")
+    ts(T.LP[:], W("OF", 40, 64), 8.0, 3.0, Op.mult, Op.add, "OFh", "LP")
+    ts(W("TA8"), T.J[:, 0:8], cg, -EPS, Op.is_lt, Op.mult, "J CF", "TA8")
+    ts(W("TA9"), T.J[:, 0:8], cg, 5 * BIG, Op.is_equal, Op.mult, "J CF", "TA9")
+    ts(W("LM1"), T.J[:, 0:32], 0.0, Wc("CD", 11), Op.mult, Op.add, "J CD11", "LM1")
+    tt(W("TAa"), W("TA8"), W("TA9"), Op.add, "TA8 TA9", "TAa")
+    ts(W("LM1"), W("LM1"), Wc("CD", 6), None, Op.mult, None, "LM1 CD6", "LM1")
+    ts(T.LT[:], W("ILT"), Wc("CD", 13), None, Op.add, None, "ILT CD13", "LT")
+    pick("L2", S * me, S * (me + 1), "C2", T.OI[:, 0:3], "C2%d OI" % (len(PARTS) - 1), "L2")
+    act(T.THA[:], W("TAa").indirect(oH), "TAa OUb", "THA", Act.Copy)
+    ba, by1, by2 = ("P0", "P1", "P2") if len(PARTS) == 2 else ("P4", "P5", "P6")
+    mm(ba, "WM", 0, "L1", 0, NP, "WMc WMs L1c L1s", arrive=P1)
+    mm(by1, "QW", 0, "L1", 0, NP, "QW")
+    tt(W("PM"), T.ML[:], W("M64"), Op.mult, "ML M4a M64", "PM", MS)
+    tt(T.Z[:], T.ML[:].indirect(T.LP[:]), T.IRB[:], Op.subtract, "ML LP IRB", "Z")
+    red(Wc("PC"), W("PM"), "PM", "PC")
+    ts(T.U[:], T.ML[:].indirect(oUN), 1.0 / UP, None, Op.mult, None, "ML OUc", "U")
+    ts(T.PJ[:, 0:1], Wc("PC"), 1.0 / UP, None, Op.mult, None, "PC", "PJa")
+    ts(T.DI[:, 0:24], T.U[:, 24:48], 16, None, Op.logical_shift_right, None, "U", "DIa")
+    ts(T.PJ[:, 1:2], T.PJ[:, 0:1], 511, None, Op.bitwise_and, None, "PJa", "PJb")
+    tt(T.AM[:], T[ba][:, 0:NP], T.Z[:], Op.min, ba + " Z", "AM")
+    ts(T.OP[:, 0:1], T.PJ[:, 1:2], Wc("AD2"), None, Op.add, None, "PJb AD2", "OP")
+    ts(T.DI[:, 24:48], T.U[:, 24:48], 9, 127, Op.logical_shift_right, Op.bitwise_and, "U", "DIc")
+    act(T.VS[:], T.Z[:], "Z", "VS", Act.Sign)
+    act(T.VM[:], T.VS[:], "VS", "VM", Act.Relu)
+    tt(W("GI"), T.AM[:].indirect(T.OP[:, 0:1]), W("DM", 0, 16), Op.mult, "AM OP DM", "GI")
+    cp(W("DF"), T.DI[:], "DIa DIc", "DF")
+    red(Wc("SI"), W("GI"), "GI", "SI", True)
+    act(T.DA[:, 192:NP], T.AM[:, 192:NP], "AM SI", "DAb", Act.Sign, bias=Wc("SI"))
+    act(T.DA[:, 0:192], T.AM[:, 0:192], "AM SI", "DAa", Act.Sign, bias=Wc("SI"))
+    tt(T.YS[:, 0:NP], T[by1][:, 0:NP], T.VM[:], Op.mult, by1 + " VM", "Y1")
+    dma("s", T.y[:, 0:NP], T.YS[:, 0:NP], "Y1", "o3")
+    tt(T.CA[:, 192:NP], T.DA[:, 192:NP], T.THA[:, 192:NP], Op.is_gt, "DAb THA", "CAb")
+    act(T.VS[:, 192:NP], T.CA[:, 192:NP], "CAb VM", "CN2", Act.Copy, accum_out=Wc("CN1", 1))
+    tt(T.CA[:, 0:192], T.DA[:, 0:192], T.THA[:, 0:192], Op.is_gt, "DAa THA", "CAa")
+    ts(W("NA"), T.U[:, 0:24], 1.0 / 512, Wc("CD", 9), Op.mult, Op.add, "U CD9", "NA")
+    red(Wc("CN1"), T.CA[:, 0:192], "CAa", "CN1")
+    tt(W("V1"), W("DF", 0, 24), W("IL", 0, 24), Op.is_gt, "DF IL", "V1")
+    ts(W("FL1"), W("LM1"), Wc("CN1", 1), Wc("CN1"), Op.subtract, Op.is_gt, "LM1 CN1 CN2", "FL1")
+    ts(W("NB"), W("DF", 24, 48), 4.0, Wc("CD", 9), Op.mult, Op.add, "DF CD9", "NB")
+    tr(W("FT1"), W("FL1"), "FL1", "FT1")
+    tt(T.NM[:, 0:24], W("NA"), W("V1"), Op.mult, "NA V1 NM", "NMa")
+    scan(W("FS1"), W("R16", 0, 32), W("FT1"), "R16 FT1", "FS1")
+    cp(W("C1A"), W("FS1").indirect(oC1), "FS1 OUa", "CA1")
+    CA = spread(T.WB, PIECE["C1A"][1], 2, "CA1")
+    tt(W("TK"), W("C1A").indirect(oTK), W("IL"), Op.is_gt, CA + " OUc IL ILp", "TK")
+    tt(W("F96"), W("C1A").indirect(T.O96[:]), W("I96"), Op.is_gt, CA + " O96 I96", "F96")
+    tt(W("LZ"), W("TK", 0, 24), W("PLZ"), Op.mult, "TK PLZ", "LZ")
+    tt(T.NM[:, 32:56], W("TK", 0, 24), W("NB"), Op.mult, "TK NB NM", "NMb")
+    ts(T.LQ[:], W("LZ"), float(NP), None, Op.add, None, "LZ", "LQ")
+    act(T.TM[:], W("F96").indirect(T.LT[:]), "F96 LT", "TM", Act.Copy)
+
+    mm(by2, "QW", 0, "L2", 0, NP, "QW L2c L2s", arrive=P2)
+    pick("OC", 0, NP, "L2", T.LQ[:], "L2c Lzc LQ", "OC", P2)
+    dma("s", T.oc[:], _u8(T.OCc[:]), "OCc", "o4")
+    tt(T.YS[:, NP:2 * NP], T[by2][:, 0:NP], T.TM[:], Op.mult, by2 + " TM", "Y2")
+    dma("s", T.y[:, NP:2 * NP], T.YS[:, NP:2 * NP], "Y2", "o5")
+    ts(T.NN[0:32, :], T.NM[0:32, :], -1.0, None, Op.add, None, "NM NMa NMb", "NN")
+    tr(T.NT[0:32, :], T.NN[0:32, :], "NN", "NT")
+    dma("s", T.nm[0:1, 0:NP], T.NT[0:24, 0:16], "NT", "o1")
+    dma("s", T.nm[0:1, NP:2 * NP], T.NT[0:24, 32:48], "NT", "o2")
+    for k in range(4):
+        dma("a", T.osc[4 * k:4 * k + 4, :], T.OCs[32 * k:32 * k + 4, :], "OCs", "o%d" % (6 + k))
+    op("s", None, "o1 o2 o3 o4 o5", "")
+    op("a", None, "o6 o7 o8 o9", "")
+    op("g", None, "", "", (("sent", sent[0]),))
+
+    known, at_issue, waits, needed = {q: 0 for q in queues}, [], [], set()
+    for i, o in enumerate(ops):
+        mine = []
+        for d in o["deps"]:
+            if not known[o["q"]] >> d & 1:
+                mine.append(d)
+                known[o["q"]] |= 1 << d | at_issue[d]
+        needed.update(mine)
+        waits.append(mine)
+        at_issue.append(known[o["q"]])
+    turn, count, before, mark, seen = {q: 0 for q in POOL}, {}, {}, {}, {q: set() for q in queues}
+    for i, o in enumerate(ops):
+        eng = queues[o["q"]]
+        for d in waits[i]:
+            eng.wait_ge(T.sem[mark[d][0]], mark[d][1])
+        for sem, val in o["arrive"]:
+            if (sem, val) not in seen[o["q"]]:
+                seen[o["q"]].add((sem, val))
+                eng.wait_ge(T.sem[sem], val)
+        if o["fn"] is None:
+            continue
+        if i not in needed:
+            o["fn"]()
+            continue
+        pool = "d" if o["dma"] else o["q"]
+        name = "x%s%d" % (pool, turn[pool] % POOL[pool])
+        turn[pool] += 1
+        if name in before and not at_issue[i] >> before[name] & 1:
+            eng.wait_ge(T.sem[name], count[name])
+        step = 16 if o["dma"] else 1
+        count[name] = count.get(name, 0) + step
+        before[name] = i
+        mark[i] = (name, count[name])
+        o["fn"]().then_inc(T.sem[name], step)

@@ -3,14 +3,16 @@ from concourse.mybir import dt, AluOpType, AxisListType, ActivationFunctionType
 
 Op, Act = AluOpType, ActivationFunctionType
 N, P, CAP, M, S = 8, 24, 12, 64, 48
-B0 = P + 2
-Z0 = 6
-NL = Z0 + N * B0
-NO = (N - 1) * B0
-NP = N * S
-EPS, BIG, UP = 1e-37, 1e29, 2.0 ** 72
-RELAY = 0
+UQ = 126
+NL, NO = UQ + 2 * N, (N - 1) * P
+K1 = 4 * P
+NA, NP = N * K1, N * S
+HW = 224
+EPS, BIG = 1e-37, 2.0 ** 80
 PARTS = ((4, 8), (0, 4))
+XA, XV, XN = (4, 5, 6, 7, 0, 1), (3, 2, 1), 24
+RELAY = {"1": 2, "m": 0, "2": 0}
+TW_ = 320
 
 F, BF, I32, U16, C, SC = "float32", "bfloat16", "int32", "uint16", "float8_e4m3fn_x4", "uint8"
 SCRATCH = {}
@@ -21,34 +23,33 @@ def _sb(dtype, **kw):
         SCRATCH[name] = ("sbuf", [128, n], dtype)
 
 
-_sb(BF, T0=512, T1=512, T2=4 * NP, TW=512, TE=2048, H=3 * NP, X1=4 * NP, X2=4 * NP, ID=128,
-    R32=64, R48=144, TH0=64, TH1=144, THG=NO, THA=NP, IR=NP, D0=64, CM0=64, SN0=64, SG=NO, CG=NO, JK=NO,
-    D1=144, CM1=144, SN1=144, VS=NP, VM=NP, TM=NP, DA=NP, CA=NP)
-for _n, _w in dict(Q0=128, Q1=128, Q2=NP, QW=128, QE=512, LC=NL, WQ=128, WM=128, V0=128, C1=NP, PV=NP, PE=NP,
-                   C2=NP, L1=NP, L2=NP + 16, OC=NP, RL=NP // 2).items():
+_sb(BF, T0=512, T1=512, T2=4 * NP, TW=512, TE=2048, JB=128, H=2 * NP, X1=4 * NA, X2=4 * NP, RR=290, R16=TW_, DM=TW_,
+    JM=TW_, RW=TW_, RM=TW_, RS=TW_, TH0=48, TB1=144, TH1=144, D0=48, CM0=50, SN0=50, D1=144, CM1=144, SN1=144,
+    THG=NO, SG=NO, CG=NO, JK=208, CA=NP + 8, NT=NA + 16)
+for _n, _w in dict(Q0=144, Q1=128, Q2=NP, QW=128, QE=512, LC=NO, WQ=128, WM=128, V0=128, C1=NA, PV=NP, PE=NP,
+                   C2=NP, L1=NA + 16, P1=NP, L2=2 * HW, OC=NP, R1=2 * K1, R2=S).items():
     _sb(C, **{_n + "c": _w})
     _sb(SC, **{_n + "s": _w})
-_sb(F, J=128, CF=10, A0=NP, DH=32, AF=192, MG=64, ML=64, IRB=NP, Z=NP, AM=NP, YS=2 * NP, NM=64, NN=64, NT=64)
-_sb(I32, PI=1, CI=10, FA=64, LI=48, U=48, DI=48, PJ=2)
-_sb(U16, OU=88, OL0=2, OL1=4, L0=24, L0b=26, LV=24, LE=24, OP=2, OG=2, OZ=2, OI=4, LP=24, LQ=24, O96=6, LT=24)
+_sb(F, CP=1, CF=8, A0=NP, DH=32, AF=192, MS=104, MG=64, ML=64, RL=16, YS=2 * NP, NR=NP, SR0=200, SS0=200)
+_sb(I32, PI=4, CI=6)
+_sb(U16, OU=60, OT=20, OW=8, OL0=2, OL1=4, OA=4, LV=24, LE=24, ON=2, LP=32, LQ=24)
 for _k in range(8):
     SCRATCH["P%d" % _k] = ("psum", [128, 512], F)
 PIECE = {}
-for _b, _d in (("K", dict(JM=256, DM=256, R16=256, CD=16, OF=64, RW=256, RM=256, RS=256, TB0=64, TT0=64, TE0=64, TB1=144,
-                          PY0=32, PYB=48, PYC=48, LM0=32, LM1=32, TA8=8, TA9=8, TAa=8, M64=64, ADJ=8, AD2=16, ILB=24,
-                          IL=32, PLZ=24, I96=96, ILT=24)),
-               ("WA", dict(M0=32, BS0=32, SR0=32, AS=32, SS=32, MS=16, NS=8, CN0=8, FL0=32, FT0=32, VL=48, PEN=48, CC=8,
-                           G0=96, GT0=96, A1=48, M1=48, BS1=48, PA=48, PB=48, SR1=48, G1=96, GT1=96)),
-               ("WB", dict(DF=48, NA=24, NB=24, V1=24, PM=64, PC=8, GI=16, SI=8, CN1=8, FL1=32, FT1=32, FS1=32,
-                           C1A=16, TK=32, LZ=24, F96=96))):
+for _b, _d in (("K", dict(CD=16, OF=64, PY0=32, JX=8, XG=16, J4=16, MK=16, ILB=40, IL=32, PLZ=24, KF=48, LM=32,
+                          TA=8, TB=8, TH8=8)),
+               ("WA", dict(M0=32, BS0=32, AS=32, MS0=16, NS=8, SE=16, SF=16, CN0=8, FL0=32, FT0=32, PEN=48, NI=8, SV=16,
+                           G0=128, GT0=128, PB=48, A1=48, M1=48, BS1=48, SR1=48, SS1=48, MS1=16, MS2=16, G1=96, GT1=96)),
+               ("WB", dict(SA=16, ZF=8, CN1=8, FL1=32, FT1=32, FS1=32, C8=16, TK=32, LZ=24, NB=32, NM=32, NN=32, NU=32))):
     _at = 0
     for _n, _w in _d.items():
         PIECE[_n] = (_b, _at, _w)
         _at += _w
     _sb(F, **{_b: _at})
 
-POOL = {"v": 48, "a": 36, "p": 20, "g": 18, "d": 20}
-SEMAPHORES = ["e1", "p1", "p2", "ms", "rc", "rs", "sent"] + ["x%s%d" % (q, i) for q, n in POOL.items() for i in range(n)]
+POOL = {"v": 46, "a": 42, "p": 16, "g": 14, "d": 20}
+SEMAPHORES = (["e1", "e2", "p1", "pa", "pb", "ms", "sent", "h1c", "h1s", "h2c", "h2s", "hL"]
+              + ["x%s%d" % (q, i) for q, n in POOL.items() for i in range(n)])
 
 
 def _mask(engines):
@@ -58,515 +59,557 @@ def _mask(engines):
     return m
 
 
-def _deal(engines, sizes):
-    out, at = [], 0
-    for s in sizes:
-        out.append(engines[at:at + s])
-        at += s
-    return out
-
-
-def _plan(T, topo):
-    cores = list(T.cores)
-    plan = {}
-    for r, c in enumerate(cores):
-        off = [q for q in range(N) if topo.chip(cores[q]) != topo.chip(c)]
-        plane = [q for q in off if topo.same_plane(topo.chip(c), topo.chip(cores[q]))]
-        far = [q for q in off if q not in plane]
-        far.sort(key=lambda q: (topo.mates(topo.chip(c), topo.chip(cores[q])), topo.die(cores[q]) == topo.die(c)))
-        plane.sort(key=lambda q: topo.die(cores[q]) == topo.die(c))
-        peer = [q for q in range(N) if q != r and q not in off]
-        free = [h for h in topo.cores_of(c) if topo.die(h) == topo.die(c) and h not in cores]
-        ha = [h for h in free if all(topo.may_write(h, cores[q]) for q in far)][0]
-        hb, hc = [h for h in free if h != ha]
-        serve = {0: {}, 1: {ha: (4, 5, 6, 7), hb: (2, 3, 1)}, 2: {hb: (2,), hc: (3,)}}[RELAY]
-        plan[r] = dict(slots=[r] + peer + plane + far, ha=ha, hb=hb, hc=hc, serve=serve)
-    return plan
-
-
-def _engines(topo, src, off_dst, on_dst):
-    off = topo.engines(src, off_dst)
-    return off, [e for e in topo.engines(src, on_dst) if e not in off]
-
-
-OFF = (4, 5, 6, 7, 2, 3)
-ENG_MS = (0, 2, 2, 2, 1, 1, 1, 1)
-ENG_D = ((0, 2, 2, 2, 1, 1, 1, 1), (0, 2, 1, 1, 2, 2, 1, 1))
-ENG_P1 = {0: ENG_D, 1: ((0, 4, 4, 4, 2, 2, 2, 2),) * 2, 2: ((0, 2, 8, 8, 2, 2, 2, 2),) * 2}[RELAY]
-ENG_P2 = ((0, 2, 2, 2, 2, 2, 2, 2), (0, 2, 4, 4, 2, 2, 2, 2)) if len(PARTS) == 2 else ENG_D
-
-
 def _dst(topo, c):
     rid, pid, _ = topo.addr(c)
     return DstId(rid=rid, pnc=pid)
 
 
-def _u8(v):
-    return v.bitcast(dt.uint8)
+def _share(topo, cores, r, ks):
+    src = cores[r]
+    far = [k for k in ks if k and topo.chip(cores[r ^ k]) != topo.chip(src)]
+    near = [k for k in ks if k and k not in far]
+    off = topo.engines(src, cores[r ^ far[0]])
+    size = {k: 1 for k in far}
+    grown = True
+    while grown:
+        grown = False
+        low = min(size.values())
+        for k in far:
+            if size[k] == low and sum(size.values()) + low <= len(off):
+                size[k] *= 2
+                grown = True
+    out, at = {}, 0
+    for k in sorted(far, key=lambda k: -size[k]):
+        out[k] = off[at:at + size[k]]
+        at += size[k]
+    for k in near:
+        out[k] = [e for e in topo.engines(src, cores[r ^ k]) if e not in off]
+    return out
 
 
-def _u32(v):
-    return v.bitcast(dt.uint32)
+def _relay(topo, cores, r, most):
+    src = cores[r]
+    free = [h for h in topo.cores_of(src) if topo.die(h) == topo.die(src) and h not in cores]
+    ks = range(*PARTS[0])
+    can = {k: [h for h in free if topo.may_write(h, cores[r ^ k])] for k in ks}
+    load = {h: [] for h in free}
+    for k in sorted(ks, key=lambda k: len(can[k])):
+        h = min(can[k], key=lambda h: len(load[h]))
+        if len(load[h]) < most:
+            load[h].append(k)
+    out = {}
+    via = [(k, h) for h in free for k in load[h]]
+    for i, (k, h) in enumerate(via):
+        off = topo.engines(h, cores[r ^ k])
+        to = topo.engines(src, h)
+        if len(via) < len(ks):
+            to = [e for e in to if e not in off]
+        n, m, j = 1 << (len(to) // len(via)).bit_length() - 1, len(off) // len(load[h]), load[h].index(k)
+        out[k] = (h, j, to[n * i:n * (i + 1)], off[m * j:m * (j + 1)])
+    return out
 
 
-def _same(v):
-    return v
+def _at2(r):
+    return HW * (r // 4) + 16 + S * (r % 4)
 
 
-def _helper(g, core, T, topo, plan):
-    cores = list(T.cores)
+def _bytes(v, x):
+    return v.bitcast(dt.uint8) if x == "c" else v
+
+
+def _helper(g, core, T, topo):
+    cores, total = list(T.cores), 0
     for r in range(N):
-        ks = plan[r]["serve"].get(core)
-        if ks is None:
-            continue
-        slots = plan[r]["slots"]
-        off, on = _engines(topo, core, cores[slots[ks[0]]], cores[r])
-        eng = _deal(off + on, [ENG_P1[0][k] for k in ks])
-        total = 0
-        for sem, src, dst, cast in (("rc", T.RLc, T.L1c, _u8), ("rs", T.RLs, T.L1s, _same)):
-            g.wait_ge(T.sem[sem], 8 if RELAY == 1 else 2)
-            at = [S * (k % 4) if RELAY == 1 else 0 for k in ks]
-            g.remote_dma_fused([RemoteDMATransfer(
-                dst_ids=[_dst(topo, cores[slots[k]])], dma_engine_mask=_mask(e), remote_sem=T.sem.p1,
-                srcs=[cast(src[:, a:a + S])], dsts=[cast(dst[:, S * r:S * (r + 1)])])
-                for k, a, e in zip(ks, at, eng)], local_sem=T.sem.sent)
-            total += sum(len(e) for e in eng)
+        for stage, w, at, sem, names in (("1", K1, K1 * r, "p1", ("L1c", "L1s")), ("m", 8, 8 * r, "ms", ("ML",)),
+                                         ("2", S, _at2(r), "pa", ("L2c", "L2s"))):
+            mine = {k: v for k, v in _relay(topo, cores, r, RELAY[stage]).items() if v[0] == core}
+            if not mine:
+                continue
+            for name in names:
+                x = name[-1]
+                g.wait_ge(T.sem["h" + name[1:]], sum(len(v[2]) for v in mine.values()))
+                src, dst = T["R" + name[1:]], T[name][:, at:at + w]
+                g.remote_dma_fused([RemoteDMATransfer(
+                    dst_ids=[_dst(topo, cores[r ^ k])], dma_engine_mask=_mask(v[3]), remote_sem=T.sem[sem],
+                    srcs=[_bytes(src[:, w * v[1]:w * (v[1] + 1)], x)], dsts=[_bytes(dst, x)])
+                    for k, v in mine.items()], local_sem=T.sem.sent)
+                total += sum(len(v[3]) for v in mine.values())
+    if total:
         g.wait_ge(T.sem.sent, total)
 
 
 def rank_program(g, core, T, topo):
-    plan = _plan(T, topo)
     me = T.rank_of(core)
     if me is None:
-        _helper(g, core, T, topo, plan)
+        _helper(g, core, T, topo)
         return
     cores = list(T.cores)
-    slots = plan[me]["slots"]
-    slot_at = [plan[q]["slots"].index(me) for q in range(N)]
-    off, on = _engines(topo, core, cores[slots[7]], cores[slots[1]])
     V, A, PE, SY = g.vector, g.scalar, g.tensor, g.sync
     queues = {"v": V, "a": A, "p": PE, "g": g, "s": SY}
 
-    def W(name, a=0, b=None, step=1):
-        buf, at, n = PIECE[name]
-        return T[buf][:, at + a:at + (n if b is None else b):step]
+    def R(name, a=0, b=None, step=1, p=(0, 128)):
+        buf, at, n = PIECE[name] if name in PIECE else (name, 0, SCRATCH[name][1][1])
+        b = n if b is None else b
+        cols = range(512) if SCRATCH[buf][0] == "psum" else range(at + a, at + b, step)
+        return (T[buf][p[0]:p[1], at + a:at + b:step], [(buf, p[0], p[1], frozenset(cols))])
 
-    def Wc(name, j=0):
-        return W(name, j, j + 1)
+    def c1(name, j=0):
+        return R(name, j, j + 1)
 
-    ops, writer, readers = [], {}, {}
+    def by(win, offs):
+        return (win[0].indirect(offs[0]), win[1] + offs[1], win[1], offs[1])
 
-    def op(q, fn, r="", w="", arrive=(), dma=False, acc=False):
-        i, deps = len(ops), set()
-        for key in r.split():
-            deps.update(writer.get(key, ()))
-            if key[0] == "P" and key[1:].isdigit():
-                deps.update(d for d in readers.get(key, ()) if ops[d]["q"] != q)
-        for key in w.split():
-            if not acc:
-                deps.update(writer.get(key, ()))
-            deps.update(readers.get(key, ()))
-        for key in r.split():
-            readers.setdefault(key, []).append(i)
-        for key in w.split():
-            writer[key] = [i]
-            readers[key] = []
+    def u8(v):
+        return (v[0].bitcast(dt.uint8), v[1])
+
+    def u32(v):
+        return (v[0].bitcast(dt.uint32), v[1])
+
+    def ap(x):
+        return x[0] if isinstance(x, tuple) else x
+
+    ops, log = [], {}
+
+    def op(q, fn, reads=(), writes=(), arrive=(), dma=False, acc=False, after=()):
+        i, deps = len(ops), set(after)
+        rd = [r for x in reads if isinstance(x, tuple) for r in x[1]]
+        wr = []
+        for x in writes:
+            if len(x) == 4:
+                wr += x[2]
+                rd += x[3]
+            else:
+                wr += x[1]
+        for kind, regs in ((0, rd), (1, wr)):
+            for buf, p0, p1, cols in regs:
+                bank = SCRATCH[buf][0] == "psum"
+                for j, k, q0, q1, cs in log.get(buf, ()):
+                    if bank:
+                        hit = ops[j]["q"] != q or (k != kind) or (k and not acc)
+                        hit = hit and (ops[j]["q"] != q or (q0 < p1 and p0 < q1))
+                    else:
+                        hit = (k or kind) and q0 < p1 and p0 < q1 and not cols.isdisjoint(cs)
+                    if hit:
+                        deps.add(j)
+        for kind, regs in ((0, rd), (1, wr)):
+            for buf, p0, p1, cols in regs:
+                log.setdefault(buf, []).append((i, kind, p0, p1, cols))
         ops.append(dict(q=q, fn=fn, deps=sorted(deps, reverse=True), arrive=arrive, dma=dma))
+        return i
 
-    def ts(out, in0, s1, s2, o0, o1, r, w):
+    def ts(out, in0, s1, s2, o0, o1=None, arrive=()):
         if s2 is None:
-            op("v", lambda: V.tensor_scalar(out, in0, s1, None, o0), r, w)
+            op("v", lambda: V.tensor_scalar(out[0], in0[0], ap(s1), None, o0), (in0, s1), (out,), arrive)
         else:
-            op("v", lambda: V.tensor_scalar(out, in0, s1, s2, o0, o1), r, w)
+            op("v", lambda: V.tensor_scalar(out[0], in0[0], ap(s1), ap(s2), o0, o1), (in0, s1, s2), (out,), arrive)
 
-    def tt(out, in0, in1, o, r, w, arrive=()):
-        op("v", lambda: V.tensor_tensor(out, in0, in1, o), r, w, arrive)
+    def tt(out, in0, in1, o, arrive=()):
+        op("v", lambda: V.tensor_tensor(out[0], in0[0], in1[0], o), (in0, in1), (out,), arrive)
 
-    def cp(out, in_, r, w, arrive=()):
-        op("v", lambda: V.tensor_copy(out, in_), r, w, arrive)
+    def cp(out, in_, arrive=()):
+        op("v", lambda: V.tensor_copy(out[0], in_[0]), (in_,), (out,), arrive)
 
-    def ms(ap, val, w, r=""):
-        op("v", lambda: V.memset(ap, val), r, w)
+    def ms(out, val):
+        op("v", lambda: V.memset(out[0], val), (), (out,))
 
-    def scan(out, reset, data, r, w):
-        op("v", lambda: V.tensor_tensor_scan(out, reset, data, 0.0, Op.mult, Op.add), r, w)
+    def scan(out, reset, data):
+        op("v", lambda: V.tensor_tensor_scan(out[0], reset[0], data[0], 0.0, Op.mult, Op.add), (reset, data), (out,))
 
-    def red(out, in_, r, w, negate=False):
-        op("v", lambda: V.tensor_reduce(out, in_, AxisListType.X, Op.add, negate=negate), r, w)
+    def red(out, in_, negate=False):
+        op("v", lambda: V.tensor_reduce(out[0], in_[0], AxisListType.X, Op.add, negate=negate), (in_,), (out,))
 
-    def tr(out, in_, r, w):
-        op("v", lambda: V.transpose(out, in_), r, w)
+    def tr(out, in_):
+        op("v", lambda: V.transpose(out[0], in_[0]), (in_,), (out,))
 
-    def act(out, in_, r, w, func=Act.Identity, arrive=(), **kw):
-        op("a", lambda: A.activation(out, in_, func, **kw), r, w, arrive)
+    def act(out, in_, func=Act.Identity, arrive=(), acc=None, **kw):
+        args = {k: ap(v) for k, v in kw.items()}
+        if acc is not None:
+            args["accum_out"] = acc[0]
+        op("a", lambda: A.activation(out[0], in_[0], func, **args), (in_,) + tuple(kw.values()),
+           (out,) if acc is None else (out, acc), arrive)
 
-    def quant(name, a, b, tile, r, w):
-        op("v", lambda: V.quantize_mx(T[name + "c"][:, a:b], T[name + "s"][:, a:b], tile[:, 4 * a:4 * b]), r, w)
+    def fill(out, n, val):
+        act(out, R("JB", 0, n), scale=0.0, bias=val)
 
-    def mm(bank, lhs, la, rhs, a, b, r, start=True, stop=True, arrive=()):
-        op("p", lambda: PE.matmul_mx(T[bank][:, 0:b - a], T[lhs + "c"][:, la:la + 128], T[lhs + "s"][:, la:la + 128],
-                                     T[rhs + "c"][:, a:b], T[rhs + "s"][:, a:b], start, stop),
-           r, bank, arrive, acc=not start)
+    def quant(name, a, b, tile):
+        o, s, i = R(name + "c", a, b), R(name + "s", a, b), R(tile, 4 * a, 4 * b)
+        op("v", lambda: V.quantize_mx(o[0], s[0], i[0]), (i,), (o, s))
 
-    def pick(dst, a, b, src, offs, r, w, arrive=()):
-        cp(_u32(T[dst + "c"][:, a:b]), _u32(T[src + "c"][:]).indirect(offs), r, w + "c", arrive)
-        act(T[dst + "s"][:, a:b], T[src + "s"][:].indirect(offs), r.replace("c ", "s "), w + "s", Act.Copy, arrive)
+    def mm(bank, lhs, la, rhs, a, b, start=True, stop=True, arrive=()):
+        v = (R(lhs + "c", la, la + 128), R(lhs + "s", la, la + 128), R(rhs + "c", a, b), R(rhs + "s", a, b))
+        o = R(bank, 0, b - a)
+        op("p", lambda: PE.matmul_mx(o[0], v[0][0], v[1][0], v[2][0], v[3][0], start, stop), v, (o,), arrive,
+           acc=not start)
 
-    def dma(q, out, in_, r, w, arrive=()):
-        op(q, lambda: queues[q].dma_start(out, in_), r, w, arrive, dma=True)
+    def pick(dst, a, b, src, offs, win=(0, None), arrive=()):
+        cp(u32(R(dst + "c", a, b)), by(u32(R(src + "c", *win)), offs), arrive)
+        act(R(dst + "s", a, b), by(R(src + "s", *win), offs), Act.Copy, arrive)
 
-    def iota(out, pattern, w, r=""):
-        op("g", lambda: g.iota(out, pattern, 0, 0, allow_small_or_imprecise_dtypes=True), r, w)
+    def dma(q, out, in_, arrive=()):
+        return op(q, lambda: queues[q].dma_start(ap(out), ap(in_)), (in_,), (out,) if isinstance(out, tuple) else (),
+                  arrive, dma=True)
+
+    def move(q, dst, a, src, b, n):
+        dma(q, u8(R(dst + "c", a, a + n)), u8(R(src + "c", b, b + n)))
+        dma(q, R(dst + "s", a, a + n), R(src + "s", b, b + n))
+
+    def iota(out, pattern, base=0, cm=0, whole=False):
+        if whole:
+            op("g", lambda: g.iota(out[0], pattern, base, cm), (), (out,))
+        else:
+            op("g", lambda: g.iota(out[0], pattern, base, cm, allow_small_or_imprecise_dtypes=True), (), (out,))
 
     sent = [0]
 
-    def remote(transfers, r):
+    def remote(transfers):
         sent[0] += sum(len(t[2]) for t in transfers)
         op("g", lambda: g.remote_dma_fused([RemoteDMATransfer(
             dst_ids=[_dst(topo, c) for c, _ in d], dma_engine_mask=_mask(e), remote_sem=T.sem[sem],
-            srcs=[s], dsts=[x for _, x in d]) for s, d, e, sem in transfers], local_sem=T.sem.sent), r, "")
+            srcs=[s[0]], dsts=[x[0] for _, x in d]) for s, d, e, sem in transfers], local_sem=T.sem.sent),
+           [t[0] for t in transfers])
 
-    def direct(src, dst, cast, w, ks, sizes, sem, first=0):
-        far = [k for k in OFF if k in ks]
-        eng = dict(zip(far, _deal(off[len(off) - sum(sizes[k] for k in far):], [sizes[k] for k in far])))
-        eng[1] = on[first:first + sizes[1]]
-        return [(cast(src[:, w * k:w * (k + 1)]), [(cores[slots[k]], cast(dst[:, w * me:w * (me + 1)]))], eng[k], sem)
-                for k in ks if k]
+    def ways(r, ks, stage):
+        via = {k: v for k, v in _relay(topo, cores, r, RELAY[stage]).items() if k in ks}
+        rest = [k for k in ks if k not in via]
+        eng = _share(topo, cores, r, rest) if rest else {}
+        used = [e for v in via.values() for e in v[2]]
+        return via, {k: [e for e in es if e not in used] for k, es in eng.items()}
 
-    def spread(buf, base, w, key):
-        def mv(po, pi, n, a, b, r, wr):
-            cp(buf[po:po + n, base + a:base + b], buf[pi:pi + n, base + a:base + b], r, wr)
-        mv(0, 32, 32, w, 2 * w, key, key + ".a")
-        mv(32, 0, 32, 0, w, key, key + ".b")
-        mv(64, 96, 32, 3 * w, 4 * w, key, key + ".c")
-        mv(96, 64, 32, 2 * w, 3 * w, key, key + ".d")
-        mv(64, 0, 64, 0, 2 * w, "%s %s.a %s.b" % (key, key, key), key + ".e")
-        mv(0, 64, 64, 2 * w, 4 * w, "%s %s.c %s.d" % (key, key, key), key + ".f")
-        return " ".join(key + x for x in ("", ".a", ".b", ".c", ".d", ".e", ".f"))
+    def direct(src, dst, cast, w, at, ks, sem, stage):
+        via, eng = ways(me, ks, stage)
+        remote([(cast(R(src, w * k, w * (k + 1))), [(cores[me ^ k], cast(R(dst, at, at + w)))], eng[k], sem)
+                for k in eng]
+               + [(cast(R(src, w * k, w * (k + 1))), [(h, cast(R("R" + dst[1:], w * j, w * (j + 1))))], to, "h" + dst[1:])
+                  for k, (h, j, to, _) in via.items()])
 
-    def col(buf, j):
-        return buf[:, j:j + 1]
+    def arrivals(sem, calls, stage, *parts):
+        n = 0
+        for ks in parts:
+            for k in ks:
+                via, eng = ways(me ^ k, ks, stage)
+                n += len(via[k][3]) if k in via else len(eng.get(k, ()))
+        return ((sem, calls * n),)
 
-    def arrivals(sem, *sizes):
-        return ((sem, sum(s[slot_at[q]] for s in sizes for q in range(N))),)
+    def same(v):
+        return v
 
-    ca, cg, cs, ck, ch, cg4, ca1, cpp, ca7 = (col(T.CF, j) for j in range(9))
-    oWQ, oWM, oV0, oG = T.OU[:, 0:8], T.OU[:, 8:16], T.OU[:, 16:24], T.OU[:, 24:30]
-    oA1, oPN, oC1, oJ4 = T.OU[:, 32:35], T.OU[:, 36:39], T.OU[:, 30:31], T.OU[:, 64:67]
-    oH = T.OU[:, 40:64]
-    oF, oMG, oUN, oTK = T.OU[:, 72:74], T.OU[:, 76:80], T.OU[:, 80:83], T.OU[:, 84:86]
+    def spread(name, base, w, on="va"):
+        def mv(q, po, pi, n, a, b):
+            o, i = R(name, base + a, base + b, 1, (po, po + n)), R(name, base + a, base + b, 1, (pi, pi + n))
+            if q == "v":
+                cp(o, i)
+            else:
+                act(o, i, Act.Copy)
+        mv(on[0], 0, 32, 32, w, 2 * w)
+        mv(on[1], 64, 96, 32, 3 * w, 4 * w)
+        mv(on[0], 32, 0, 32, 0, w)
+        mv(on[1], 96, 64, 32, 2 * w, 3 * w)
+        mv(on[0], 64, 0, 64, 0, 2 * w)
+        mv(on[1], 0, 64, 64, 2 * w, 4 * w)
 
-    dma("s", T.T0[:, 4 * Z0:4 * (Z0 + P)], T.r0[:], "", "T0a")
-    dma("a", T.T0[:, 4 * (Z0 + P):128], T.u[:, 0:8], "", "T0b")
-    dma("s", T.T1[:, 0:16 * P], T.r1[:], "", "T1a")
-    dma("s", T.T2[:], T.r2[:], "", "T2")
-    op("g", lambda: g.iota(T.PI[:], [[0, 1]], 0, 1), "", "PI")
-    iota(T.J[:], [[1, 128]], "J")
-    iota(W("JM"), [[0, 16], [1, 16]], "JM")
-    iota(W("TB0"), [[-16, 2], [1, 32]], "TB0")
-    iota(W("PY0"), [[2048, 32]], "PY0")
-    ms(T.T0[:, 0:4 * Z0], 0.0, "T0d")
-    ms(T.T0[:, 128:512], 0.0, "T0c")
-    ms(T.T1[:, 16 * P:512], 0.0, "T1b")
-    ms(T.TE[:], 0.0, "TE")
-    ms(W("OF"), 0.0, "OF")
-    ms(W("RW"), 0.0, "RW")
-    for j, (s1, s2) in enumerate(((0, 15), (4, 7), (2, 3), (0, 3))):
-        ts(col(T.CI, j), T.PI[:], s1, s2, Op.logical_shift_right, Op.bitwise_and, "PI", "CI%d" % j)
-    quant("Q0", 0, 128, T.T0, "T0a T0b T0c T0d", "Q0")
-    for j, (s1, s2) in enumerate(((4, 1), (4, 3), (0, 1), (0, 127), (0, 7)), 4):
-        ts(col(T.CI, j), T.PI[:], s1, s2, Op.logical_shift_right, Op.bitwise_and, "PI", "CI%d" % j)
-    cp(T.CF[:, 0:9], T.CI[:, 0:9], " ".join("CI%d" % j for j in range(9)), "CF")
+    cg, ca, cs, ck, ch = (c1("CF", j) for j in range(5))
+    cPN, cSV, cOA, cBG, c64, cLM, cK1, cPZ = (c1("CD", j) for j in range(8))
+    oWQ, oV0, oG, oPN, oSV, oGR, oH, oI = (R("OU", a, b) for a, b in ((0, 8), (8, 16), (16, 22), (22, 25), (26, 27),
+                                                                       (28, 29), (32, 56), (56, 59)))
+    oF, oF0, oMG, oN1, oW0, oTK, oC1 = (R("OT", a, b) for a, b in ((0, 3), (4, 7), (8, 12), (12, 14), (14, 16),
+                                                                   (16, 18), (18, 19)))
 
-    for j, (src, dst, cast) in enumerate(((T.Q0c, T.LCc, _u8), (T.Q0s, T.LCs, _same))):
-        land = [(cores[q], cast(dst[:, Z0 + B0 * slot_at[q]:Z0 + B0 * (slot_at[q] + 1)])) for q in slots]
-        remote([(cast(src[:, Z0:Z0 + B0]), [land[k] for k in OFF], off, "e1"),
-                (cast(src[:, Z0:Z0 + B0]), land[1:2], on[j:j + 1], "e1")], "Q0")
-    E1 = (("e1", 2 * (6 * len(off) + 1)),)
-    dma("s", T.TW[:], T.w[:], "", "TW", E1)
+    def JB(n):
+        return R("JB", 0, n)
 
-    iota(W("RW", 0, 48), [[0, 8], [16, 2], [32, 3]], "RW0", "RW")
-    for k in range(2):
-        op("g", lambda k=k: g.iota(W("RW", 64 + 3 * k, 128, 8), [[3, 8]], 32 * k, 0, allow_small_or_imprecise_dtypes=True),
-           "RW", "RX%d" % k)
-    iota(W("RW", 128, 176), [[3, 2], [8, 8], [1, 3]], "RW2", "RW")
-    iota(W("RW", 192, 240), [[1, 16], [0, 3]], "RW3", "RW")
-    iota(W("OF", 40, 64), [[1, 8], [0, 3]], "OFh", "OF")
-    iota(W("TB1"), [[-16, 3], [1, 48]], "TB1")
-    iota(W("PYB"), [[4, 12], [513, 4]], "PYB")
-    iota(W("ILB"), [[0, 8], [4, 3]], "ILB")
-    iota(W("I96"), [[1, 12], [0, 8]], "I96")
-    iota(W("ILT"), [[1, 8], [32, 3]], "ILT")
-    iota(T.IR[:], [[0, 8], [1, 12], [0, 4]], "IR")
+    def quad(name, q, a, b):
+        return R(name, a, b, 1, (32 * q, 32 * q + 32))
 
-    ts(T.ID[:], T.J[:], cpp, None, Op.is_equal, None, "J CF", "ID")
-    act(W("OF", 0, 8), T.J[:, 0:8], "J OF", "OF0", scale=float(B0), bias=float(Z0 + P))
-    act(W("OF", 8, 16), T.J[:, 0:8], "J OF", "OF1", scale=0.0, bias=float(Z0 + P))
-    act(W("OF", 24, 30, 2), T.J[:, 0:3], "J OF CF", "OF3", scale=4.0, bias=cs)
-    act(W("OF", 25, 30, 2), T.J[:, 0:3], "J OF CF", "OF4", scale=4.0, bias=cs)
-    act(W("OF", 30, 31), ca1, "OF CF", "OF5", scale=16.0, bias=15.0)
+    dma("s", R("T0", 0, 4 * P), T.r0[:])
+    dma("a", R("T0", 4 * UQ), T.u[:, 0:8])
+    dma("s", R("T1", 0, 4 * K1), T.r1[:])
+    dma("s", R("T2"), T.r2[:])
+    iota(R("PI", 0, 3, 2), [[0, 2]], 0, 1, True)
+    iota(c1("PI", 1), [[0, 1]], 0, 16, True)
+    iota(c1("PI", 3), [[0, 1]], 0, 4, True)
+    iota(R("JB"), [[1, 128]])
+    iota(R("CP"), [[0, 1]], 0, 1)
+    ms(R("RW"), 0.0)
+    iota(R("RW", 0, 48, 2), [[0, 4], [16, 2], [32, 3]])
+    iota(R("RW", 65, 112, 2), [[0, 4], [16, 2], [0, 3]], 96)
+    iota(R("RW", 128, 192), [[6, 8], [48, 2], [2, 4]])
+    iota(R("JX"), [[(1 - 2 * (me >> i & 1)) << i, 2] for i in (2, 1, 0)], me)
+    ms(R("T0", 4 * P, 4 * UQ), 0.0)
+    ts(R("CI", 0, 2), R("PI", 0, 2), 4, 15, Op.logical_shift_right, Op.bitwise_and)
+    ts(R("CI", 2, 4), R("PI", 2, 4), 2, 3, Op.logical_shift_right, Op.bitwise_and)
+    ts(c1("CI", 4), c1("PI"), 4, 1, Op.logical_shift_right, Op.bitwise_and)
+    ms(R("OF"), 0.0)
+    cp(R("CF", 0, 5), R("CI", 0, 5))
+    ms(R("TE"), 0.0)
+    quant("Q0", 0, 128, "T0")
+
+    eng = _share(topo, cores, me, range(N))
+    far = [k for k in eng if topo.chip(cores[me ^ k]) != topo.chip(core)]
+    near = [k for k in eng if k not in far]
+    off = sorted(e for k in far for e in eng[k])
+    on = eng[near[0]]
+    for j, (x, cast) in enumerate((("c", u8), ("s", same))):
+        land = {k: (cores[me ^ k], cast(R("Q0" + x, UQ + 2 * k, UQ + 2 * k + 2))) for k in eng}
+        remote([(cast(R("Q0" + x, UQ, UQ + 2)), [land[k] for k in far], off, "e1")]
+               + [(cast(R("Q0" + x, UQ, UQ + 2)), [land[k]], on[2 * j:2 * j + 1], "e1") for k in near])
+    E1 = (("e1", 2 * (len(far) * len(off) + len(near))),)
+    for x, cast in (("c", u8), ("s", same)):
+        src = cast(R("Q0" + x, 0, P))
+        land = {k: (cores[me ^ k], cast(R("LC" + x, P * (k - 1), P * k))) for k in eng}
+        remote([(src, [land[k] for k in far], off, "e2")] + [(src, [land[k]], on[0:3:2], "e2") for k in near])
+    E2 = (("e2", 2 * (len(far) * len(off) + 2 * len(near))),)
+    dma("s", R("TW"), T.w[:], E2)
+    move("s", "L1", NA, "Q0", 32, 16)
+    move("s", "L2", 0, "Q0", 32, 16)
+    move("s", "L2", HW, "Q0", 32, 16)
+
+    iota(R("NT", 0, NA), [[0, N], [1, K1]])
+    iota(R("ILB", 0, 33), [[0, 11], [4, 3]])
+    act(R("JM", 0, 16), JB(16), Act.Copy)
+    for a in (16, 32, 64, 128, 256):
+        act(R("JM", a, min(2 * a, TW_)), R("JM", 0, min(a, TW_ - a)), Act.Copy)
+    act(R("OF", 0, 8), JB(8), scale=2.0, bias=float(UQ))
+    act(R("OF", 8, 16), JB(8), scale=4.0, bias=cs)
+    act(cPN, ch, scale=16.0, bias=cs)
+    act(cSV, ch, scale=16.0, bias=ca)
+    act(R("OF", 16, 22, 2), JB(3), scale=4.0, bias=cs)
+    act(R("OF", 17, 22, 2), JB(3), scale=4.0, bias=cs)
+    act(R("OF", 22, 25), JB(3), scale=4.0, bias=cPN)
+    act(c1("OF", 26), cSV, Act.Copy)
+    act(c1("OF", 28), cg, Act.Copy)
+    act(R("OF", 56, 60), JB(4), scale=16.0, bias=ca)
+    for j in range(3):
+        act(R("OF", 32 + j, 56, 3), JB(8), Act.Copy)
     for b in range(4):
-        cp(T.TE[:, 512 * b + b:512 * (b + 1):4], T.ID[:], "ID TE", "TE%d" % b)
-    ts(Wc("CD", 0), cg4, 48.0, ca, Op.mult, Op.add, "CF", "CD0")
-    ts(Wc("CD", 1), ch, 16.0, cs, Op.mult, Op.add, "CF", "CD1")
-    ts(Wc("CD", 14), cs, float(Z0), None, Op.add, None, "CF", "CD14")
-    ts(Wc("CD", 2), cg, 48.0, None, Op.mult, None, "CF", "CD2")
-    ts(Wc("CD", 3), ca, 8.0, None, Op.is_ge, None, "CF", "CD3")
-    ts(Wc("CD", 4), ca, float(CAP), None, Op.is_lt, None, "CF", "CD4")
-    ts(Wc("CD", 5), ca, -1.0, float(M), Op.mult, Op.add, "CF", "CD5")
-    ts(Wc("CD", 6), ck, 3.0, None, Op.is_lt, None, "CF", "CD6")
-    ts(Wc("CD", 7), ck, 4.0, cs, Op.mult, Op.add, "CF", "CD7")
-    ts(T.OI[:], T.J[:, 0:4], 16.0, ca, Op.mult, Op.add, "J CF", "OI")
-    ts(T.OZ[:], T.J[:, 0:2], 0.0, None, Op.mult, None, "J", "OZ")
-    ts(T.OU[:, 64:68], T.J[:, 0:4], 4.0, cs, Op.mult, Op.add, "J CF", "OUd")
-    act(W("OF", 16, 24), T.J[:, 0:8], "J OF CD14", "OF2", scale=4.0, bias=Wc("CD", 14))
-    act(W("OF", 32, 35), T.J[:, 0:3], "J OF CD0", "OF6", scale=16.0, bias=Wc("CD", 0))
-    act(W("OF", 36, 39), T.J[:, 0:3], "J OF CD1", "OF7", scale=4.0, bias=Wc("CD", 1))
-    act(Wc("CD", 8), cg, "CF", "CD8", scale=8.0, bias=ck)
-    act(Wc("CD", 9), ck, "CF", "CD9", bias=1.0)
-    act(Wc("CD", 10), ca, "CF", "CD10", bias=-float(NP))
-    act(Wc("CD", 11), Wc("CD", 7), "CD7", "CD11", scale=-1.0, bias=float(M))
-    act(Wc("CD", 13), cs, "CF", "CD13", Act.Copy, scale=8.0)
-    quant("QE", 0, 512, T.TE, "TE TE0 TE1 TE2 TE3", "QE")
-    cp(T.OU[:, 0:32], W("OF", 0, 32), "OF OF0 OF1 OF2 OF3 OF4 OF5", "OUa")
-    pick("LC", 0, 32, "Q0", T.OI[:, 0:2], "Q0 OI", "LC")
-    pick("L2", NP, NP + 16, "Q0", T.OZ[:, 0:1], "Q0 OZ", "Lz")
-    quant("Q1", 0, 128, T.T1, "T1a T1b", "Q1")
-    pick("V0", 0, 128, "Q0", oV0, "Q0 OUa", "V0")
-    for b in range(4):
-        mm("P%d" % b, "QE", 128 * b, "V0", 0, 128, "QE V0c V0s", True, False)
-        mm("P%d" % b, "QE", 128 * b, "Q1", 0, 128, "QE Q1", False, True)
-    ts(W("DM"), W("JM"), ca, None, Op.is_equal, None, "JM CF", "DM")
-    ts(W("R16"), W("JM"), 0.0, None, Op.is_gt, None, "JM", "R16")
-    ts(W("TT0"), W("TB0"), ca, -2 * BIG, Op.is_lt, Op.mult, "TB0 CF", "TT0")
-    ts(W("TE0"), W("TB0"), ca, -EPS, Op.is_lt, Op.mult, "TB0 CF", "TE0")
-    for s in range(2):
-        ts(T.R32[:, 32 * s:32 * s + 32], T.J[:, 0:32], 0.0, None, Op.is_gt, None, "J", "R32%d" % s)
+        ts(R("TE", 512 * b + b, 512 * (b + 1), 4), R("JB"), R("CP"), None, Op.is_equal)
+    ms(R("T1", 4 * K1), 0.0)
+    ms(R("OW"), UQ)
+    cp(R("OU"), R("OF", 0, 60))
     for s in range(3):
-        ts(T.R48[:, 48 * s:48 * s + 48], T.J[:, 0:48], 0.0, None, Op.is_gt, None, "J", "R48%d" % s)
-    ms(T.THG[:], 2.0, "THG")
-    ts(W("TT0"), W("TT0"), BIG, None, Op.add, None, "TT0", "TT0")
-    pick("WM", 0, 128, "Q0", oWM, "Q0 OUa", "WM")
-    ts(W("TT0", 0, P), W("TT0", 0, P), 0.0, None, Op.mult, None, "TT0", "TT1")
-    ts(W("TT0", 32, 32 + P), W("TT0", 32, 32 + P), Wc("CD", 3), None, Op.mult, None, "TT0 CD3", "TT2")
-    for k in range(1, N):
-        ms(T.THG[:, B0 * (k - 1):B0 * (k - 1) + P], -0.5 if slots[k] < me else 0.0, "THG%d" % k, "THG")
-    THG = "THG " + " ".join("THG%d" % k for k in range(1, N))
-    tt(T.TH0[:], W("TT0"), W("TE0"), Op.add, "TT0 TT1 TT2 TE0", "TH0")
+        act(R("TB1", 48 * s, 48 * s + 48), JB(48), bias=-16.0 * s)
+    act(c64, ca, scale=-1.0, bias=float(M))
+    quant("QE", 0, 512, "TE")
+    pick("V0", 0, 128, "Q0", oV0, (0, 128))
+    quant("Q1", 0, 128, "T1")
     for b in range(4):
-        act(T.A0[:, 96 * b:96 * (b + 1)], T["P%d" % b][:, 0:96], "P%d" % b, "A0%d" % b, Act.Copy)
-    ts(W("LM0"), T.J[:, 0:32], 0.0, Wc("CD", 5), Op.mult, Op.add, "J CD5", "LM0")
-    ms(T.NM[:], 0.0, "NM")
-    cp(T.OG[:, 0:1], cg, "CF", "OG")
-    ts(W("LM0"), W("LM0"), Wc("CD", 4), None, Op.mult, None, "LM0 CD4", "LM0")
-    ms(W("IL", 24, 32), 0.0, "ILp")
-    quant("Q2", 0, NP, T.T2, "T2", "Q2")
-    for k in range(2):
-        for c in (1, 2):
-            act(W("RW", 64 + 3 * k + c, 128, 8), W("RW", 64 + 3 * k, 128, 8), "RX%d" % k, "RY%d%d" % (k, c), bias=float(c))
-    tt(W("RM"), W("RW"), W("DM"), Op.mult, "RW RW0 RX0 RX1 RY01 RY02 RY11 RY12 RW2 RW3 DM", "RM")
-    ts(T.O96[:], T.J[:, 0:6], 0.0, ca7, Op.mult, Op.add, "J CF", "O96")
-    scan(W("RS"), W("R16"), W("RM"), "R16 RM", "RS")
-    cp(T.OU[:, 32:64], W("OF", 32, 64), "OF OF6 OF7 OFh", "OUb")
-    cp(T.OU[:, 72:88], W("RS", 15, 256, 16), "RS", "OUc")
-    ts(T.TH1[:], W("TB1"), ca, -EPS, Op.is_lt, Op.mult, "TB1 CF", "TH1")
-    act(W("PYC"), W("PYB"), "PYB CD2", "PYC", bias=Wc("CD", 2))
+        mm("P%d" % b, "QE", 128 * b, "V0", 0, 128, True, False)
+        mm("P%d" % b, "QE", 128 * b, "Q1", 0, 128, False, True)
+    for j in range(3):
+        act(R("J4", 4 * j, 4 * j + 4), JB(4), Act.Copy)
+        act(R("RW", 192 + j, 216, 3), JB(8), scale=8.0, bias=float(j))
+        act(R("RW", 256 + j, 280, 3), R("JX"), Act.Copy)
+    for j in range(2):
+        fill(R("RW", 288 + j, 304, 2), 8, 15.0 + 16 * j)
+    act(R("RW", 1, 48, 2), R("RW", 0, 48, 2), Act.Copy)
+    act(R("RW", 64, 112, 2), R("RW", 0, 48, 2), Act.Copy)
+    fill(R("RW", 131, 192, 8), 8, 96.0)
+    act(R("RW", 135, 192, 8), JB(8), scale=6.0, bias=49.0)
+    act(R("RW", 224, 248), R("RW", 192, 216), bias=4.0)
+    act(R("XG"), by(R("JX"), oGR), Act.Copy)
+    ts(R("TH1"), R("TB1"), ca, -EPS, Op.is_lt, Op.mult)
+    ts(R("DM"), R("JM"), ca, None, Op.is_equal)
+    ms(R("RR"), 1.0)
+    ms(R("R16"), 1.0)
+    ts(cLM, ca, float(CAP), c64, Op.is_lt, Op.mult)
+    ms(R("RR", 0, 290, 96), 0.0)
+    ms(R("R16", 0, TW_, 16), 0.0)
+    ts(R("MK", 0, 12), R("J4", 0, 12), cs, None, Op.is_equal)
+    pick("WM", 0, 128, "Q0", R("OW"), (0, 128))
+    for b in range(4):
+        act(R("A0", K1 * b, K1 * (b + 1)), R("P%d" % b, 0, K1), Act.Copy)
+    act(cBG, ca, Act.Relu, scale=BIG, bias=-7 * BIG)
+    act(c1("CM0", 48), ca, Act.Relu, scale=24.0, bias=-168.0)
+    act(cOA, ch, scale=float(K1), bias=ck)
+    act(R("PY0"), JB(32), scale=4.0, bias=float(K1 * me - NA))
+    act(R("TH0", 0, P), R("TH1", 0, P), Act.Copy)
+    act(R("TH0", P, 2 * P), R("TH1", 48, 48 + P), bias=cBG)
+    act(cOA, cOA, bias=float(NA - K1 * me))
+    for a, b in ((1, 2), (2, 4), (4, 8)):
+        fill(R("THG", P * (a - 1), P * (b - 1)), P * (b - a), -0.5 if (me ^ a) < me else 0.0)
+    fill(R("LM"), 32, cLM)
+    act(R("KF", 1, 48, 2), R("OF", 32, 56), scale=float(K1))
+    act(cPZ, ca, bias=16.0)
+    act(cK1, ck, bias=1.0)
+    for h in range(2):
+        act(R("PLZ", 12 * h, 12 * h + 12), JB(12), scale=16.0, bias=cPZ)
+    quant("Q2", 0, NP, "T2")
+    tt(R("RM"), R("RW"), R("DM"), Op.mult)
+    ts(c1("ON"), c1("XG"), 8.0, 3.0, Op.mult, Op.add)
+    scan(R("RS"), R("R16"), R("RM"))
+    ts(R("TA"), JB(8), c1("XG"), -EPS, Op.is_lt, Op.mult)
+    ts(R("TB"), JB(8), c1("XG"), 4 * BIG, Op.is_equal, Op.mult)
+    cp(R("OT"), R("RS", 15, TW_, 16))
+    tt(R("TH8"), R("TA"), R("TB"), Op.add)
+    ms(R("KF", 0, 48, 2), 0.0)
+    ms(R("MS", 97, 104), 0.0)
+    ms(R("NT", NA), -1.0)
 
-    pick("WQ", 0, 128, "LC", oWQ, "LCc OUa", "WQ", E1)
-    for b in range(2):
-        mm("P%d" % b, "QE", 128 * b, "LC", 0, NL, "QE LCc LCs", arrive=E1)
-    mm("P4", "WQ", 0, "LC", 0, NL, "WQc WQs")
-    for b in range(2, 4):
-        mm("P%d" % b, "QE", 128 * b, "LC", 0, NL, "QE")
-    tt(W("M0"), T.P4[:, Z0:Z0 + 32], W("DM", 0, 32), Op.mult, "P4 DM", "M0")
-    cp(W("AS"), T.P4[:, Z0:Z0 + 32], "P4", "AS")
-    scan(W("BS0"), W("R16", 0, 32), W("M0"), "R16 M0", "BS0")
-    for s in range(2):
-        ts(T.D0[:, 32 * s:32 * s + 32], W("AS"), Wc("BS0", 16 * s + 15), None, Op.subtract, None, "AS BS0", "D0%d" % s)
-    tt(T.CM0[:], T.D0[:], T.TH0[:], Op.is_gt, "D00 D01 TH0", "CM0")
-    scan(T.SN0[:], T.R32[:], T.CM0[:], "R320 R321 CM0", "SN0")
-    cp(T.OL0[:], T.SN0[:, 31:64:32], "SN0", "OL0")
-    cp(W("SR0").indirect(T.OL0[:]), W("PY0"), "OL0 PY0", "SR0")
-    cp(W("SS").indirect(T.OL0[:]), W("AS"), "OL0 AS", "SS")
-    cp(W("G0"), W("SR0").indirect(oG), "SR0 OUa", "G0")
-    tt(W("MS"), W("SS", 0, 16), W("DM", 0, 16), Op.mult, "SS DM", "MS")
-    tr(W("GT0"), W("G0"), "G0", "GT0")
-    red(Wc("NS"), W("MS"), "MS", "NS", True)
-    cp(T.FA[:, 0:32], W("GT0").indirect(oF), "GT0 OUc", "F0")
-    for b in range(4):
-        act(T.DH[:, 8 * b:8 * b + 8], T["P%d" % b][:, Z0 + P + 1:NL:B0], "P%d" % b, "DH%d" % b, Act.Copy)
+    pick("WQ", 0, 128, "Q0", oWQ, (0, NL), E1)
     for b in range(3):
-        act(T.H[:, NP * b:NP * (b + 1)], T.DH[:, 8 * b:8 * b + 8].indirect(oH), "DH%d OUb" % b, "H%d" % b, Act.Copy)
-    act(T.SG[:], T.P4[:, 32:NL], "P4 NS", "SG", Act.Sign, bias=Wc("NS"))
-    F0 = spread(T.FA, 0, 6, "F0")
-    ts(T.L0[:], T.FA[:, 0:24], 1.0 / 512, ck, Op.mult, Op.add, F0 + " CF", "L0")
-    ts(T.L0b[:, 1:25], T.FA[:, 0:24], 1.0 / 512, ck, Op.mult, Op.add, F0 + " CF", "L0b")
-    keys = []
-    for b, n in ((0, 8), (1, 8), (2, 6)):
-        keys.append("X1%d" % b)
-        tt(T.X1[:, b:4 * S * n:4], T.A0[:, 96 * b:96 * (b + 1)].indirect(T.L0[:, 0:3 * n]), T.H[:, NP * b:NP * b + S * n],
-           Op.add, "A0%d L0 H%d" % (b, b), keys[-1])
-        if b == 0:
-            tt(T.CG[:], T.SG[:], T.THG[:], Op.is_gt, "SG " + THG, "CG")
-        if b == 1:
-            ts(W("FL0"), W("LM0"), Wc("CN0"), None, Op.is_gt, None, "LM0 CN0", "FL0")
-        if b == 0:
-            for i, (bb, k) in enumerate([(3, k) for k in range(N)] + [(2, 6), (2, 7)]):
-                lst = T.L0b[:, 3 * k + 1:3 * k + 4] if k % 2 else T.L0[:, 3 * k:3 * k + 3]
-                keys.append("X1%d%d" % (bb, k))
-                act(T.X1[:, 4 * S * k + bb:4 * S * (k + 1):4], T.A0[:, 96 * bb:96 * (bb + 1)].indirect(lst),
-                    "A0%d L0 DH%d" % (bb, bb) + (" L0b" if k % 2 else ""), keys[-1], bias=col(T.DH, 8 * bb + k))
-                if i == 5:
-                    act(T.JK[:], T.CG[:], "CG", "CN0", Act.Copy, accum_out=Wc("CN0"))
-    tr(W("FT0"), W("FL0"), "FL0", "FT0")
-    quant("C1", 0, 192, T.X1, " ".join(keys), "C0")
-    quant("C1", 192, NP, T.X1, " ".join(keys), "C1")
-    mm("P5", "WQ", 0, "C1", 0, 192, "C0")
-    mm("P6", "WQ", 0, "C1", 192, NP, "C1")
+        mm("P%d" % b, "QE", 128 * b, "Q0", NL - 128, NL, arrive=E1)
+    mm("P4", "WQ", 0, "Q0", 0, 128)
+    mm("P3", "QE", 128 * 3, "Q0", NL - 128, NL)
+    for b in range(4):
+        act(R("DH", 8 * b, 8 * b + 8), R("P%d" % b, 128 - 2 * N + 1, 128, 2), Act.Copy)
 
-    for j, (src, rl, dst, cast, sem) in enumerate(((T.C1c, T.RLc, T.L1c, _u8, "rc"), (T.C1s, T.RLs, T.L1s, _same, "rs"))):
-        if RELAY == 1:
-            eng = _deal(off + on, (4, 4, 4, 4))
-            remote([(cast(src[:, 96 * i:96 * (i + 1)]),
-                     [(plan[me]["hb" if i < 2 else "ha"], cast(rl[:, 96 * (i % 2):96 * (i % 2 + 1)]))], eng[3 - i], sem)
-                    for i in range(4)], "C0 C1")
-        elif RELAY == 2:
-            remote(direct(src, dst, cast, S, (1, 4, 5, 6, 7), ENG_P1[j], "p1")
-                   + [(cast(src[:, S * k:S * (k + 1)]), [(plan[me][h], cast(rl[:, 0:S]))], on[2 * k - 2:2 * k], sem)
-                      for k, h in ((2, "hb"), (3, "hc"))], "C0 C1")
+    def child(q, k, b):
+        o, i, h = R("X1", 4 * K1 * k + b, 4 * K1 * (k + 1), 4), R("A0", K1 * b, K1 * (b + 1)), c1("DH", 8 * b + k)
+        if q == "v":
+            ts(o, i, h, None, Op.add)
         else:
-            remote(direct(src, dst, cast, S, range(N), ENG_P1[j], "p1"), "C0 C1")
-    P1 = arrivals("p1", *ENG_P1)
+            act(o, i, bias=h)
 
-    ts(W("VL"), W("FT0").indirect(oPN), 16384.0, None, Op.mult, None, "FT0 OUb", "VL")
-    tt(W("PA"), W("SR0").indirect(oJ4), W("PYC"), Op.add, "SR0 OUd PYC", "PA")
-    ts(W("PEN"), W("VL"), -16384.0, BIG / 16384, Op.add, Op.mult, "VL", "PEN")
-    act(T.AF[0:64, :], T.P5[0:64, 0:192], "P5", "AFa", Act.Copy)
-    cp(T.AF[64:128, :], T.P6[64:128, 0:192], "P6", "AFb")
-    act(W("IL", 0, 24), W("ILB"), "ILB CF", "IL", bias=cs)
-    act(W("PLZ"), T.J[:, 0:24], "J CD10", "PLZ", scale=16.0, bias=Wc("CD", 10))
-    act(T.IRB[:], T.IR[:], "IR", "IRB", scale=65536.0 * UP, bias=65535.5 * UP)
-    for q in range(N):
-        act(Wc("ADJ", q), Wc("CD", 6), "CD6", "ADJ%d" % q, Act.Copy, scale=float(S * (q - slot_at[q])))
-    act(W("AD2"), W("ADJ").indirect(T.OG[:, 0:1]), "OG " + " ".join("ADJ%d" % q for q in range(N)), "AD2", Act.Copy)
-    red(Wc("CC"), W("VL"), "VL", "CC")
-    tt(W("A1"), T.AF[:].indirect(oA1), W("PEN"), Op.add, "AFa AFb OUb PEN", "A1")
-    ts(W("PB"), W("PA"), Wc("CC"), None, Op.add, None, "PA CC", "PB")
-    tt(W("M1"), W("A1"), W("DM", 0, 48), Op.mult, "A1 DM", "M1")
-    scan(W("BS1"), W("R16", 0, 48), W("M1"), "R16 M1", "BS1")
+    xa = [(k, b) for k in XA for b in range(4)][:XN]
+    xv = [(k, b) for k in XV for b in range(4) if (k, b) not in xa]
+    tt(R("M0"), R("P4", 0, 32), R("DM", 0, 32), Op.mult)
+    cp(R("AS"), R("P4", 0, 32))
+    scan(R("BS0"), R("R16", 0, 32), R("M0"))
+    for s in range(2):
+        ts(R("D0", P * s, P * s + P), R("AS", 0, P), c1("BS0", 16 * s + 15), None, Op.subtract)
+    tt(R("CM0", 0, 48), R("D0"), R("TH0"), Op.is_gt)
+    scan(R("SN0", 0, 49), R("RR", 48, 146, 2), R("CM0", 0, 49))
+    cp(R("OL0"), R("SN0", 23, 49, 25))
+    cp(by(R("SS0"), R("OL0")), R("AS"))
+    cp(by(R("SR0"), R("OL0")), R("PY0"))
+    tt(R("MS0"), R("SS0", 0, 16), R("DM", 0, 16), Op.mult)
+    tt(R("SE", 0, 12), R("SR0", 0, 12), R("MK", 0, 12), Op.mult)
+    red(c1("NS"), R("MS0"), True)
+    scan(R("SF", 0, 12), R("RR", 0, 288, 24), R("SE", 0, 12))
+    for kb in xa[:22]:
+        child("a", *kb)
+    for kb in xv[:2]:
+        child("v", *kb)
+    ts(R("OA", 0, 3), R("SF", 3, 12, 4), cOA, None, Op.add)
+    for kb in xv[2:8]:
+        child("v", *kb)
+    mm("P3", "WQ", 0, "LC", 0, NO, arrive=E2)
+    act(R("SG"), R("P3", 0, NO), Act.Sign, bias=c1("NS"))
+    quant("C1", NA // 2, NA, "X1")
+    mm("P6", "WQ", 0, "C1", NA // 2, NA)
+    for kb in xa[22:]:
+        child("a", *kb)
+    quant("C1", 192, NA // 2, "X1")
+    mm("P7", "WQ", 0, "C1", 192, NA // 2)
+    tt(R("CG"), R("SG"), R("THG"), Op.is_gt)
+    act(R("JK", 0, NO), R("CG"), Act.Copy, acc=c1("CN0"))
+    for kb in xv[8:]:
+        child("v", *kb)
+    quant("C1", 0, 192, "X1")
+    mm("P5", "WQ", 0, "C1", 0, 192)
+    ts(R("FL0"), R("LM"), c1("CN0"), None, Op.is_gt)
+    tr(R("FT0"), R("FL0"))
+    ts(R("PEN"), by(R("FT0"), oPN), -1.0, BIG, Op.add, Op.mult)
+    for k0, k1 in PARTS:
+        for x, cast in (("c", u8), ("s", same)):
+            direct("C1" + x, "L1" + x, cast, K1, K1 * me, range(k0, k1), "p1", "1")
+    P1 = arrivals("p1", 2, "1", *[range(*p) for p in PARTS])
+    move("s", "L1", K1 * me, "C1", 0, K1)
+
+    for q in (2, 3):
+        act(quad("AF", q, 0, 192), quad("P6", q, 192 * (q % 2), 192 * (q % 2 + 1)), Act.Copy)
+    act(quad("AF", 1, 0, 192), quad("P7", 1, 0, 192), Act.Copy)
+    cp(quad("AF", 0, 0, 192), quad("P5", 0, 0, 192))
+    tt(R("SV"), by(R("FT0"), oSV), R("SR0", 0, 16), Op.mult)
+    act(R("PB"), by(R("NT", 0, 192), R("OA", 0, 3)), Act.Copy)
+    act(R("JK", 0, 48), R("PEN"), Act.Copy, scale=1.0 / BIG, acc=c1("NI"))
+    act(R("G0", 0, 96), by(R("SV"), oG), bias=float(NA))
+    fill(R("G0", 96, 128), 32, c1("NI"))
+    act(R("H", 0, NP), by(R("DH", 0, 8), oH), Act.Copy)
+    tt(R("A1"), by(R("AF"), R("OA", 0, 3)), R("PEN"), Op.add)
+    tt(R("M1"), R("A1"), R("DM", 0, 48), Op.mult)
+    scan(R("BS1"), R("R16", 0, 48), R("M1"))
+    tr(R("GT0"), R("G0"))
     for s in range(3):
-        ts(T.D1[:, 48 * s:48 * s + 48], W("A1"), Wc("BS1", 16 * s + 15), None, Op.subtract, None, "A1 BS1", "D1%d" % s)
-    tt(T.CM1[:], T.D1[:], T.TH1[:], Op.is_gt, "D10 D11 D12 TH1", "CM1")
-    scan(T.SN1[:], T.R48[:], T.CM1[:], "R480 R481 R482 CM1", "SN1")
-    cp(T.OL1[:, 0:3], T.SN1[:, 47:144:48], "SN1", "OL1")
-    cp(W("SR1").indirect(T.OL1[:, 0:3]), W("PB"), "OL1 PB", "SR1")
-    cp(W("G1"), W("SR1").indirect(oG), "SR1 OUa", "G1")
-    tr(W("GT1"), W("G1"), "G1", "GT1")
-    cp(T.FA[:, 32:64], W("GT1").indirect(oF), "GT1 OUc", "F1")
-    F1 = spread(T.FA, 32, 6, "F1")
-    ts(T.LI[:, 0:24], T.FA[:, 32:56], 511, None, Op.bitwise_and, None, F1, "LIa")
-    ts(T.LI[:, 24:48], T.FA[:, 32:56], 9, 127, Op.logical_shift_right, Op.bitwise_and, F1, "LIb")
-    ts(T.MG[:], T.FA[:].indirect(oMG), UP, None, Op.mult, None, F0 + " " + F1 + " OUc", "MG")
-    cp(T.LV[:], T.LI[:, 0:24], "LIa", "LV")
-    ts(T.LE[:], T.LI[:, 24:48], 4.0, ck, Op.mult, Op.add, "LIb CF", "LE")
-    remote(direct(T.MG, T.ML, _same, 8, range(N), ENG_MS, "ms"), "MG")
-    MS = arrivals("ms", ENG_MS)
+        ts(R("D1", 48 * s, 48 * s + 48), R("A1"), c1("BS1", 16 * s + 15), None, Op.subtract)
+    tt(R("CM1"), R("D1"), R("TH1"), Op.is_gt)
+    scan(R("SN1"), R("RR", 0, 288, 2), R("CM1"))
+    cp(R("OL1", 0, 3), R("SN1", 47, 144, 48))
+    act(R("MS", 48, 96), by(R("GT0"), oF0), Act.Copy)
+    spread("MS", 48, 12, "aa")
+    act(R("H", NP, 2 * NP), by(R("DH", 8, 16), oH), Act.Copy)
+    cp(by(R("SR1"), R("OL1", 0, 3)), R("PB"))
+    cp(R("G1"), by(R("SR1"), oG))
+    cp(by(R("SS1"), R("OL1", 0, 3)), R("A1"))
+    tr(R("GT1"), R("G1"))
+    tt(R("MS1"), R("SS1", 0, 16), R("DM", 0, 16), Op.mult)
+    tt(R("MS", 0, 48), by(R("GT1"), oF), R("KF"), Op.add)
+    act(R("MS2"), R("MS1"), Act.Copy, acc=c1("MS", 96))
+    spread("MS", 0, 12)
+    cp(R("LV"), R("MS", 1, 48, 2))
+    ts(R("LE"), R("MS", 0, 48, 2), 4.0, ck, Op.mult, Op.add)
+    act(R("MG"), by(R("MS"), oMG), Act.Copy)
+    direct("MG", "ML", same, 8, 8 * me, range(N), "ms", "m")
+    MS = arrivals("ms", 1, "m", range(N))
+    for k0, k1 in PARTS:
+        pick("PV", S * k0, S * k1, "C1", R("LV", 3 * k0, 3 * k1))
+        pick("PE", S * k0, S * k1, "Q2", R("LE", 3 * k0, 3 * k1))
+    order = (0, 2, 1, 3)
     for i, (k0, k1) in enumerate(PARTS):
-        pick("PV", S * k0, S * k1, "C1", T.LV[:, 3 * k0:3 * k1], "C0 C1 LV", "PV%d" % i)
-        pick("PE", S * k0, S * k1, "Q2", T.LE[:, 3 * k0:3 * k1], "Q2 LE", "PE%d" % i)
-    order = (3, 0, 1, 2)
+        for src, first in (("PV", True), ("PE", False)):
+            for j in order:
+                mm("P%d" % (4 * i + j), "QE", 128 * j, src, S * k0, S * k1, first, not first)
+    at2 = _at2(me)
     for i, (k0, k1) in enumerate(PARTS):
         a, b = S * k0, S * k1
-        for j in order:
-            mm("P%d" % (4 * i + j), "QE", 128 * j, "PV", a, b, "QE PV%dc PV%ds" % (i, i), True, False)
-        for j in order:
-            mm("P%d" % (4 * i + j), "QE", 128 * j, "PE", a, b, "QE PE%dc PE%ds" % (i, i), False, True)
-    for i, (k0, k1) in enumerate(PARTS):
-        a, b = S * k0, S * k1
-        keys = []
-        for k in range(k0, k1):
-            keys.append("X23%d" % k)
-            act(T.X2[:, 4 * S * k + 3:4 * S * (k + 1):4], T["P%d" % (4 * i + 3)][:, S * (k - k0):S * (k - k0 + 1)],
-                "P%d DH3" % (4 * i + 3), keys[-1], bias=col(T.DH, 24 + k))
-        for j in range(3):
-            keys.append("X2%d%d" % (j, i))
-            tt(T.X2[:, 4 * a + j:4 * b:4], T["P%d" % (4 * i + j)][:, 0:b - a], T.H[:, NP * j + a:NP * j + b], Op.add,
-               "P%d H%d" % (4 * i + j, j), keys[-1])
-        quant("C2", a, b, T.X2, " ".join(keys), "C2%d" % i)
-        for j, (src, dst, cast) in enumerate(((T.C2c, T.L2c, _u8), (T.C2s, T.L2s, _same))):
-            remote(direct(src, dst, cast, S, range(k0, k1), ENG_P2[j], "p2", 2 * j * (RELAY > 0)), "C2%d" % i)
-    P2 = arrivals("p2", *ENG_P2)
+        for j in (2, 3):
+            for k in range(k0, k1):
+                act(R("X2", 4 * S * k + j, 4 * S * (k + 1), 4), R("P%d" % (4 * i + j), S * (k - k0), S * (k - k0 + 1)),
+                    bias=c1("DH", 8 * j + k))
+        for j in range(2):
+            tt(R("X2", 4 * a + j, 4 * b, 4), R("P%d" % (4 * i + j), 0, b - a), R("H", NP * j + a, NP * j + b), Op.add)
+        if i == 0:
+            quant("QW", 0, 128, "TW")
+        quant("C2", a, b, "X2")
+        for x, cast in (("c", u8), ("s", same)):
+            direct("C2" + x, "L2" + x, cast, S, at2, range(k0, k1), ("pa", "pb")[i], "2")
+    P2 = [arrivals(("pa", "pb")[i], 2, "2", range(*p)) for i, p in enumerate(PARTS)]
 
-    cp(T.ML[:, 8 * me:8 * me + 8], T.MG[:, 0:8], "MG", "ML")
-    pick("L1", S * me, S * (me + 1), "C1", T.OI[:, 0:3], "C0 OI", "L1")
-    quant("QW", 0, 128, T.TW, "TW", "QW")
-    ms(W("M64", 0, 3), 0.0, "M4a")
-    ts(W("M64", 3, 64), T.J[:, 0:61], Wc("CD", 8), Wc("CD", 6), Op.is_equal, Op.mult, "J CD8 CD6", "M64")
-    ts(T.LP[:], W("OF", 40, 64), 8.0, 3.0, Op.mult, Op.add, "OFh", "LP")
-    ts(W("TA8"), T.J[:, 0:8], cg, -EPS, Op.is_lt, Op.mult, "J CF", "TA8")
-    ts(W("TA9"), T.J[:, 0:8], cg, 5 * BIG, Op.is_equal, Op.mult, "J CF", "TA9")
-    ts(W("LM1"), T.J[:, 0:32], 0.0, Wc("CD", 11), Op.mult, Op.add, "J CD11", "LM1")
-    tt(W("TAa"), W("TA8"), W("TA9"), Op.add, "TA8 TA9", "TAa")
-    ts(W("LM1"), W("LM1"), Wc("CD", 6), None, Op.mult, None, "LM1 CD6", "LM1")
-    ts(T.LT[:], W("ILT"), Wc("CD", 13), None, Op.add, None, "ILT CD13", "LT")
-    pick("L2", S * me, S * (me + 1), "C2", T.OI[:, 0:3], "C2%d OI" % (len(PARTS) - 1), "L2")
-    act(T.THA[:], W("TAa").indirect(oH), "TAa OUb", "THA", Act.Copy)
-    ba, by1, by2 = ("P0", "P1", "P2") if len(PARTS) == 2 else ("P4", "P5", "P6")
-    mm(ba, "WM", 0, "L1", 0, NP, "WMc WMs L1c L1s", arrive=P1)
-    mm(by1, "QW", 0, "L1", 0, NP, "QW")
-    tt(W("PM"), T.ML[:], W("M64"), Op.mult, "ML M4a M64", "PM", MS)
-    tt(T.Z[:], T.ML[:].indirect(T.LP[:]), T.IRB[:], Op.subtract, "ML LP IRB", "Z")
-    red(Wc("PC"), W("PM"), "PM", "PC")
-    ts(T.U[:], T.ML[:].indirect(oUN), 1.0 / UP, None, Op.mult, None, "ML OUc", "U")
-    ts(T.PJ[:, 0:1], Wc("PC"), 1.0 / UP, None, Op.mult, None, "PC", "PJa")
-    ts(T.DI[:, 0:24], T.U[:, 24:48], 16, None, Op.logical_shift_right, None, "U", "DIa")
-    ts(T.PJ[:, 1:2], T.PJ[:, 0:1], 511, None, Op.bitwise_and, None, "PJa", "PJb")
-    tt(T.AM[:], T[ba][:, 0:NP], T.Z[:], Op.min, ba + " Z", "AM")
-    ts(T.OP[:, 0:1], T.PJ[:, 1:2], Wc("AD2"), None, Op.add, None, "PJb AD2", "OP")
-    ts(T.DI[:, 24:48], T.U[:, 24:48], 9, 127, Op.logical_shift_right, Op.bitwise_and, "U", "DIc")
-    act(T.VS[:], T.Z[:], "Z", "VS", Act.Sign)
-    act(T.VM[:], T.VS[:], "VS", "VM", Act.Relu)
-    tt(W("GI"), T.AM[:].indirect(T.OP[:, 0:1]), W("DM", 0, 16), Op.mult, "AM OP DM", "GI")
-    cp(W("DF"), T.DI[:], "DIa DIc", "DF")
-    red(Wc("SI"), W("GI"), "GI", "SI", True)
-    act(T.DA[:, 192:NP], T.AM[:, 192:NP], "AM SI", "DAb", Act.Sign, bias=Wc("SI"))
-    act(T.DA[:, 0:192], T.AM[:, 0:192], "AM SI", "DAa", Act.Sign, bias=Wc("SI"))
-    tt(T.YS[:, 0:NP], T[by1][:, 0:NP], T.VM[:], Op.mult, by1 + " VM", "Y1")
-    dma("s", T.y[:, 0:NP], T.YS[:, 0:NP], "Y1", "o3")
-    tt(T.CA[:, 192:NP], T.DA[:, 192:NP], T.THA[:, 192:NP], Op.is_gt, "DAb THA", "CAb")
-    act(T.VS[:, 192:NP], T.CA[:, 192:NP], "CAb VM", "CN2", Act.Copy, accum_out=Wc("CN1", 1))
-    tt(T.CA[:, 0:192], T.DA[:, 0:192], T.THA[:, 0:192], Op.is_gt, "DAa THA", "CAa")
-    ts(W("NA"), T.U[:, 0:24], 1.0 / 512, Wc("CD", 9), Op.mult, Op.add, "U CD9", "NA")
-    red(Wc("CN1"), T.CA[:, 0:192], "CAa", "CN1")
-    tt(W("V1"), W("DF", 0, 24), W("IL", 0, 24), Op.is_gt, "DF IL", "V1")
-    ts(W("FL1"), W("LM1"), Wc("CN1", 1), Wc("CN1"), Op.subtract, Op.is_gt, "LM1 CN1 CN2", "FL1")
-    ts(W("NB"), W("DF", 24, 48), 4.0, Wc("CD", 9), Op.mult, Op.add, "DF CD9", "NB")
-    tr(W("FT1"), W("FL1"), "FL1", "FT1")
-    tt(T.NM[:, 0:24], W("NA"), W("V1"), Op.mult, "NA V1 NM", "NMa")
-    scan(W("FS1"), W("R16", 0, 32), W("FT1"), "R16 FT1", "FS1")
-    cp(W("C1A"), W("FS1").indirect(oC1), "FS1 OUa", "CA1")
-    CA = spread(T.WB, PIECE["C1A"][1], 2, "CA1")
-    tt(W("TK"), W("C1A").indirect(oTK), W("IL"), Op.is_gt, CA + " OUc IL ILp", "TK")
-    tt(W("F96"), W("C1A").indirect(T.O96[:]), W("I96"), Op.is_gt, CA + " O96 I96", "F96")
-    tt(W("LZ"), W("TK", 0, 24), W("PLZ"), Op.mult, "TK PLZ", "LZ")
-    tt(T.NM[:, 32:56], W("TK", 0, 24), W("NB"), Op.mult, "TK NB NM", "NMb")
-    ts(T.LQ[:], W("LZ"), float(NP), None, Op.add, None, "LZ", "LQ")
-    act(T.TM[:], W("F96").indirect(T.LT[:]), "F96 LT", "TM", Act.Copy)
+    act(R("ML", 8 * me, 8 * me + 8), R("MG", 0, 8), Act.Copy)
+    act(R("IL"), R("ILB", 0, 32), bias=cs)
+    pick("L2", at2, at2 + S, "C2", oI)
+    ts(R("LP"), by(R("ML"), oW0), ck, None, Op.add, arrive=MS)
+    pick("P1", 0, NP, "L1", R("LP", 0, 24), arrive=P1)
+    mm("P0", "WM", 0, "P1", 0, NP)
+    mm("P1", "QW", 0, "P1", 0, NP)
+    cp(R("SA"), by(R("ML"), c1("ON")))
+    ts(R("ZF"), R("TH8"), c1("SA"), 0.0, Op.add, Op.is_lt)
+    ts(R("NB"), by(R("ML"), oN1), 4.0, cK1, Op.mult, Op.add)
+    tt(R("CA", NP), R("ZF"), R("ML", 7, 64, 8), Op.mult)
+    for q in (4, 5, 6, 7, 0, 1, 2, 3):
+        ts(R("CA", S * q, S * (q + 1)), R("P0", S * q, S * (q + 1)), c1("SA"), c1("TH8", q), Op.subtract, Op.is_gt)
+    act(R("NR"), by(R("NT"), R("LP", 0, 24)), Act.Copy)
+    act(R("JK", 0, 200), R("CA", 192), Act.Copy, acc=c1("CN1", 1))
+    act(R("YS", 0, NP), R("P1", 0, NP), Act.Copy)
+    out = [dma("s", T.nm[0:1, 0:NP], R("NR", 0, NP, 1, (0, 1))),
+           dma("s", T.y[:, 0:NP], R("YS", 0, NP), (("sent", sent[0]),))]
+    red(c1("CN1"), R("CA", 0, 192))
+    ts(R("FL1"), R("LM"), c1("CN1", 1), c1("CN1"), Op.subtract, Op.is_gt)
+    tr(R("FT1"), R("FL1"))
+    scan(R("FS1"), R("R16", 0, 32), R("FT1"))
+    cp(R("C8"), by(R("FS1"), oC1))
+    spread("C8", 0, 2)
+    tt(R("TK"), by(R("C8"), oTK), R("IL"), Op.is_gt)
+    tt(R("LZ"), R("TK", 0, 24), R("PLZ"), Op.mult)
+    tt(quad("NM", 0, 0, 32), quad("TK", 0, 0, 32), quad("NB", 0, 0, 32), Op.mult)
+    cp(R("LQ"), R("LZ"))
+    act(quad("NN", 0, 0, 32), quad("NM", 0, 0, 32), bias=-1.0)
 
-    mm(by2, "QW", 0, "L2", 0, NP, "QW L2c L2s", arrive=P2)
-    pick("OC", 0, NP, "L2", T.LQ[:], "L2c Lzc LQ", "OC", P2)
-    dma("s", T.oc[:], _u8(T.OCc[:]), "OCc", "o4")
-    tt(T.YS[:, NP:2 * NP], T[by2][:, 0:NP], T.TM[:], Op.mult, by2 + " TM", "Y2")
-    dma("s", T.y[:, NP:2 * NP], T.YS[:, NP:2 * NP], "Y2", "o5")
-    ts(T.NN[0:32, :], T.NM[0:32, :], -1.0, None, Op.add, None, "NM NMa NMb", "NN")
-    tr(T.NT[0:32, :], T.NN[0:32, :], "NN", "NT")
-    dma("s", T.nm[0:1, 0:NP], T.NT[0:24, 0:16], "NT", "o1")
-    dma("s", T.nm[0:1, NP:2 * NP], T.NT[0:24, 32:48], "NT", "o2")
-    for k in range(4):
-        dma("a", T.osc[4 * k:4 * k + 4, :], T.OCs[32 * k:32 * k + 4, :], "OCs", "o%d" % (6 + k))
-    op("s", None, "o1 o2 o3 o4 o5", "")
-    op("a", None, "o6 o7 o8 o9", "")
-    op("g", None, "", "", (("sent", sent[0]),))
+    halves = [(me ^ k0) // 4 for k0, _ in PARTS]
+    for i, h in enumerate(halves):
+        pick("OC", 192 * h, 192 * (h + 1), "L2", R("LQ", 12 * h, 12 * h + 12), (HW * h, HW * h + 208), P2[i])
+        mm("P%d" % (2 + i), "QW", 0, "OC", 192 * h, 192 * (h + 1))
+        out.append(dma("s", T.oc[:, 768 * h:768 * (h + 1)], u8(R("OCc", 192 * h, 192 * (h + 1)))))
+        if i == 0:
+            tr(quad("NU", 0, 0, 32), quad("NN", 0, 0, 32))
+            out.append(dma("s", T.nm[0:1, NP:2 * NP], R("NU", 0, 16, 1, (0, 24))))
+    oa = [dma("a", T.osc[4 * k:4 * k + 4, :], R("OCs", 0, NP, 1, (32 * k, 32 * k + 4))) for k in range(4)]
+    for i, h in enumerate(halves):
+        a = NP + 192 * h
+        cp(R("YS", a, a + 192), R("P%d" % (2 + i), 0, 192))
+        out.append(dma("s", T.y[:, a:a + 192], R("YS", a, a + 192)))
+    op("s", None, after=out)
+    op("a", None, after=oa)
+    op("g", None, arrive=(("sent", sent[0]),))
 
     known, at_issue, waits, needed = {q: 0 for q in queues}, [], [], set()
     for i, o in enumerate(ops):

@@ -10,8 +10,8 @@ NA, NP = N * K1, N * S
 HW = 224
 EPS, BIG = 1e-37, 2.0 ** 80
 PARTS = ((4, 8), (0, 4))
-XA, XV, XN = (4, 5, 6, 7, 0, 1), (3, 2, 1), 24
-RELAY = {"1": 2, "m": 0, "2": 0}
+XA, XN = (4, 5, 6, 7, 1, 2, 3), 26
+VIA = 2
 TW_ = 320
 
 F, BF, I32, U16, C, SC = "float32", "bfloat16", "int32", "uint16", "float8_e4m3fn_x4", "uint8"
@@ -23,15 +23,15 @@ def _sb(dtype, **kw):
         SCRATCH[name] = ("sbuf", [128, n], dtype)
 
 
-_sb(BF, T0=512, T1=512, T2=4 * NP, TW=512, TE=2048, JB=128, H=2 * NP, X1=4 * NA, X2=4 * NP, RR=290, R16=TW_, DM=TW_,
-    JM=TW_, RW=TW_, RM=TW_, RS=TW_, TH0=48, TB1=144, TH1=144, D0=48, CM0=50, SN0=50, D1=144, CM1=144, SN1=144,
-    THG=NO, SG=NO, CG=NO, JK=208, CA=NP + 8, NT=NA + 16)
+_sb(BF, T0=512, T1=512, T2=4 * NP, TW=512, TE=2048, JB=128, X1=4 * NA, X2=4 * NP, RR=290, R16=TW_, DM=TW_,
+    JM=TW_, RW=TW_, RM=TW_, RS=TW_, TH0=48, DN=48, TB1=144, TH1=144, D0=48, CM0=50, SN0=50, D1=144, CM1=144, SN1=144,
+    CG=NO, JK=296, CA=NP + 8, NT=NA + 16)
 for _n, _w in dict(Q0=144, Q1=128, Q2=NP, QW=128, QE=512, LC=NO, WQ=128, WM=128, V0=128, C1=NA, PV=NP, PE=NP,
-                   C2=NP, L1=NA + 16, P1=NP, L2=2 * HW, OC=NP, R1=2 * K1, R2=S).items():
+                   C2=NP, L1=NA + 16, P1=NP, L2=2 * HW, OC=NP, R1=K1).items():
     _sb(C, **{_n + "c": _w})
     _sb(SC, **{_n + "s": _w})
-_sb(F, CP=1, CF=8, A0=NP, DH=32, AF=192, MS=104, MG=64, ML=64, RL=16, YS=2 * NP, NR=NP, SR0=200, SS0=200)
-_sb(I32, PI=4, CI=6)
+_sb(F, CP=1, CF=8, A0=NP, DH=32, AF=192, MS=96, ML=48, YS=2 * NP, NR=NP, NQ=NP, SR0=200, SS0=200)
+_sb(I32, PI=2, CI=6)
 _sb(U16, OU=60, OT=20, OW=8, OL0=2, OL1=4, OA=4, LV=24, LE=24, ON=2, LP=32, LQ=24)
 for _k in range(8):
     SCRATCH["P%d" % _k] = ("psum", [128, 512], F)
@@ -40,15 +40,15 @@ for _b, _d in (("K", dict(CD=16, OF=64, PY0=32, JX=8, XG=16, J4=16, MK=16, ILB=4
                           TA=8, TB=8, TH8=8)),
                ("WA", dict(M0=32, BS0=32, AS=32, MS0=16, NS=8, SE=16, SF=16, CN0=8, FL0=32, FT0=32, PEN=48, NI=8, SV=16,
                            G0=128, GT0=128, PB=48, A1=48, M1=48, BS1=48, SR1=48, SS1=48, MS1=16, MS2=16, G1=96, GT1=96)),
-               ("WB", dict(SA=16, ZF=8, CN1=8, FL1=32, FT1=32, FS1=32, C8=16, TK=32, LZ=24, NB=32, NM=32, NN=32, NU=32))):
+               ("WB", dict(SA=16, ZF=8, CN1=8, FL1=32, FT1=32, FS1=32, C8=16, TK=32, LZ=24, NM=8, NN=128, NU=128))):
     _at = 0
     for _n, _w in _d.items():
         PIECE[_n] = (_b, _at, _w)
         _at += _w
     _sb(F, **{_b: _at})
 
-POOL = {"v": 46, "a": 42, "p": 16, "g": 14, "d": 20}
-SEMAPHORES = (["e1", "e2", "p1", "pa", "pb", "ms", "sent", "h1c", "h1s", "h2c", "h2s", "hL"]
+POOL = {"v": 46, "a": 44, "p": 16, "g": 12, "d": 22}
+SEMAPHORES = (["e1", "e2", "p1", "pa", "pbc", "pbs", "ms", "sent", "h1c", "h1s"]
               + ["x%s%d" % (q, i) for q, n in POOL.items() for i in range(n)])
 
 
@@ -87,55 +87,35 @@ def _share(topo, cores, r, ks):
     return out
 
 
-def _relay(topo, cores, r, most):
+def _relay(topo, cores, r):
     src = cores[r]
     free = [h for h in topo.cores_of(src) if topo.die(h) == topo.die(src) and h not in cores]
-    ks = range(*PARTS[0])
-    can = {k: [h for h in free if topo.may_write(h, cores[r ^ k])] for k in ks}
-    load = {h: [] for h in free}
-    for k in sorted(ks, key=lambda k: len(can[k])):
-        h = min(can[k], key=lambda h: len(load[h]))
-        if len(load[h]) < most:
-            load[h].append(k)
     out = {}
-    via = [(k, h) for h in free for k in load[h]]
-    for i, (k, h) in enumerate(via):
+    for i, k in enumerate(range(PARTS[0][0], PARTS[0][0] + VIA)):
+        h = [h for h in free if topo.may_write(h, cores[r ^ k])][0]
+        free.remove(h)
         off = topo.engines(h, cores[r ^ k])
-        to = topo.engines(src, h)
-        if len(via) < len(ks):
-            to = [e for e in to if e not in off]
-        n, m, j = 1 << (len(to) // len(via)).bit_length() - 1, len(off) // len(load[h]), load[h].index(k)
-        out[k] = (h, j, to[n * i:n * (i + 1)], off[m * j:m * (j + 1)])
+        to = [e for e in topo.engines(src, h) if e not in off]
+        n = len(to) // VIA
+        out[k] = (h, to[n * i:n * (i + 1)], off)
     return out
 
 
-def _at2(r):
-    return HW * (r // 4) + 16 + S * (r % 4)
-
-
-def _bytes(v, x):
-    return v.bitcast(dt.uint8) if x == "c" else v
-
-
 def _helper(g, core, T, topo):
-    cores, total = list(T.cores), 0
+    cores = list(T.cores)
     for r in range(N):
-        for stage, w, at, sem, names in (("1", K1, K1 * r, "p1", ("L1c", "L1s")), ("m", 8, 8 * r, "ms", ("ML",)),
-                                         ("2", S, _at2(r), "pa", ("L2c", "L2s"))):
-            mine = {k: v for k, v in _relay(topo, cores, r, RELAY[stage]).items() if v[0] == core}
-            if not mine:
+        for k, (h, to, off) in _relay(topo, cores, r).items():
+            if h != core:
                 continue
-            for name in names:
-                x = name[-1]
-                g.wait_ge(T.sem["h" + name[1:]], sum(len(v[2]) for v in mine.values()))
-                src, dst = T["R" + name[1:]], T[name][:, at:at + w]
+            for x in "cs":
+                src, dst = T["R1" + x][:], T["L1" + x][:, K1 * r:K1 * (r + 1)]
+                if x == "c":
+                    src, dst = src.bitcast(dt.uint8), dst.bitcast(dt.uint8)
+                g.wait_ge(T.sem["h1" + x], len(to))
                 g.remote_dma_fused([RemoteDMATransfer(
-                    dst_ids=[_dst(topo, cores[r ^ k])], dma_engine_mask=_mask(v[3]), remote_sem=T.sem[sem],
-                    srcs=[_bytes(src[:, w * v[1]:w * (v[1] + 1)], x)], dsts=[_bytes(dst, x)])
-                    for k, v in mine.items()], local_sem=T.sem.sent)
-                total += sum(len(v[3]) for v in mine.values())
-    if total:
-        g.wait_ge(T.sem.sent, total)
+                    dst_ids=[_dst(topo, cores[r ^ k])], dma_engine_mask=_mask(off), remote_sem=T.sem.p1,
+                    srcs=[src], dsts=[dst])], local_sem=T.sem.sent)
+            g.wait_ge(T.sem.sent, 2 * len(off))
 
 
 def rank_program(g, core, T, topo):
@@ -215,8 +195,8 @@ def rank_program(g, core, T, topo):
     def scan(out, reset, data):
         op("v", lambda: V.tensor_tensor_scan(out[0], reset[0], data[0], 0.0, Op.mult, Op.add), (reset, data), (out,))
 
-    def red(out, in_, negate=False):
-        op("v", lambda: V.tensor_reduce(out[0], in_[0], AxisListType.X, Op.add, negate=negate), (in_,), (out,))
+    def red(out, in_):
+        op("v", lambda: V.tensor_reduce(out[0], in_[0], AxisListType.X, Op.add), (in_,), (out,))
 
     def tr(out, in_):
         op("v", lambda: V.transpose(out[0], in_[0]), (in_,), (out,))
@@ -268,30 +248,17 @@ def rank_program(g, core, T, topo):
             srcs=[s[0]], dsts=[x[0] for _, x in d]) for s, d, e, sem in transfers], local_sem=T.sem.sent),
            [t[0] for t in transfers])
 
-    def ways(r, ks, stage):
-        via = {k: v for k, v in _relay(topo, cores, r, RELAY[stage]).items() if k in ks}
-        rest = [k for k in ks if k not in via]
-        eng = _share(topo, cores, r, rest) if rest else {}
-        used = [e for v in via.values() for e in v[2]]
-        return via, {k: [e for e in es if e not in used] for k, es in eng.items()}
+    def direct(src, dst, cast, w, at, ks, sem, base=0):
+        remote([(cast(R(src, base + w * k, base + w * (k + 1))), [(cores[me ^ k], cast(R(dst, at, at + w)))], e, sem)
+                for k, e in _share(topo, cores, me, ks).items()])
 
-    def direct(src, dst, cast, w, at, ks, sem, stage):
-        via, eng = ways(me, ks, stage)
-        remote([(cast(R(src, w * k, w * (k + 1))), [(cores[me ^ k], cast(R(dst, at, at + w)))], eng[k], sem)
-                for k in eng]
-               + [(cast(R(src, w * k, w * (k + 1))), [(h, cast(R("R" + dst[1:], w * j, w * (j + 1))))], to, "h" + dst[1:])
-                  for k, (h, j, to, _) in via.items()])
-
-    def arrivals(sem, calls, stage, *parts):
-        n = 0
-        for ks in parts:
-            for k in ks:
-                via, eng = ways(me ^ k, ks, stage)
-                n += len(via[k][3]) if k in via else len(eng.get(k, ()))
-        return ((sem, calls * n),)
+    def landed(*parts):
+        return sum(len(_share(topo, cores, me ^ k, ks)[k]) for ks in parts for k in ks if k)
 
     def same(v):
         return v
+
+    both = (("c", u8), ("s", same))
 
     def spread(name, base, w, on="va"):
         def mv(q, po, pi, n, a, b):
@@ -308,11 +275,10 @@ def rank_program(g, core, T, topo):
         mv(on[1], 0, 64, 64, 2 * w, 4 * w)
 
     cg, ca, cs, ck, ch = (c1("CF", j) for j in range(5))
-    cPN, cSV, cOA, cBG, c64, cLM, cK1, cPZ = (c1("CD", j) for j in range(8))
-    oWQ, oV0, oG, oPN, oSV, oGR, oH, oI = (R("OU", a, b) for a, b in ((0, 8), (8, 16), (16, 22), (22, 25), (26, 27),
-                                                                       (28, 29), (32, 56), (56, 59)))
-    oF, oF0, oMG, oN1, oW0, oTK, oC1 = (R("OT", a, b) for a, b in ((0, 3), (4, 7), (8, 12), (12, 14), (14, 16),
-                                                                   (16, 18), (18, 19)))
+    cPN, cOA, cBG, c64, cLM, cK1, cPZ = (c1("CD", j) for j in range(7))
+    oWQ, oV0, oG, oPN, oSV, oGR, oI = (R("OU", a, b) for a, b in ((0, 8), (8, 16), (16, 22), (22, 25), (26, 27),
+                                                                   (28, 29), (56, 59)))
+    oF, oF0, oW0, oTK, oC1, oNM = (R("OT", a, b) for a, b in ((0, 3), (4, 7), (8, 10), (10, 12), (12, 13), (14, 20)))
 
     def JB(n):
         return R("JB", 0, n)
@@ -320,66 +286,82 @@ def rank_program(g, core, T, topo):
     def quad(name, q, a, b):
         return R(name, a, b, 1, (32 * q, 32 * q + 32))
 
+    def shifted(q, out, in_, k, b):
+        if q == "v":
+            ts(out, in_, c1("DH", 8 * b + k), None, Op.add)
+        else:
+            act(out, in_, bias=c1("DH", 8 * b + k))
+
+    def child(q, k, b):
+        shifted(q, R("X1", 4 * K1 * k + b, 4 * K1 * (k + 1), 4), R("A0", K1 * b, K1 * (b + 1)), k, b)
+
+    def twice(a):
+        act(R("JM", a, min(2 * a, TW_)), R("JM", 0, min(a, TW_ - a)), Act.Copy)
+
     dma("s", R("T0", 0, 4 * P), T.r0[:])
     dma("a", R("T0", 4 * UQ), T.u[:, 0:8])
     dma("s", R("T1", 0, 4 * K1), T.r1[:])
     dma("s", R("T2"), T.r2[:])
-    iota(R("PI", 0, 3, 2), [[0, 2]], 0, 1, True)
-    iota(c1("PI", 1), [[0, 1]], 0, 16, True)
-    iota(c1("PI", 3), [[0, 1]], 0, 4, True)
+    dma("s", R("TW"), T.w[:])
+    iota(c1("PI"), [[0, 1]], 0, 1, True)
     iota(R("JB"), [[1, 128]])
-    iota(R("CP"), [[0, 1]], 0, 1)
     ms(R("RW"), 0.0)
     iota(R("RW", 0, 48, 2), [[0, 4], [16, 2], [32, 3]])
     iota(R("RW", 65, 112, 2), [[0, 4], [16, 2], [0, 3]], 96)
-    iota(R("RW", 128, 192), [[6, 8], [48, 2], [2, 4]])
+    iota(R("RW", 128, 152), [[6, 8], [2, 3]])
+    iota(R("RW", 224, 320), [[16 - 32 * (me % 2), 2], [1, CAP], [32, 4]], 16 * (me % 2))
     iota(R("JX"), [[(1 - 2 * (me >> i & 1)) << i, 2] for i in (2, 1, 0)], me)
     ms(R("T0", 4 * P, 4 * UQ), 0.0)
-    ts(R("CI", 0, 2), R("PI", 0, 2), 4, 15, Op.logical_shift_right, Op.bitwise_and)
-    ts(R("CI", 2, 4), R("PI", 2, 4), 2, 3, Op.logical_shift_right, Op.bitwise_and)
-    ts(c1("CI", 4), c1("PI"), 4, 1, Op.logical_shift_right, Op.bitwise_and)
+    for j, (s1, s2) in enumerate(((4, 15), (0, 15), (2, 3), (0, 3), (4, 1))):
+        ts(c1("CI", j), c1("PI"), s1, s2, Op.logical_shift_right, Op.bitwise_and)
     ms(R("OF"), 0.0)
     cp(R("CF", 0, 5), R("CI", 0, 5))
-    ms(R("TE"), 0.0)
+    cp(R("CP"), c1("PI"))
+    ms(R("TE", 0, 1024), 0.0)
     quant("Q0", 0, 128, "T0")
+    ms(R("TE", 1024), 0.0)
 
     eng = _share(topo, cores, me, range(N))
     far = [k for k in eng if topo.chip(cores[me ^ k]) != topo.chip(core)]
     near = [k for k in eng if k not in far]
     off = sorted(e for k in far for e in eng[k])
     on = eng[near[0]]
-    for j, (x, cast) in enumerate((("c", u8), ("s", same))):
+    for j, (x, cast) in enumerate(both):
         land = {k: (cores[me ^ k], cast(R("Q0" + x, UQ + 2 * k, UQ + 2 * k + 2))) for k in eng}
         remote([(cast(R("Q0" + x, UQ, UQ + 2)), [land[k] for k in far], off, "e1")]
                + [(cast(R("Q0" + x, UQ, UQ + 2)), [land[k]], on[2 * j:2 * j + 1], "e1") for k in near])
     E1 = (("e1", 2 * (len(far) * len(off) + len(near))),)
-    for x, cast in (("c", u8), ("s", same)):
+    for x, cast in both:
         src = cast(R("Q0" + x, 0, P))
-        land = {k: (cores[me ^ k], cast(R("LC" + x, P * (k - 1), P * k))) for k in eng}
+        at = {k: P * (me - (me > me ^ k)) for k in eng}
+        land = {k: (cores[me ^ k], cast(R("LC" + x, at[k], at[k] + P))) for k in eng}
         remote([(src, [land[k] for k in far], off, "e2")] + [(src, [land[k]], on[0:3:2], "e2") for k in near])
     E2 = (("e2", 2 * (len(far) * len(off) + 2 * len(near))),)
-    dma("s", R("TW"), T.w[:], E2)
+    op("s", None, arrive=E2)
     move("s", "L1", NA, "Q0", 32, 16)
     move("s", "L2", 0, "Q0", 32, 16)
     move("s", "L2", HW, "Q0", 32, 16)
 
+    iota(R("KF", 0, 48, 2), [[0, 24]])
     iota(R("NT", 0, NA), [[0, N], [1, K1]])
+    iota(R("NT", NA), [[0, 16]], -1)
     iota(R("ILB", 0, 33), [[0, 11], [4, 3]])
     act(R("JM", 0, 16), JB(16), Act.Copy)
-    for a in (16, 32, 64, 128, 256):
-        act(R("JM", a, min(2 * a, TW_)), R("JM", 0, min(a, TW_ - a)), Act.Copy)
     act(R("OF", 0, 8), JB(8), scale=2.0, bias=float(UQ))
     act(R("OF", 8, 16), JB(8), scale=4.0, bias=cs)
+    twice(16)
     act(cPN, ch, scale=16.0, bias=cs)
-    act(cSV, ch, scale=16.0, bias=ca)
+    act(c1("OF", 26), ch, scale=16.0, bias=ca)
+    twice(32)
     act(R("OF", 16, 22, 2), JB(3), scale=4.0, bias=cs)
     act(R("OF", 17, 22, 2), JB(3), scale=4.0, bias=cs)
+    twice(64)
     act(R("OF", 22, 25), JB(3), scale=4.0, bias=cPN)
-    act(c1("OF", 26), cSV, Act.Copy)
     act(c1("OF", 28), cg, Act.Copy)
+    twice(128)
     act(R("OF", 56, 60), JB(4), scale=16.0, bias=ca)
-    for j in range(3):
-        act(R("OF", 32 + j, 56, 3), JB(8), Act.Copy)
+    act(c64, ca, scale=-1.0, bias=float(M))
+    twice(256)
     for b in range(4):
         ts(R("TE", 512 * b + b, 512 * (b + 1), 4), R("JB"), R("CP"), None, Op.is_equal)
     ms(R("T1", 4 * K1), 0.0)
@@ -387,24 +369,22 @@ def rank_program(g, core, T, topo):
     cp(R("OU"), R("OF", 0, 60))
     for s in range(3):
         act(R("TB1", 48 * s, 48 * s + 48), JB(48), bias=-16.0 * s)
-    act(c64, ca, scale=-1.0, bias=float(M))
     quant("QE", 0, 512, "TE")
     pick("V0", 0, 128, "Q0", oV0, (0, 128))
     quant("Q1", 0, 128, "T1")
     for b in range(4):
         mm("P%d" % b, "QE", 128 * b, "V0", 0, 128, True, False)
         mm("P%d" % b, "QE", 128 * b, "Q1", 0, 128, False, True)
+    for b in range(4):
+        mm("P%d" % (4 + b), "QE", 128 * b, "Q0", 0, 128)
     for j in range(3):
         act(R("J4", 4 * j, 4 * j + 4), JB(4), Act.Copy)
-        act(R("RW", 192 + j, 216, 3), JB(8), scale=8.0, bias=float(j))
-        act(R("RW", 256 + j, 280, 3), R("JX"), Act.Copy)
+        act(R("RW", 160 + j, 184, 3), R("JX"), Act.Copy)
+        act(R("KF", 1 + 2 * j, 48, 6), JB(8), Act.Copy, scale=float(K1))
     for j in range(2):
-        fill(R("RW", 288 + j, 304, 2), 8, 15.0 + 16 * j)
+        fill(R("RW", 192 + j, 208, 2), 8, 15.0 + 16 * j)
     act(R("RW", 1, 48, 2), R("RW", 0, 48, 2), Act.Copy)
     act(R("RW", 64, 112, 2), R("RW", 0, 48, 2), Act.Copy)
-    fill(R("RW", 131, 192, 8), 8, 96.0)
-    act(R("RW", 135, 192, 8), JB(8), scale=6.0, bias=49.0)
-    act(R("RW", 224, 248), R("RW", 192, 216), bias=4.0)
     act(R("XG"), by(R("JX"), oGR), Act.Copy)
     ts(R("TH1"), R("TB1"), ca, -EPS, Op.is_lt, Op.mult)
     ts(R("DM"), R("JM"), ca, None, Op.is_equal)
@@ -414,9 +394,6 @@ def rank_program(g, core, T, topo):
     ms(R("RR", 0, 290, 96), 0.0)
     ms(R("R16", 0, TW_, 16), 0.0)
     ts(R("MK", 0, 12), R("J4", 0, 12), cs, None, Op.is_equal)
-    pick("WM", 0, 128, "Q0", R("OW"), (0, 128))
-    for b in range(4):
-        act(R("A0", K1 * b, K1 * (b + 1)), R("P%d" % b, 0, K1), Act.Copy)
     act(cBG, ca, Act.Relu, scale=BIG, bias=-7 * BIG)
     act(c1("CM0", 48), ca, Act.Relu, scale=24.0, bias=-168.0)
     act(cOA, ch, scale=float(K1), bias=ck)
@@ -424,25 +401,26 @@ def rank_program(g, core, T, topo):
     act(R("TH0", 0, P), R("TH1", 0, P), Act.Copy)
     act(R("TH0", P, 2 * P), R("TH1", 48, 48 + P), bias=cBG)
     act(cOA, cOA, bias=float(NA - K1 * me))
-    for a, b in ((1, 2), (2, 4), (4, 8)):
-        fill(R("THG", P * (a - 1), P * (b - 1)), P * (b - a), -0.5 if (me ^ a) < me else 0.0)
     fill(R("LM"), 32, cLM)
-    act(R("KF", 1, 48, 2), R("OF", 32, 56), scale=float(K1))
+    act(cK1, cBG, Act.Sign)
     act(cPZ, ca, bias=16.0)
-    act(cK1, ck, bias=1.0)
-    for h in range(2):
-        act(R("PLZ", 12 * h, 12 * h + 12), JB(12), scale=16.0, bias=cPZ)
+    act(R("DN"), R("DM", 0, 48), Act.Copy, scale=-1.0)
+    act(cK1, cK1, bias=3.0, scale=2.0)
+    for b in range(4):
+        act(R("A0", K1 * b, K1 * (b + 1)), R("P%d" % b, 0, K1), Act.Copy)
+    for b in range(4):
+        act(c1("DH", 8 * b), R("P%d" % (4 + b), UQ + 1, UQ + 2), Act.Copy)
+    for b in range(4):
+        child("a", 0, b)
     quant("Q2", 0, NP, "T2")
     tt(R("RM"), R("RW"), R("DM"), Op.mult)
-    ts(c1("ON"), c1("XG"), 8.0, 3.0, Op.mult, Op.add)
-    scan(R("RS"), R("R16"), R("RM"))
     ts(R("TA"), JB(8), c1("XG"), -EPS, Op.is_lt, Op.mult)
+    scan(R("RS"), R("R16"), R("RM"))
     ts(R("TB"), JB(8), c1("XG"), 4 * BIG, Op.is_equal, Op.mult)
     cp(R("OT"), R("RS", 15, TW_, 16))
     tt(R("TH8"), R("TA"), R("TB"), Op.add)
-    ms(R("KF", 0, 48, 2), 0.0)
-    ms(R("MS", 97, 104), 0.0)
-    ms(R("NT", NA), -1.0)
+    ts(c1("ON"), c1("XG"), 6.0, cK1, Op.mult, Op.add)
+    quant("QW", 0, 128, "TW")
 
     pick("WQ", 0, 128, "Q0", oWQ, (0, NL), E1)
     for b in range(3):
@@ -450,17 +428,10 @@ def rank_program(g, core, T, topo):
     mm("P4", "WQ", 0, "Q0", 0, 128)
     mm("P3", "QE", 128 * 3, "Q0", NL - 128, NL)
     for b in range(4):
-        act(R("DH", 8 * b, 8 * b + 8), R("P%d" % b, 128 - 2 * N + 1, 128, 2), Act.Copy)
-
-    def child(q, k, b):
-        o, i, h = R("X1", 4 * K1 * k + b, 4 * K1 * (k + 1), 4), R("A0", K1 * b, K1 * (b + 1)), c1("DH", 8 * b + k)
-        if q == "v":
-            ts(o, i, h, None, Op.add)
-        else:
-            act(o, i, bias=h)
-
-    xa = [(k, b) for k in XA for b in range(4)][:XN]
-    xv = [(k, b) for k in XV for b in range(4) if (k, b) not in xa]
+        act(R("DH", 8 * b + 1, 8 * b + 8), R("P%d" % b, 128 - 2 * N + 3, 128, 2), Act.Copy)
+    xs = [(k, b) for k in XA for b in range(4)]
+    for k, b in xs[:XN]:
+        child("a", k, b)
     tt(R("M0"), R("P4", 0, 32), R("DM", 0, 32), Op.mult)
     cp(R("AS"), R("P4", 0, 32))
     scan(R("BS0"), R("R16", 0, 32), R("M0"))
@@ -469,144 +440,155 @@ def rank_program(g, core, T, topo):
     tt(R("CM0", 0, 48), R("D0"), R("TH0"), Op.is_gt)
     scan(R("SN0", 0, 49), R("RR", 48, 146, 2), R("CM0", 0, 49))
     cp(R("OL0"), R("SN0", 23, 49, 25))
+    quant("C1", K1 * 4, K1 * 6, "X1")
+    for x, cast in both:
+        remote([(cast(R("C1" + x, K1 * k, K1 * (k + 1))), [(h, cast(R("R1" + x)))], to, "h1" + x)
+                for k, (h, to, _) in _relay(topo, cores, me).items()])
     cp(by(R("SS0"), R("OL0")), R("AS"))
     cp(by(R("SR0"), R("OL0")), R("PY0"))
     tt(R("MS0"), R("SS0", 0, 16), R("DM", 0, 16), Op.mult)
     tt(R("SE", 0, 12), R("SR0", 0, 12), R("MK", 0, 12), Op.mult)
-    red(c1("NS"), R("MS0"), True)
+    red(c1("NS"), R("MS0"))
     scan(R("SF", 0, 12), R("RR", 0, 288, 24), R("SE", 0, 12))
-    for kb in xa[:22]:
-        child("a", *kb)
-    for kb in xv[:2]:
-        child("v", *kb)
+    quant("C1", K1 * 6, K1 * 8, "X1")
+    for x, cast in both:
+        direct("C1" + x, "L1" + x, cast, K1, K1 * me, range(6, 8), "p1")
     ts(R("OA", 0, 3), R("SF", 3, 12, 4), cOA, None, Op.add)
-    for kb in xv[2:8]:
-        child("v", *kb)
-    mm("P3", "WQ", 0, "LC", 0, NO, arrive=E2)
-    act(R("SG"), R("P3", 0, NO), Act.Sign, bias=c1("NS"))
-    quant("C1", NA // 2, NA, "X1")
+    for k, b in xs[XN:]:
+        child("v", k, b)
     mm("P6", "WQ", 0, "C1", NA // 2, NA)
-    for kb in xa[22:]:
-        child("a", *kb)
+    quant("C1", 0, 192, "X1")
+    mm("P3", "WQ", 0, "LC", 0, NO, arrive=E2)
+    mm("P5", "WQ", 0, "C1", 0, 192)
+    for a, b, o in ((0, P * me, Op.is_ge), (P * me, NO, Op.is_gt)):
+        if a < b:
+            ts(R("CG", a, b), R("P3", a, b), c1("NS"), None, o)
     quant("C1", 192, NA // 2, "X1")
     mm("P7", "WQ", 0, "C1", 192, NA // 2)
-    tt(R("CG"), R("SG"), R("THG"), Op.is_gt)
-    act(R("JK", 0, NO), R("CG"), Act.Copy, acc=c1("CN0"))
-    for kb in xv[8:]:
-        child("v", *kb)
-    quant("C1", 0, 192, "X1")
-    mm("P5", "WQ", 0, "C1", 0, 192)
+    red(c1("CN0"), R("CG"))
     ts(R("FL0"), R("LM"), c1("CN0"), None, Op.is_gt)
     tr(R("FT0"), R("FL0"))
     ts(R("PEN"), by(R("FT0"), oPN), -1.0, BIG, Op.add, Op.mult)
-    for k0, k1 in PARTS:
-        for x, cast in (("c", u8), ("s", same)):
-            direct("C1" + x, "L1" + x, cast, K1, K1 * me, range(k0, k1), "p1", "1")
-    P1 = arrivals("p1", 2, "1", *[range(*p) for p in PARTS])
+    for x, cast in both:
+        direct("C1" + x, "L1" + x, cast, K1, K1 * me, range(4), "p1")
+    P1 = (("p1", 2 * (landed(range(6, 8), range(4))
+                      + sum(len(_relay(topo, cores, me ^ k)[k][2]) for k in _relay(topo, cores, me)))),)
     move("s", "L1", K1 * me, "C1", 0, K1)
 
     for q in (2, 3):
         act(quad("AF", q, 0, 192), quad("P6", q, 192 * (q % 2), 192 * (q % 2 + 1)), Act.Copy)
+    act(quad("AF", 0, 0, 192), quad("P5", 0, 0, 192), Act.Copy)
     act(quad("AF", 1, 0, 192), quad("P7", 1, 0, 192), Act.Copy)
-    cp(quad("AF", 0, 0, 192), quad("P5", 0, 0, 192))
-    tt(R("SV"), by(R("FT0"), oSV), R("SR0", 0, 16), Op.mult)
     act(R("PB"), by(R("NT", 0, 192), R("OA", 0, 3)), Act.Copy)
     act(R("JK", 0, 48), R("PEN"), Act.Copy, scale=1.0 / BIG, acc=c1("NI"))
-    act(R("G0", 0, 96), by(R("SV"), oG), bias=float(NA))
     fill(R("G0", 96, 128), 32, c1("NI"))
-    act(R("H", 0, NP), by(R("DH", 0, 8), oH), Act.Copy)
     tt(R("A1"), by(R("AF"), R("OA", 0, 3)), R("PEN"), Op.add)
-    tt(R("M1"), R("A1"), R("DM", 0, 48), Op.mult)
+    tt(R("M1"), R("A1"), R("DN"), Op.mult)
     scan(R("BS1"), R("R16", 0, 48), R("M1"))
-    tr(R("GT0"), R("G0"))
-    for s in range(3):
-        ts(R("D1", 48 * s, 48 * s + 48), R("A1"), c1("BS1", 16 * s + 15), None, Op.subtract)
+    tt(R("SV"), by(R("FT0"), oSV), R("SR0", 0, 16), Op.mult)
+    for s in range(2):
+        act(R("D1", 48 * s, 48 * s + 48), R("A1"), bias=c1("BS1", 16 * s + 15))
+    ts(R("D1", 96, 144), R("A1"), c1("BS1", 47), None, Op.add)
     tt(R("CM1"), R("D1"), R("TH1"), Op.is_gt)
+    act(R("G0", 0, 96), by(R("SV"), oG), bias=float(NA))
     scan(R("SN1"), R("RR", 0, 288, 2), R("CM1"))
+    tr(R("GT0"), R("G0"))
     cp(R("OL1", 0, 3), R("SN1", 47, 144, 48))
     act(R("MS", 48, 96), by(R("GT0"), oF0), Act.Copy)
     spread("MS", 48, 12, "aa")
-    act(R("H", NP, 2 * NP), by(R("DH", 8, 16), oH), Act.Copy)
     cp(by(R("SR1"), R("OL1", 0, 3)), R("PB"))
-    cp(R("G1"), by(R("SR1"), oG))
     cp(by(R("SS1"), R("OL1", 0, 3)), R("A1"))
-    tr(R("GT1"), R("G1"))
+    cp(R("G1"), by(R("SR1"), oG))
     tt(R("MS1"), R("SS1", 0, 16), R("DM", 0, 16), Op.mult)
+    tr(R("GT1"), R("G1"))
+    tt(R("MS0"), R("SR1", 0, 16), R("DM", 0, 16), Op.mult)
+    act(R("MS2"), R("MS1"), Act.Copy, acc=c1("NI", 1))
+    act(R("SE"), R("MS0"), scale=4.0, bias=1.0 / 16, acc=c1("NI", 2))
+    fill(R("MS", 51, 96, 6), 8, c1("NI", 1))
+    fill(R("MS", 53, 96, 6), 8, c1("NI", 2))
+    for p in PARTS:
+        direct("MS", "ML", same, 6, 6 * me, range(*p), "ms", 48)
+    MS = (("ms", landed(*[range(*p) for p in PARTS])),)
+    dma("s", R("ML", 6 * me, 6 * me + 6), R("MS", 48, 54))
     tt(R("MS", 0, 48), by(R("GT1"), oF), R("KF"), Op.add)
-    act(R("MS2"), R("MS1"), Act.Copy, acc=c1("MS", 96))
     spread("MS", 0, 12)
     cp(R("LV"), R("MS", 1, 48, 2))
     ts(R("LE"), R("MS", 0, 48, 2), 4.0, ck, Op.mult, Op.add)
-    act(R("MG"), by(R("MS"), oMG), Act.Copy)
-    direct("MG", "ML", same, 8, 8 * me, range(N), "ms", "m")
-    MS = arrivals("ms", 1, "m", range(N))
-    for k0, k1 in PARTS:
-        pick("PV", S * k0, S * k1, "C1", R("LV", 3 * k0, 3 * k1))
-        pick("PE", S * k0, S * k1, "Q2", R("LE", 3 * k0, 3 * k1))
-    order = (0, 2, 1, 3)
+    at2 = HW * (me // 4) + 16 + S * (me % 4)
     for i, (k0, k1) in enumerate(PARTS):
-        for src, first in (("PV", True), ("PE", False)):
-            for j in order:
-                mm("P%d" % (4 * i + j), "QE", 128 * j, src, S * k0, S * k1, first, not first)
-    at2 = _at2(me)
+        for src, pool, offs in (("PV", "C1", "LV"), ("PE", "Q2", "LE")):
+            pick(src, S * k0, S * k1, pool, R(offs, 3 * k0, 3 * k1))
+            for j in (0, 2, 1, 3):
+                mm("P%d" % (4 * i + j), "QE", 128 * j, src, S * k0, S * k1, src == "PV", src == "PE")
     for i, (k0, k1) in enumerate(PARTS):
-        a, b = S * k0, S * k1
-        for j in (2, 3):
+        for j in (2, 3, 0, 1):
             for k in range(k0, k1):
-                act(R("X2", 4 * S * k + j, 4 * S * (k + 1), 4), R("P%d" % (4 * i + j), S * (k - k0), S * (k - k0 + 1)),
-                    bias=c1("DH", 8 * j + k))
-        for j in range(2):
-            tt(R("X2", 4 * a + j, 4 * b, 4), R("P%d" % (4 * i + j), 0, b - a), R("H", NP * j + a, NP * j + b), Op.add)
+                shifted("a" if j > 1 else "v", R("X2", 4 * S * k + j, 4 * S * (k + 1), 4),
+                        R("P%d" % (4 * i + j), S * (k - k0), S * (k - k0 + 1)), k, j)
+        quant("C2", S * k0, S * k1, "X2")
+        for x, cast in both[::1 - 2 * i]:
+            direct("C2" + x, "L2" + x, cast, S, at2, range(k0, k1), ("pa", "pb" + x)[i])
         if i == 0:
-            quant("QW", 0, 128, "TW")
-        quant("C2", a, b, "X2")
-        for x, cast in (("c", u8), ("s", same)):
-            direct("C2" + x, "L2" + x, cast, S, at2, range(k0, k1), ("pa", "pb")[i], "2")
-    P2 = [arrivals(("pa", "pb")[i], 2, "2", range(*p)) for i, p in enumerate(PARTS)]
+            pick("WM", 0, 128, "Q0", R("OW"), (0, 128))
+    PA = (("pa", 2 * landed(range(*PARTS[0]))),)
+    PB = {x: (("pb" + x, landed(range(*PARTS[1]))),) for x in "cs"}
 
-    act(R("ML", 8 * me, 8 * me + 8), R("MG", 0, 8), Act.Copy)
     act(R("IL"), R("ILB", 0, 32), bias=cs)
-    pick("L2", at2, at2 + S, "C2", oI)
+    for h in range(2):
+        act(R("PLZ", 12 * h, 12 * h + 12), JB(12), scale=16.0, bias=cPZ)
     ts(R("LP"), by(R("ML"), oW0), ck, None, Op.add, arrive=MS)
     pick("P1", 0, NP, "L1", R("LP", 0, 24), arrive=P1)
     mm("P0", "WM", 0, "P1", 0, NP)
     mm("P1", "QW", 0, "P1", 0, NP)
     cp(R("SA"), by(R("ML"), c1("ON")))
     ts(R("ZF"), R("TH8"), c1("SA"), 0.0, Op.add, Op.is_lt)
-    ts(R("NB"), by(R("ML"), oN1), 4.0, cK1, Op.mult, Op.add)
-    tt(R("CA", NP), R("ZF"), R("ML", 7, 64, 8), Op.mult)
-    for q in (4, 5, 6, 7, 0, 1, 2, 3):
+    tt(R("CA", NP), R("ZF"), R("ML", 1, 48, 6), Op.mult)
+    for q in (2, 3, 4, 5, 6, 7, 0, 1):
         ts(R("CA", S * q, S * (q + 1)), R("P0", S * q, S * (q + 1)), c1("SA"), c1("TH8", q), Op.subtract, Op.is_gt)
     act(R("NR"), by(R("NT"), R("LP", 0, 24)), Act.Copy)
-    act(R("JK", 0, 200), R("CA", 192), Act.Copy, acc=c1("CN1", 1))
+    act(R("JK"), R("CA", 2 * S), Act.Copy, acc=c1("CN1", 1))
     act(R("YS", 0, NP), R("P1", 0, NP), Act.Copy)
-    out = [dma("s", T.nm[0:1, 0:NP], R("NR", 0, NP, 1, (0, 1))),
-           dma("s", T.y[:, 0:NP], R("YS", 0, NP), (("sent", sent[0]),))]
-    red(c1("CN1"), R("CA", 0, 192))
+    out = [dma("s", T.nm[0:1, 0:NP], R("NR", 0, NP, 1, (0, 1))), dma("s", T.y[:, 0:NP], R("YS", 0, NP))]
+    red(c1("CN1"), R("CA", 0, 2 * S))
+    pick("L2", at2, at2 + S, "C2", oI)
     ts(R("FL1"), R("LM"), c1("CN1", 1), c1("CN1"), Op.subtract, Op.is_gt)
     tr(R("FT1"), R("FL1"))
+    ts(R("NM", 0, 4), JB(4), c1("SA", 8), c1("FL1"), Op.add, Op.mult)
     scan(R("FS1"), R("R16", 0, 32), R("FT1"))
     cp(R("C8"), by(R("FS1"), oC1))
     spread("C8", 0, 2)
+    for j in range(4):
+        fill(R("NN", 32 * j, 32 * j + 32), 32, c1("NM", j))
     tt(R("TK"), by(R("C8"), oTK), R("IL"), Op.is_gt)
     tt(R("LZ"), R("TK", 0, 24), R("PLZ"), Op.mult)
-    tt(quad("NM", 0, 0, 32), quad("TK", 0, 0, 32), quad("NB", 0, 0, 32), Op.mult)
+    tr(R("NU"), R("NN"))
     cp(R("LQ"), R("LZ"))
-    act(quad("NN", 0, 0, 32), quad("NM", 0, 0, 32), bias=-1.0)
 
-    halves = [(me ^ k0) // 4 for k0, _ in PARTS]
-    for i, h in enumerate(halves):
-        pick("OC", 192 * h, 192 * (h + 1), "L2", R("LQ", 12 * h, 12 * h + 12), (HW * h, HW * h + 208), P2[i])
-        mm("P%d" % (2 + i), "QW", 0, "OC", 192 * h, 192 * (h + 1))
-        out.append(dma("s", T.oc[:, 768 * h:768 * (h + 1)], u8(R("OCc", 192 * h, 192 * (h + 1)))))
-        if i == 0:
-            tr(quad("NU", 0, 0, 32), quad("NN", 0, 0, 32))
-            out.append(dma("s", T.nm[0:1, NP:2 * NP], R("NU", 0, 16, 1, (0, 24))))
-    oa = [dma("a", T.osc[4 * k:4 * k + 4, :], R("OCs", 0, NP, 1, (32 * k, 32 * k + 4))) for k in range(4)]
-    for i, h in enumerate(halves):
-        a = NP + 192 * h
-        cp(R("YS", a, a + 192), R("P%d" % (2 + i), 0, 192))
-        out.append(dma("s", T.y[:, a:a + 192], R("YS", a, a + 192)))
+    ha, hb = ((me ^ k0) // 4 for k0, _ in PARTS)
+
+    def half(name, h, base=0):
+        return R(name, base + 192 * h, base + 192 * (h + 1))
+
+    def window(name, h):
+        return R(name, HW * h, HW * h + 208)
+
+    at = [K1 * (me // 2 ^ q) for q in range(4)]
+    pick("OC", 192 * ha, 192 * (ha + 1), "L2", R("LQ", 12 * ha, 12 * ha + 12), (HW * ha, HW * ha + 208), PA)
+    mm("P2", "QW", 0, "OC", 192 * ha, 192 * (ha + 1))
+    out.append(dma("s", T.oc[:, 768 * ha:768 * (ha + 1)], u8(half("OCc", ha))))
+    act(half("OCs", hb), by(window("L2s", hb), R("LQ", 12 * hb, 12 * hb + 12)), Act.Copy, PB["s"])
+    act(half("YS", ha, NP), R("P2", 0, 192), Act.Copy)
+    oa = [dma("a", T.osc[4 * q:4 * q + 4, :], R("OCs", 0, NP, 1, (32 * q, 32 * q + 4))) for q in range(4)]
+    out.append(dma("s", T.y[:, NP + 192 * ha:NP + 192 * (ha + 1)], half("YS", ha, NP)))
+    cp(u32(half("OCc", hb)), by(u32(window("L2c", hb)), R("LQ", 12 * hb, 12 * hb + 12)), PB["c"])
+    mm("P3", "QW", 0, "OC", 192 * hb, 192 * (hb + 1))
+    out.append(dma("s", T.oc[:, 768 * hb:768 * (hb + 1)], u8(half("OCc", hb))))
+    ts(R("NQ", at[0], at[0] + K1), by(R("NU"), oNM), -1.0, None, Op.add)
+    cp(half("YS", hb, NP), R("P3", 0, 192))
+    out.append(dma("s", T.y[:, NP + 192 * hb:NP + 192 * (hb + 1)], half("YS", hb, NP)))
+    for q in range(1, 4):
+        cp(quad("NQ", 0, at[q], at[q] + K1), quad("NQ", q, at[0], at[0] + K1))
+    out.append(dma("s", T.nm[0:1, NP:2 * NP], R("NQ", 0, NP, 1, (0, 1))))
     op("s", None, after=out)
     op("a", None, after=oa)
     op("g", None, arrive=(("sent", sent[0]),))

@@ -6,13 +6,19 @@ N, P, CAP, M, S = 8, 24, 12, 64, 48
 UQ = 126
 NL, NO = UQ + 2 * N, (N - 1) * P
 K1 = 4 * P
-NA, NP = N * K1, N * S
-HW = 224
-EPS, BIG = 1e-37, 2.0 ** 80
+NP = N * S
+ZC = 32
+LZ = (N - 1) * K1
+OWN = LZ + ZC
+HH, HB, HA = NP // 2, 3 * S, 7 * S + 16
+AW = 100
+EPS, BIG, HUGE = 1e-37, 2.0 ** 80, 2.0 ** 90
 PARTS = ((4, 8), (0, 4))
-XA, XN = (4, 5, 6, 7, 1, 2, 3), 26
-VIA = 2
-TW_ = 320
+XA = (4, 5, 6, 7, 1, 2, 3)
+XV = (4, 5, 6, 7, 18, 19, 26, 27)
+VIA0, VIA1, VIA2 = (4, 5), (4, 5), (4, 5)
+SPQ = "vv"
+OWNQ = "aava"
 
 F, BF, I32, U16, C, SC = "float32", "bfloat16", "int32", "uint16", "float8_e4m3fn_x4", "uint8"
 SCRATCH = {}
@@ -23,32 +29,31 @@ def _sb(dtype, **kw):
         SCRATCH[name] = ("sbuf", [128, n], dtype)
 
 
-_sb(BF, T0=512, T1=512, T2=4 * NP, TW=512, TE=2048, JB=128, X1=4 * NA, X2=4 * NP, RR=290, R16=TW_, DM=TW_,
-    JM=TW_, RW=TW_, RM=TW_, RS=TW_, TH0=48, DN=48, TB1=144, TH1=144, D0=48, CM0=50, SN0=50, D1=144, CM1=144, SN1=144,
-    CG=NO, JK=296, CA=NP + 8, NT=NA + 16)
-for _n, _w in dict(Q0=144, Q1=128, Q2=NP, QW=128, QE=512, LC=NO, WQ=128, WM=128, V0=128, C1=NA, PV=NP, PE=NP,
-                   C2=NP, L1=NA + 16, P1=NP, L2=2 * HW, OC=NP, R1=K1).items():
+_sb(BF, T0=512, T1=512, T2=4 * NP, TW=512, TE=516, JB=128, JM=48, JQ=128, X1=4 * (OWN + K1), X2=4 * (HA + HH + 4),
+    RR=144, R4=128, DM=48, DN=48, TB1=144, TH1=144, TH0=48, D0=48, CM0=50, SN0=50, D1=144, CM1=144, SN1=144,
+    CG=NO, CH=NO, CA=NP + 8, CB=NP + 8, LMM=128, FV=128, FT=128, FS=128, NT=2 * K1, MX=16, JK=48, PS=2)
+for _n, _w in dict(Q0=144, Q1=128, Q2=NP, QW=128, QE=512, LC=NO, WQ=128, WM=128, V0=128, C1=OWN + N * K1, PE=NP,
+                   L2=HH, PV=NP, P1=NP, C2=HA + HH + 4, OC=NP, R0=P, R1=K1, R2=S).items():
     _sb(C, **{_n + "c": _w})
     _sb(SC, **{_n + "s": _w})
-_sb(F, CP=1, CF=8, A0=NP, DH=32, AF=192, MS=96, ML=48, YS=2 * NP, NR=NP, NQ=NP, SR0=200, SS0=200)
-_sb(I32, PI=2, CI=6)
-_sb(U16, OU=60, OT=20, OW=8, OL0=2, OL1=4, OA=4, LV=24, LE=24, ON=2, LP=32, LQ=24)
+_sb(F, CP=1, CF=8, A0=4 * AW, DH=32, AF=2 * K1, MS=64, ML=64, YS=2 * NP, SR0=200, SS0=200)
+_sb(I32, PI=4, CI=8, KI=2)
+_sb(U16, OU=48, OL0=2, OL1=4, OA=4, LO=16, LV=32, LE=32, LP=32, LQ=32)
 for _k in range(8):
     SCRATCH["P%d" % _k] = ("psum", [128, 512], F)
 PIECE = {}
-for _b, _d in (("K", dict(CD=16, OF=64, PY0=32, JX=8, XG=16, J4=16, MK=16, ILB=40, IL=32, PLZ=24, KF=48, LM=32,
-                          TA=8, TB=8, TH8=8)),
-               ("WA", dict(M0=32, BS0=32, AS=32, MS0=16, NS=8, SE=16, SF=16, CN0=8, FL0=32, FT0=32, PEN=48, NI=8, SV=16,
-                           G0=128, GT0=128, PB=48, A1=48, M1=48, BS1=48, SR1=48, SS1=48, MS1=16, MS2=16, G1=96, GT1=96)),
-               ("WB", dict(SA=16, ZF=8, CN1=8, FL1=32, FT1=32, FS1=32, C8=16, TK=32, LZ=24, NM=8, NN=128, NU=128))):
+for _b, _d in (("K", dict(CD=16, OF=48, PY0=32, MK=16, LM=32, TA=8, TB=8, TH8=8, BQ=48, TT=8, KF=16)),
+               ("WA", dict(M0=32, BS0=32, AS=32, NS=16, SE=16, SF=16, FL0=32, FT0=32, PEN=48, NI=8, SV=16,
+                           G0=128, GT0=128, PB=48, A1=48, M1=48, BS1=48, SR1=48, SS1=48, G1=96, GT1=128, LF=16)),
+               ("WB", dict(LX=48, ZF=8, N1=32, N1B=32, N1T=32, T2N=32, N2=32, N2B=32, N2T=32))):
     _at = 0
     for _n, _w in _d.items():
         PIECE[_n] = (_b, _at, _w)
         _at += _w
     _sb(F, **{_b: _at})
 
-POOL = {"v": 46, "a": 44, "p": 16, "g": 12, "d": 22}
-SEMAPHORES = (["e1", "e2", "p1", "pa", "pbc", "pbs", "ms", "sent", "h1c", "h1s"]
+POOL = {"v": 47, "a": 44, "p": 18, "g": 12, "d": 16}
+SEMAPHORES = (["e1", "e2", "p1", "ms", "pa", "pb", "sent", "R0c", "R0s", "R1c", "R1s", "R2c", "R2s"]
               + ["x%s%d" % (q, i) for q, n in POOL.items() for i in range(n)])
 
 
@@ -87,35 +92,53 @@ def _share(topo, cores, r, ks):
     return out
 
 
-def _relay(topo, cores, r):
+def _relay(topo, cores, r, ks):
     src = cores[r]
     free = [h for h in topo.cores_of(src) if topo.die(h) == topo.die(src) and h not in cores]
     out = {}
-    for i, k in enumerate(range(PARTS[0][0], PARTS[0][0] + VIA)):
-        h = [h for h in free if topo.may_write(h, cores[r ^ k])][0]
-        free.remove(h)
-        off = topo.engines(h, cores[r ^ k])
-        to = [e for e in topo.engines(src, h) if e not in off]
-        n = len(to) // VIA
-        out[k] = (h, to[n * i:n * (i + 1)], off)
+    for k in ks:
+        can = [h for h in free if topo.may_write(h, cores[r ^ k])]
+        out.setdefault(min(can, key=lambda h: len(out.get(h, ()))), []).append(k)
     return out
+
+
+def _inner(topo, cores, r):
+    src = cores[r]
+    far = [c for c in cores if topo.chip(c) != topo.chip(src)][0]
+    mate = [c for c in topo.cores_of(src) if c != src][0]
+    return [e for e in topo.engines(src, mate) if e not in topo.engines(src, far)]
+
+
+def _roots_at(r, k):
+    return P * (r - (r > r ^ k))
+
+
+STAGES = (("R0", VIA0, "LC", _roots_at, P, "e2", True),
+          ("R1", VIA1, "C1", lambda r, k: OWN + K1 * k, K1, "p1", False),
+          ("R2", VIA2, "L2", lambda r, k: S * (r % 4), S, "pa", False))
 
 
 def _helper(g, core, T, topo):
     cores = list(T.cores)
+    sent = 0
     for r in range(N):
-        for k, (h, to, off) in _relay(topo, cores, r).items():
-            if h != core:
+        for buf, via, land, at, w, sem, shared in STAGES:
+            plan = _relay(topo, cores, r, via)
+            if core not in plan:
                 continue
+            ks = plan[core]
+            off = topo.engines(core, cores[r ^ ks[0]])
             for x in "cs":
-                src, dst = T["R1" + x][:], T["L1" + x][:, K1 * r:K1 * (r + 1)]
+                src, dsts = T[buf + x][:], [T[land + x][:, at(r, k):at(r, k) + w] for k in ks]
                 if x == "c":
-                    src, dst = src.bitcast(dt.uint8), dst.bitcast(dt.uint8)
-                g.wait_ge(T.sem["h1" + x], len(to))
+                    src, dsts = src.bitcast(dt.uint8), [d.bitcast(dt.uint8) for d in dsts]
+                g.wait_ge(T.sem[buf + x], len(_inner(topo, cores, r)) // (2 if shared else len(plan)))
                 g.remote_dma_fused([RemoteDMATransfer(
-                    dst_ids=[_dst(topo, cores[r ^ k])], dma_engine_mask=_mask(off), remote_sem=T.sem.p1,
-                    srcs=[src], dsts=[dst])], local_sem=T.sem.sent)
-            g.wait_ge(T.sem.sent, 2 * len(off))
+                    dst_ids=[_dst(topo, cores[r ^ k]) for k in ks], dma_engine_mask=_mask(off), remote_sem=T.sem[sem],
+                    srcs=[src], dsts=dsts)], local_sem=T.sem.sent)
+                sent += len(off)
+    if sent:
+        g.wait_ge(T.sem.sent, sent)
 
 
 def rank_program(g, core, T, topo):
@@ -192,11 +215,8 @@ def rank_program(g, core, T, topo):
     def ms(out, val):
         op("v", lambda: V.memset(out[0], val), (), (out,))
 
-    def scan(out, reset, data):
-        op("v", lambda: V.tensor_tensor_scan(out[0], reset[0], data[0], 0.0, Op.mult, Op.add), (reset, data), (out,))
-
-    def red(out, in_):
-        op("v", lambda: V.tensor_reduce(out[0], in_[0], AxisListType.X, Op.add), (in_,), (out,))
+    def scan(out, reset, data, o0=Op.mult, o1=Op.add):
+        op("v", lambda: V.tensor_tensor_scan(out[0], reset[0], data[0], 0.0, o0, o1), (reset, data), (out,))
 
     def tr(out, in_):
         op("v", lambda: V.transpose(out[0], in_[0]), (in_,), (out,))
@@ -211,8 +231,9 @@ def rank_program(g, core, T, topo):
     def fill(out, n, val):
         act(out, R("JB", 0, n), scale=0.0, bias=val)
 
-    def quant(name, a, b, tile):
-        o, s, i = R(name + "c", a, b), R(name + "s", a, b), R(tile, 4 * a, 4 * b)
+    def quant(name, a, b, tile, at=None):
+        at = 4 * a if at is None else at
+        o, s, i = R(name + "c", a, b), R(name + "s", a, b), R(tile, at, at + 4 * (b - a))
         op("v", lambda: V.quantize_mx(o[0], s[0], i[0]), (i,), (o, s))
 
     def mm(bank, lhs, la, rhs, a, b, start=True, stop=True, arrive=()):
@@ -221,17 +242,19 @@ def rank_program(g, core, T, topo):
         op("p", lambda: PE.matmul_mx(o[0], v[0][0], v[1][0], v[2][0], v[3][0], start, stop), v, (o,), arrive,
            acc=not start)
 
-    def pick(dst, a, b, src, offs, win=(0, None), arrive=()):
+    def pickc(dst, a, b, src, offs, win=(0, None), arrive=()):
         cp(u32(R(dst + "c", a, b)), by(u32(R(src + "c", *win)), offs), arrive)
+
+    def picks(dst, a, b, src, offs, win=(0, None), arrive=()):
         act(R(dst + "s", a, b), by(R(src + "s", *win), offs), Act.Copy, arrive)
+
+    def pick(*a, **kw):
+        pickc(*a, **kw)
+        picks(*a, **kw)
 
     def dma(q, out, in_, arrive=()):
         return op(q, lambda: queues[q].dma_start(ap(out), ap(in_)), (in_,), (out,) if isinstance(out, tuple) else (),
                   arrive, dma=True)
-
-    def move(q, dst, a, src, b, n):
-        dma(q, u8(R(dst + "c", a, a + n)), u8(R(src + "c", b, b + n)))
-        dma(q, R(dst + "s", a, a + n), R(src + "s", b, b + n))
 
     def iota(out, pattern, base=0, cm=0, whole=False):
         if whole:
@@ -248,8 +271,8 @@ def rank_program(g, core, T, topo):
             srcs=[s[0]], dsts=[x[0] for _, x in d]) for s, d, e, sem in transfers], local_sem=T.sem.sent),
            [t[0] for t in transfers])
 
-    def direct(src, dst, cast, w, at, ks, sem, base=0):
-        remote([(cast(R(src, base + w * k, base + w * (k + 1))), [(cores[me ^ k], cast(R(dst, at, at + w)))], e, sem)
+    def direct(src, dst, cast, w, frm, to, ks, sem):
+        remote([(cast(R(src, frm(k), frm(k) + w)), [(cores[me ^ k], cast(R(dst, to(k), to(k) + w)))], e, sem)
                 for k, e in _share(topo, cores, me, ks).items()])
 
     def landed(*parts):
@@ -260,25 +283,26 @@ def rank_program(g, core, T, topo):
 
     both = (("c", u8), ("s", same))
 
-    def spread(name, base, w, on="va"):
+    def spread(name, base, w, on="va", step=1):
         def mv(q, po, pi, n, a, b):
-            o, i = R(name, base + a, base + b, 1, (po, po + n)), R(name, base + a, base + b, 1, (pi, pi + n))
+            a, b = base + w * a, base - base % step + w * b
+            o, i = R(name, a, b, step, (po, po + n)), R(name, a, b, step, (pi, pi + n))
             if q == "v":
                 cp(o, i)
             else:
                 act(o, i, Act.Copy)
-        mv(on[0], 0, 32, 32, w, 2 * w)
-        mv(on[1], 64, 96, 32, 3 * w, 4 * w)
-        mv(on[0], 32, 0, 32, 0, w)
-        mv(on[1], 96, 64, 32, 2 * w, 3 * w)
-        mv(on[0], 64, 0, 64, 0, 2 * w)
-        mv(on[1], 0, 64, 64, 2 * w, 4 * w)
+        return [lambda: mv(on[0], 0, 32, 32, 1, 2), lambda: mv(on[1], 64, 96, 32, 3, 4),
+                lambda: mv(on[0], 32, 0, 32, 0, 1), lambda: mv(on[1], 96, 64, 32, 2, 3),
+                lambda: mv(on[0], 64, 0, 64, 0, 2), lambda: mv(on[1], 0, 64, 64, 2, 4)]
 
-    cg, ca, cs, ck, ch = (c1("CF", j) for j in range(5))
-    cPN, cOA, cBG, c64, cLM, cK1, cPZ = (c1("CD", j) for j in range(7))
-    oWQ, oV0, oG, oPN, oSV, oGR, oI = (R("OU", a, b) for a, b in ((0, 8), (8, 16), (16, 22), (22, 25), (26, 27),
-                                                                   (28, 29), (56, 59)))
-    oF, oF0, oW0, oTK, oC1, oNM = (R("OT", a, b) for a, b in ((0, 3), (4, 7), (8, 10), (10, 12), (12, 13), (14, 20)))
+    def run(calls):
+        for c in calls:
+            c()
+
+    cg, ca, c4, cs, ck, ch, c2 = (c1("CF", j) for j in range(7))
+    cPN, cOA, cBG, c64, cLM, cB, cPS, cZ, cF, cX = (c1("CD", j) for j in range(10))
+    oWQ, oV0, oWM, oG, oPN, oSV, oF, oU1, oU, oU0, oUS, oLQ = (R("OU", a, b) for a, b in (
+        (0, 8), (8, 16), (16, 24), (24, 30), (30, 33), (34, 35), (36, 38), (38, 40), (40, 42), (40, 41), (40, 43), (44, 46)))
 
     def JB(n):
         return R("JB", 0, n)
@@ -286,46 +310,48 @@ def rank_program(g, core, T, topo):
     def quad(name, q, a, b):
         return R(name, a, b, 1, (32 * q, 32 * q + 32))
 
-    def shifted(q, out, in_, k, b):
+    def shifted(q, out, in_, h):
         if q == "v":
-            ts(out, in_, c1("DH", 8 * b + k), None, Op.add)
+            ts(out, in_, h, None, Op.add)
         else:
-            act(out, in_, bias=c1("DH", 8 * b + k))
+            act(out, in_, bias=h)
+
+    def made(k):
+        return K1 * XA.index(k) if k else OWN
 
     def child(q, k, b):
-        shifted(q, R("X1", 4 * K1 * k + b, 4 * K1 * (k + 1), 4), R("A0", K1 * b, K1 * (b + 1)), k, b)
-
-    def twice(a):
-        act(R("JM", a, min(2 * a, TW_)), R("JM", 0, min(a, TW_ - a)), Act.Copy)
+        shifted(q, R("X1", 4 * made(k) + b, 4 * (made(k) + K1), 4), R("A0", AW * b, AW * b + K1),
+                c1("DH", 8 * b + k) if k else c1("A0", AW * b + K1))
 
     dma("s", R("T0", 0, 4 * P), T.r0[:])
     dma("a", R("T0", 4 * UQ), T.u[:, 0:8])
     dma("s", R("T1", 0, 4 * K1), T.r1[:])
     dma("s", R("T2"), T.r2[:])
-    dma("s", R("TW"), T.w[:])
     iota(c1("PI"), [[0, 1]], 0, 1, True)
     iota(R("JB"), [[1, 128]])
-    ms(R("RW"), 0.0)
-    iota(R("RW", 0, 48, 2), [[0, 4], [16, 2], [32, 3]])
-    iota(R("RW", 65, 112, 2), [[0, 4], [16, 2], [0, 3]], 96)
-    iota(R("RW", 128, 152), [[6, 8], [2, 3]])
-    iota(R("RW", 224, 320), [[16 - 32 * (me % 2), 2], [1, CAP], [32, 4]], 16 * (me % 2))
-    iota(R("JX"), [[(1 - 2 * (me >> i & 1)) << i, 2] for i in (2, 1, 0)], me)
+    for j in (1, 2):
+        iota(c1("PI", j), [[0, 1]], 0, 4 ** j, True)
+    iota(R("JM"), [[0, 3], [1, 16]])
+    iota(R("TB1"), [[-16, 3], [1, 48]])
     ms(R("T0", 4 * P, 4 * UQ), 0.0)
-    for j, (s1, s2) in enumerate(((4, 15), (0, 15), (2, 3), (0, 3), (4, 1))):
-        ts(c1("CI", j), c1("PI"), s1, s2, Op.logical_shift_right, Op.bitwise_and)
-    ms(R("OF"), 0.0)
-    cp(R("CF", 0, 5), R("CI", 0, 5))
+    ms(R("TE"), 0.0)
     cp(R("CP"), c1("PI"))
-    ms(R("TE", 0, 1024), 0.0)
+    ms(R("T1", 4 * K1), 0.0)
+    ts(R("TE", 3, 515, 4), R("JB"), R("CP"), None, Op.is_equal)
+    ms(R("X1", 4 * LZ, 4 * OWN), 0.0)
+    quant("QE", 0, 128, "TE", 3)
+    for a, b, v, m in ((0, 2, R("PI", 0, 3, 2), 15), (2, 5, R("PI", 0, 3), 3), (5, 7, R("PI", 0, 2), 1)):
+        ts(R("CI", a, b), v, 4, m, Op.logical_shift_right, Op.bitwise_and)
+    cp(R("CF", 0, 7), R("CI", 0, 7))
+    quant("QE", 128, 256, "TE", 2)
     quant("Q0", 0, 128, "T0")
-    ms(R("TE", 1024), 0.0)
 
     eng = _share(topo, cores, me, range(N))
     far = [k for k in eng if topo.chip(cores[me ^ k]) != topo.chip(core)]
     near = [k for k in eng if k not in far]
     off = sorted(e for k in far for e in eng[k])
-    on = eng[near[0]]
+    on = _inner(topo, cores, me)
+    half = len(on) // 2
     for j, (x, cast) in enumerate(both):
         land = {k: (cores[me ^ k], cast(R("Q0" + x, UQ + 2 * k, UQ + 2 * k + 2))) for k in eng}
         remote([(cast(R("Q0" + x, UQ, UQ + 2)), [land[k] for k in far], off, "e1")]
@@ -333,262 +359,290 @@ def rank_program(g, core, T, topo):
     E1 = (("e1", 2 * (len(far) * len(off) + len(near))),)
     for x, cast in both:
         src = cast(R("Q0" + x, 0, P))
-        at = {k: P * (me - (me > me ^ k)) for k in eng}
-        land = {k: (cores[me ^ k], cast(R("LC" + x, at[k], at[k] + P))) for k in eng}
-        remote([(src, [land[k] for k in far], off, "e2")] + [(src, [land[k]], on[0:3:2], "e2") for k in near])
+        land = {k: (cores[me ^ k], cast(R("LC" + x, _roots_at(me, k), _roots_at(me, k) + P))) for k in eng}
+        remote([(src, [land[k] for k in far if k not in VIA0], off, "e2")]
+               + [(src, [land[k]], on[0:3:2], "e2") for k in near]
+               + [(src, [(h, cast(R("R0" + x))) for h in _relay(topo, cores, me, VIA0)], on[half:], "R0" + x)][:len(VIA0)])
     E2 = (("e2", 2 * (len(far) * len(off) + 2 * len(near))),)
-    op("s", None, arrive=E2)
-    move("s", "L1", NA, "Q0", 32, 16)
-    move("s", "L2", 0, "Q0", 32, 16)
-    move("s", "L2", HW, "Q0", 32, 16)
 
-    iota(R("KF", 0, 48, 2), [[0, 24]])
-    iota(R("NT", 0, NA), [[0, N], [1, K1]])
-    iota(R("NT", NA), [[0, 16]], -1)
-    iota(R("ILB", 0, 33), [[0, 11], [4, 3]])
-    act(R("JM", 0, 16), JB(16), Act.Copy)
+    def relay(src, buf, via, w, frm):
+        plan = _relay(topo, cores, me, via)
+        n = len(on) // len(plan)
+        for x, cast in both:
+            remote([(cast(R(src + x, frm(ks[0]), frm(ks[0]) + w)), [(h, cast(R(buf + x)))], on[n * i:n * (i + 1)], buf + x)
+                    for i, (h, ks) in enumerate(plan.items())])
+
+    iota(R("NT"), [[0, 2], [1, K1]])
+    iota(R("KF"), [[0, 16]], OWN)
+    iota(R("X2", 4 * HH, 4 * (HH + 16)), [[0, 64]])
+    iota(R("KF", 3, 12), [[K1, 3], [0, 3]], made(1))
+    iota(R("X2", 4 * (HA + HH)), [[0, 16]])
+    iota(R("JQ"), [[0, 8], [1, 4], [0, 4]])
+    dma("s", R("TW"), T.w[:], E1)
+    fill(R("OF", 14, 16), 2, float(UQ + 1))
     act(R("OF", 0, 8), JB(8), scale=2.0, bias=float(UQ))
-    act(R("OF", 8, 16), JB(8), scale=4.0, bias=cs)
-    twice(16)
-    act(cPN, ch, scale=16.0, bias=cs)
-    act(c1("OF", 26), ch, scale=16.0, bias=ca)
-    twice(32)
-    act(R("OF", 16, 22, 2), JB(3), scale=4.0, bias=cs)
-    act(R("OF", 17, 22, 2), JB(3), scale=4.0, bias=cs)
-    twice(64)
-    act(R("OF", 22, 25), JB(3), scale=4.0, bias=cPN)
-    act(c1("OF", 28), cg, Act.Copy)
-    twice(128)
-    act(R("OF", 56, 60), JB(4), scale=16.0, bias=ca)
-    act(c64, ca, scale=-1.0, bias=float(M))
-    twice(256)
-    for b in range(4):
-        ts(R("TE", 512 * b + b, 512 * (b + 1), 4), R("JB"), R("CP"), None, Op.is_equal)
-    ms(R("T1", 4 * K1), 0.0)
-    ms(R("OW"), UQ)
-    cp(R("OU"), R("OF", 0, 60))
-    for s in range(3):
-        act(R("TB1", 48 * s, 48 * s + 48), JB(48), bias=-16.0 * s)
-    quant("QE", 0, 512, "TE")
-    pick("V0", 0, 128, "Q0", oV0, (0, 128))
+    fill(R("OF", 16, 24), 8, float(UQ))
+    fill(R("RR", 0, 128), 128, 1.0)
+    fill(R("RR", 128, 144), 16, 1.0)
+    act(R("OF", 8, 14), JB(6), scale=4.0, bias=cs)
+    act(cX, ca, scale=4.0 / 3, bias=2.0 / 3)
+    act(cBG, ca, Act.Relu, scale=BIG, bias=-7 * BIG)
+    fill(R("RR", 0, 144, 48), 3, 0.0)
+    act(R("TT", 0, 2), JB(2), scale=64.0 / 3, bias=cX)
+    act(c1("CM0", 48), ca, Act.Relu, scale=24.0, bias=-168.0)
+    act(cB, cg, scale=float(K1), bias=float(ZC))
+    act(cOA, ch, scale=float(K1), bias=ck)
+    quant("QE", 256, 384, "TE", 1)
+    cp(R("OU", 0, 24), R("OF", 0, 24))
     quant("Q1", 0, 128, "T1")
+    pick("V0", 0, 128, "Q0", oV0, (0, 128))
+    quant("QE", 384, 512, "TE", 0)
     for b in range(4):
         mm("P%d" % b, "QE", 128 * b, "V0", 0, 128, True, False)
         mm("P%d" % b, "QE", 128 * b, "Q1", 0, 128, False, True)
-    for b in range(4):
-        mm("P%d" % (4 + b), "QE", 128 * b, "Q0", 0, 128)
-    for j in range(3):
-        act(R("J4", 4 * j, 4 * j + 4), JB(4), Act.Copy)
-        act(R("RW", 160 + j, 184, 3), R("JX"), Act.Copy)
-        act(R("KF", 1 + 2 * j, 48, 6), JB(8), Act.Copy, scale=float(K1))
-    for j in range(2):
-        fill(R("RW", 192 + j, 208, 2), 8, 15.0 + 16 * j)
-    act(R("RW", 1, 48, 2), R("RW", 0, 48, 2), Act.Copy)
-    act(R("RW", 64, 112, 2), R("RW", 0, 48, 2), Act.Copy)
-    act(R("XG"), by(R("JX"), oGR), Act.Copy)
     ts(R("TH1"), R("TB1"), ca, -EPS, Op.is_lt, Op.mult)
+    cp(R("KI"), R("TT", 0, 2))
     ts(R("DM"), R("JM"), ca, None, Op.is_equal)
-    ms(R("RR"), 1.0)
-    ms(R("R16"), 1.0)
-    ts(cLM, ca, float(CAP), c64, Op.is_lt, Op.mult)
-    ms(R("RR", 0, 290, 96), 0.0)
-    ms(R("R16", 0, TW_, 16), 0.0)
-    ts(R("MK", 0, 12), R("J4", 0, 12), cs, None, Op.is_equal)
-    act(cBG, ca, Act.Relu, scale=BIG, bias=-7 * BIG)
-    act(c1("CM0", 48), ca, Act.Relu, scale=24.0, bias=-168.0)
-    act(cOA, ch, scale=float(K1), bias=ck)
-    act(R("PY0"), JB(32), scale=4.0, bias=float(K1 * me - NA))
-    act(R("TH0", 0, P), R("TH1", 0, P), Act.Copy)
-    act(R("TH0", P, 2 * P), R("TH1", 48, 48 + P), bias=cBG)
-    act(cOA, cOA, bias=float(NA - K1 * me))
-    fill(R("LM"), 32, cLM)
-    act(cK1, cBG, Act.Sign)
-    act(cPZ, ca, bias=16.0)
-    act(R("DN"), R("DM", 0, 48), Act.Copy, scale=-1.0)
-    act(cK1, cK1, bias=3.0, scale=2.0)
+    ts(R("TT", 4, 6), R("KI"), 31.0, 2.0, Op.min, Op.mult)
+    ts(R("MK", 0, 12), R("JM", 0, 48, 4), 0.25, cs, Op.mult, Op.is_equal)
+    act(R("PY0"), JB(32), scale=4.0, bias=cB)
+    act(cOA, cB, scale=-1.0, bias=cOA)
+    act(cPN, ch, scale=16.0, bias=cs)
+    act(cF, c2, scale=16.0, bias=15.0)
+    small = [lambda: act(R("TH0", 0, P), R("TH1", 0, P), Act.Copy),
+             lambda: act(R("TH0", P, 2 * P), R("TH1", 48, 48 + P), bias=cBG),
+             lambda: act(R("MX"), R("DM", 0, 16), scale=-2 * HUGE, bias=HUGE),
+             lambda: act(R("OF", 24, 30, 2), JB(3), scale=4.0, bias=cs),
+             lambda: act(R("OF", 25, 30, 2), JB(3), scale=4.0, bias=cs),
+             lambda: act(R("OF", 30, 34), JB(4), scale=4.0, bias=cPN)]
     for b in range(4):
-        act(R("A0", K1 * b, K1 * (b + 1)), R("P%d" % b, 0, K1), Act.Copy)
+        act(R("A0", AW * b, AW * b + K1 + 1), R("P%d" % b, 0, K1 + 1), Act.Copy)
+        run(small[2 * b:2 * b + 2])
     for b in range(4):
-        act(c1("DH", 8 * b), R("P%d" % (4 + b), UQ + 1, UQ + 2), Act.Copy)
-    for b in range(4):
-        child("a", 0, b)
+        child(OWNQ[b], 0, b)
     quant("Q2", 0, NP, "T2")
-    tt(R("RM"), R("RW"), R("DM"), Op.mult)
-    ts(R("TA"), JB(8), c1("XG"), -EPS, Op.is_lt, Op.mult)
-    scan(R("RS"), R("R16"), R("RM"))
-    ts(R("TB"), JB(8), c1("XG"), 4 * BIG, Op.is_equal, Op.mult)
-    cp(R("OT"), R("RS", 15, TW_, 16))
-    tt(R("TH8"), R("TA"), R("TB"), Op.add)
-    ts(c1("ON"), c1("XG"), 6.0, cK1, Op.mult, Op.add)
-    quant("QW", 0, 128, "TW")
+    act(R("OF", 34, 36), R("CF", 5, 7), scale=16.0, bias=ca)
+    act(c1("OF", 36), ck, scale=32.0, bias=cF)
+    act(c1("OF", 37), ck, scale=32.0, bias=cF)
+    act(R("OF", 38, 40), R("TT", 4, 6), bias=1.0)
+    act(R("OF", 40, 42), R("TT", 4, 6), Act.Copy)
+    act(R("OF", 42, 44), R("CF", 0, 2), Act.Copy, scale=8.0)
+    act(R("OF", 44, 46), R("TT", 4, 6), scale=2.0, bias=-1.0)
+    act(c64, ca, scale=-1.0, bias=float(M))
+    act(cLM, ca, Act.Relu, scale=100.0, bias=-100.0 * (CAP - 1))
+    quant("C1", LZ, LZ + 128, "X1")
+    cp(R("OU", 24, 46), R("OF", 24, 46))
+    act(cLM, cLM, scale=-1.0, bias=c64)
+    act(R("DN"), R("DM"), Act.Copy, scale=-1.0)
+    fill(R("LM"), 32, cLM)
+    ha, hb = ((me ^ k0) // 4 for k0, _ in PARTS)
+    s0, s1 = 1 - 2 * (me & 1), 1 - (me & 2)
+    pa, pb = ((64 * h, 64 * h + 64) for h in (ha, hb))
+    late = [
+        lambda: act(R("CD", 6, 7, 1, pa), R("CF", 2, 3, 1, pa), scale=-float(S), bias=float(HH)),
+        lambda: act(R("CD", 6, 7, 1, pb), R("CF", 2, 3, 1, pb), scale=float(S * s1), bias=float(S * (1 + me % 4))),
+        lambda: act(cZ, ck, bias=float(HH)),
+        lambda: act(R("CD", 6, 7, 1, pb), R("CF", 5, 6, 1, pb), scale=float(S * (s0 - s1)), bias=R("CD", 6, 7, 1, pb)),
+        lambda: act(c1("PS"), ca, scale=-4.0, bias=cPS)]
+    gaps = [lambda: ts(R("TA"), JB(8), cg, -EPS, Op.is_lt, Op.mult),
+            lambda: ts(R("TB"), JB(8), cg, 4 * BIG, Op.is_equal, Op.mult),
+            lambda: ts(R("LMM"), R("JQ"), ck, cLM, Op.is_equal, Op.mult),
+            lambda: tt(R("TH8"), R("TA"), R("TB"), Op.add)]
 
     pick("WQ", 0, 128, "Q0", oWQ, (0, NL), E1)
     for b in range(3):
         mm("P%d" % b, "QE", 128 * b, "Q0", NL - 128, NL, arrive=E1)
     mm("P4", "WQ", 0, "Q0", 0, 128)
     mm("P3", "QE", 128 * 3, "Q0", NL - 128, NL)
+    mm("P7", "WQ", 0, "C1", LZ, LZ + 128)
     for b in range(4):
         act(R("DH", 8 * b + 1, 8 * b + 8), R("P%d" % b, 128 - 2 * N + 3, 128, 2), Act.Copy)
     xs = [(k, b) for k in XA for b in range(4)]
-    for k, b in xs[:XN]:
-        child("a", k, b)
+    xv = [xs[i] for i in XV]
+    for k, b in xs:
+        if (k, b) not in xv:
+            child("a", k, b)
+
+    def more(n=1):
+        for _ in range(n):
+            if xv:
+                child("v", *xv.pop(0))
+
+    def group(ks, bank):
+        while any(k in ks for k, _ in xv):
+            more()
+        a, b = made(ks[0]), made(ks[-1]) + K1
+        quant("C1", a, b, "X1")
+        return lambda: mm(bank, "WQ", 0, "C1", a, b)
+
+    got = [len(VIA1) * len(off)]
+
+    def send(ks):
+        if ks[0] in VIA1:
+            return relay("C1", "R1", VIA1, K1, made)
+        for x, cast in both:
+            direct("C1" + x, "C1" + x, cast, K1, made, lambda k: OWN + K1 * k, ks, "p1")
+        got.append(landed(ks))
+
     tt(R("M0"), R("P4", 0, 32), R("DM", 0, 32), Op.mult)
     cp(R("AS"), R("P4", 0, 32))
-    scan(R("BS0"), R("R16", 0, 32), R("M0"))
+    scan(R("BS0"), R("RR", 0, 96, 3), R("M0"))
+    more()
     for s in range(2):
         ts(R("D0", P * s, P * s + P), R("AS", 0, P), c1("BS0", 16 * s + 15), None, Op.subtract)
+    more()
     tt(R("CM0", 0, 48), R("D0"), R("TH0"), Op.is_gt)
-    scan(R("SN0", 0, 49), R("RR", 48, 146, 2), R("CM0", 0, 49))
+    more()
+    scan(R("SN0", 0, 49), R("RR", 24, 73), R("CM0", 0, 49))
+    more()
     cp(R("OL0"), R("SN0", 23, 49, 25))
-    quant("C1", K1 * 4, K1 * 6, "X1")
-    for x, cast in both:
-        remote([(cast(R("C1" + x, K1 * k, K1 * (k + 1))), [(h, cast(R("R1" + x)))], to, "h1" + x)
-                for k, (h, to, _) in _relay(topo, cores, me).items()])
+    group(XA[:2], "P5")()
+    send(XA[:2])
     cp(by(R("SS0"), R("OL0")), R("AS"))
     cp(by(R("SR0"), R("OL0")), R("PY0"))
-    tt(R("MS0"), R("SS0", 0, 16), R("DM", 0, 16), Op.mult)
+    scan(R("NS"), R("MX"), R("SS0", 0, 16), Op.min, Op.max)
     tt(R("SE", 0, 12), R("SR0", 0, 12), R("MK", 0, 12), Op.mult)
-    red(c1("NS"), R("MS0"))
-    scan(R("SF", 0, 12), R("RR", 0, 288, 24), R("SE", 0, 12))
-    quant("C1", K1 * 6, K1 * 8, "X1")
-    for x, cast in both:
-        direct("C1" + x, "L1" + x, cast, K1, K1 * me, range(6, 8), "p1")
+    more()
+    scan(R("SF", 0, 12), R("RR", 0, 144, 12), R("SE", 0, 12))
+    more()
     ts(R("OA", 0, 3), R("SF", 3, 12, 4), cOA, None, Op.add)
-    for k, b in xs[XN:]:
-        child("v", k, b)
-    mm("P6", "WQ", 0, "C1", NA // 2, NA)
-    quant("C1", 0, 192, "X1")
+    later = group(XA[2:5], "P6")
+    send(XA[2:4])
     mm("P3", "WQ", 0, "LC", 0, NO, arrive=E2)
-    mm("P5", "WQ", 0, "C1", 0, 192)
+    later()
+    more(9)
     for a, b, o in ((0, P * me, Op.is_ge), (P * me, NO, Op.is_gt)):
         if a < b:
-            ts(R("CG", a, b), R("P3", a, b), c1("NS"), None, o)
-    quant("C1", 192, NA // 2, "X1")
-    mm("P7", "WQ", 0, "C1", 192, NA // 2)
-    red(c1("CN0"), R("CG"))
-    ts(R("FL0"), R("LM"), c1("CN0"), None, Op.is_gt)
+            ts(R("CG", a, b), R("P3", a, b), c1("NS", 15), None, o)
+    group(XA[5:], "P0")()
+    send(XA[4:])
+    iota(R("BQ", P), [[0, P]])
+    for m in range(3):
+        iota(R("BQ", m, P, 3), [[K1 * (1 - 2 * (me >> i & 1)) << i, 2] for i in (2, 1, 0)], ZC + K1 * me)
+    iota(R("R4"), [[0, 32], [256, 4]])
+    scan(R("CH"), R("CG"), R("CG"), Op.add, Op.max)
+    P1 = (("p1", 2 * sum(got)),)
+    act(quad("AF", 0, 0, K1), quad("P7", 0, ZC, 128), Act.Copy)
+    act(quad("AF", XA[0] // 2, 0, 192), quad("P5", XA[0] // 2, 0, 192), Act.Copy)
+    act(quad("AF", XA[2] // 2, 0, 192), quad("P6", XA[2] // 2, 0, 192), Act.Copy)
+    act(quad("AF", 0, K1, 192), quad("P6", 0, 192, 192 + K1), Act.Copy)
+    act(quad("AF", 1, 0, 192), quad("P0", 1, 0, 192), Act.Copy)
+    ts(R("FL0"), R("LM"), c1("CH", NO - 1), None, Op.is_gt)
+    gaps[0]()
     tr(R("FT0"), R("FL0"))
+    gaps[1]()
     ts(R("PEN"), by(R("FT0"), oPN), -1.0, BIG, Op.add, Op.mult)
-    for x, cast in both:
-        direct("C1" + x, "L1" + x, cast, K1, K1 * me, range(4), "p1")
-    P1 = (("p1", 2 * (landed(range(6, 8), range(4))
-                      + sum(len(_relay(topo, cores, me ^ k)[k][2]) for k in _relay(topo, cores, me)))),)
-    move("s", "L1", K1 * me, "C1", 0, K1)
 
-    for q in (2, 3):
-        act(quad("AF", q, 0, 192), quad("P6", q, 192 * (q % 2), 192 * (q % 2 + 1)), Act.Copy)
-    act(quad("AF", 0, 0, 192), quad("P5", 0, 0, 192), Act.Copy)
-    act(quad("AF", 1, 0, 192), quad("P7", 1, 0, 192), Act.Copy)
-    act(R("PB"), by(R("NT", 0, 192), R("OA", 0, 3)), Act.Copy)
-    act(R("JK", 0, 48), R("PEN"), Act.Copy, scale=1.0 / BIG, acc=c1("NI"))
-    fill(R("G0", 96, 128), 32, c1("NI"))
-    tt(R("A1"), by(R("AF"), R("OA", 0, 3)), R("PEN"), Op.add)
-    tt(R("M1"), R("A1"), R("DN"), Op.mult)
-    scan(R("BS1"), R("R16", 0, 48), R("M1"))
     tt(R("SV"), by(R("FT0"), oSV), R("SR0", 0, 16), Op.mult)
+    tt(R("A1"), by(R("AF"), R("OA", 0, 3)), R("PEN"), Op.add)
+    act(R("JK"), R("PEN"), Act.Copy, scale=1.0 / BIG, acc=c1("NI"))
+    act(R("G0", 32, 128), by(R("SV"), oG), Act.Copy)
+    gaps[2]()
+    tt(R("M1"), R("A1"), R("DN"), Op.mult)
+    gaps[3]()
+    scan(R("BS1"), R("RR", 0, 144, 3), R("M1"))
+    fill(R("G0", 0, 32), 32, c1("NI"))
     for s in range(2):
         act(R("D1", 48 * s, 48 * s + 48), R("A1"), bias=c1("BS1", 16 * s + 15))
     ts(R("D1", 96, 144), R("A1"), c1("BS1", 47), None, Op.add)
-    tt(R("CM1"), R("D1"), R("TH1"), Op.is_gt)
-    act(R("G0", 0, 96), by(R("SV"), oG), bias=float(NA))
-    scan(R("SN1"), R("RR", 0, 288, 2), R("CM1"))
     tr(R("GT0"), R("G0"))
+    act(R("PB"), by(R("NT"), R("OA", 0, 3)), Act.Copy)
+    tt(R("CM1"), R("D1"), R("TH1"), Op.is_gt)
+    act(R("MS", 1, 64, 2), by(R("GT0"), oF), Act.Copy)
+    scan(R("SN1"), R("RR"), R("CM1"))
+    run(spread("MS", 1, 16, "aa", 2))
     cp(R("OL1", 0, 3), R("SN1", 47, 144, 48))
-    act(R("MS", 48, 96), by(R("GT0"), oF0), Act.Copy)
-    spread("MS", 48, 12, "aa")
     cp(by(R("SR1"), R("OL1", 0, 3)), R("PB"))
     cp(by(R("SS1"), R("OL1", 0, 3)), R("A1"))
-    cp(R("G1"), by(R("SR1"), oG))
-    tt(R("MS1"), R("SS1", 0, 16), R("DM", 0, 16), Op.mult)
-    tr(R("GT1"), R("G1"))
-    tt(R("MS0"), R("SR1", 0, 16), R("DM", 0, 16), Op.mult)
-    act(R("MS2"), R("MS1"), Act.Copy, acc=c1("NI", 1))
-    act(R("SE"), R("MS0"), scale=4.0, bias=1.0 / 16, acc=c1("NI", 2))
-    fill(R("MS", 51, 96, 6), 8, c1("NI", 1))
-    fill(R("MS", 53, 96, 6), 8, c1("NI", 2))
+    act(R("G1"), by(R("SR1"), oG), Act.Copy)
+    run(late)
+    at = PIECE["SS1"][1] - 16 * (me % 2)
+    tr(R("GT1", 0, 32), R("WA", at, at + 32))
+    tr(R("GT1", 32, 128), R("G1"))
+    cp(R("MS", 0, 64, 2), by(R("GT1"), oF))
+    run(spread("MS", 0, 16, "va", 2))
     for p in PARTS:
-        direct("MS", "ML", same, 6, 6 * me, range(*p), "ms", 48)
+        direct("MS", "ML", same, 8, lambda k: 8 * k, lambda k: 8 * me, range(*p), "ms")
     MS = (("ms", landed(*[range(*p) for p in PARTS])),)
-    dma("s", R("ML", 6 * me, 6 * me + 6), R("MS", 48, 54))
-    tt(R("MS", 0, 48), by(R("GT1"), oF), R("KF"), Op.add)
-    spread("MS", 0, 12)
-    cp(R("LV"), R("MS", 1, 48, 2))
-    ts(R("LE"), R("MS", 0, 48, 2), 4.0, ck, Op.mult, Op.add)
-    at2 = HW * (me // 4) + 16 + S * (me % 4)
-    for i, (k0, k1) in enumerate(PARTS):
-        for src, pool, offs in (("PV", "C1", "LV"), ("PE", "Q2", "LE")):
-            pick(src, S * k0, S * k1, pool, R(offs, 3 * k0, 3 * k1))
-            for j in (0, 2, 1, 3):
-                mm("P%d" % (4 * i + j), "QE", 128 * j, src, S * k0, S * k1, src == "PV", src == "PE")
-    for i, (k0, k1) in enumerate(PARTS):
-        for j in (2, 3, 0, 1):
-            for k in range(k0, k1):
-                shifted("a" if j > 1 else "v", R("X2", 4 * S * k + j, 4 * S * (k + 1), 4),
-                        R("P%d" % (4 * i + j), S * (k - k0), S * (k - k0 + 1)), k, j)
-        quant("C2", S * k0, S * k1, "X2")
-        for x, cast in both[::1 - 2 * i]:
-            direct("C2" + x, "L2" + x, cast, S, at2, range(k0, k1), ("pa", "pb" + x)[i])
-        if i == 0:
-            pick("WM", 0, 128, "Q0", R("OW"), (0, 128))
-    PA = (("pa", 2 * landed(range(*PARTS[0]))),)
-    PB = {x: (("pb" + x, landed(range(*PARTS[1]))),) for x in "cs"}
+    ts(R("LE"), by(R("MS"), oU), 4.0, ck, Op.mult, Op.add)
+    tt(R("LF"), by(R("MS"), oU0), R("KF"), Op.add)
+    act(R("ML", 8 * me, 8 * me + 8), R("MS", 0, 8), Act.Copy)
+    pick("PE", HH, NP, "Q2", R("LE", 12, 24))
+    cp(R("LO"), R("LF"))
+    rest = [k for k in range(*PARTS[0]) if k not in VIA2]
+    if VIA2:
+        relay("PE", "R2", VIA2, S, lambda k: S * k)
+    for x, cast in both:
+        direct("PE" + x, "L2" + x, cast, S, lambda k: S * k, lambda k: S * (me % 4), rest, "pa")
+    PA = (("pa", 2 * (landed(rest) + len(VIA2) * len(off))),)
+    pick("PV", 0, HH, "C1", R("LO", 0, 12), (0, OWN + K1))
+    pick("PE", 0, HH, "Q2", R("LE", 0, 12))
+    for b, src in zip((0, 2, 0, 2, 1, 1, 3, 3), ("PV", "PV", "PE", "PE", "PV", "PE", "PV", "PE")):
+        mm("P%d" % b, "QE", 128 * b, src, 0, HH, src == "PV", src == "PE")
+    pick("WM", 0, 128, "Q0", oWM, (0, 128))
 
-    act(R("IL"), R("ILB", 0, 32), bias=cs)
-    for h in range(2):
-        act(R("PLZ", 12 * h, 12 * h + 12), JB(12), scale=16.0, bias=cPZ)
-    ts(R("LP"), by(R("ML"), oW0), ck, None, Op.add, arrive=MS)
-    pick("P1", 0, NP, "L1", R("LP", 0, 24), arrive=P1)
-    mm("P0", "WM", 0, "P1", 0, NP)
-    mm("P1", "QW", 0, "P1", 0, NP)
-    cp(R("SA"), by(R("ML"), c1("ON")))
-    ts(R("ZF"), R("TH8"), c1("SA"), 0.0, Op.add, Op.is_lt)
-    tt(R("CA", NP), R("ZF"), R("ML", 1, 48, 6), Op.mult)
-    for q in (2, 3, 4, 5, 6, 7, 0, 1):
-        ts(R("CA", S * q, S * (q + 1)), R("P0", S * q, S * (q + 1)), c1("SA"), c1("TH8", q), Op.subtract, Op.is_gt)
-    act(R("NR"), by(R("NT"), R("LP", 0, 24)), Act.Copy)
-    act(R("JK"), R("CA", 2 * S), Act.Copy, acc=c1("CN1", 1))
-    act(R("YS", 0, NP), R("P1", 0, NP), Act.Copy)
-    out = [dma("s", T.nm[0:1, 0:NP], R("NR", 0, NP, 1, (0, 1))), dma("s", T.y[:, 0:NP], R("YS", 0, NP))]
-    red(c1("CN1"), R("CA", 0, 2 * S))
-    pick("L2", at2, at2 + S, "C2", oI)
-    ts(R("FL1"), R("LM"), c1("CN1", 1), c1("CN1"), Op.subtract, Op.is_gt)
-    tr(R("FT1"), R("FL1"))
-    ts(R("NM", 0, 4), JB(4), c1("SA", 8), c1("FL1"), Op.add, Op.mult)
-    scan(R("FS1"), R("R16", 0, 32), R("FT1"))
-    cp(R("C8"), by(R("FS1"), oC1))
-    spread("C8", 0, 2)
-    for j in range(4):
-        fill(R("NN", 32 * j, 32 * j + 32), 32, c1("NM", j))
-    tt(R("TK"), by(R("C8"), oTK), R("IL"), Op.is_gt)
-    tt(R("LZ"), R("TK", 0, 24), R("PLZ"), Op.mult)
-    tr(R("NU"), R("NN"))
-    cp(R("LQ"), R("LZ"))
+    def two(k):
+        return HB + S * k + (16 if k else 0)
 
-    ha, hb = ((me ^ k0) // 4 for k0, _ in PARTS)
+    for b in (2, 0, 3, 1):
+        for k in range(4):
+            shifted("a" if b > 1 else "v", R("X2", 4 * two(k) + b, 4 * (two(k) + S), 4), R("P%d" % b, S * k, S * (k + 1)),
+                    c1("DH", 8 * b + k) if k else c1("A0", AW * b + K1))
+    quant("C2", HB, HA, "X2")
+    for x, cast in both:
+        direct("C2" + x, "C2" + x, cast, S, two, lambda k: HB - S * k, range(4), "pb")
+    PB = (("pb", 2 * landed(range(4))),)
 
-    def half(name, h, base=0):
-        return R(name, base + 192 * h, base + 192 * (h + 1))
+    low, banks, cSA = (0, 32), ("P6", "P7", "P0", "P1"), c1("LX", 32)
 
-    def window(name, h):
-        return R(name, HW * h, HW * h + 208)
+    def halfof(name, h, base=0):
+        return R(name, base + HH * h, base + HH * (h + 1))
 
-    at = [K1 * (me // 2 ^ q) for q in range(4)]
-    pick("OC", 192 * ha, 192 * (ha + 1), "L2", R("LQ", 12 * ha, 12 * ha + 12), (HW * ha, HW * ha + 208), PA)
-    mm("P2", "QW", 0, "OC", 192 * ha, 192 * (ha + 1))
-    out.append(dma("s", T.oc[:, 768 * ha:768 * (ha + 1)], u8(half("OCc", ha))))
-    act(half("OCs", hb), by(window("L2s", hb), R("LQ", 12 * hb, 12 * hb + 12)), Act.Copy, PB["s"])
-    act(half("YS", ha, NP), R("P2", 0, 192), Act.Copy)
+    ts(R("LP"), by(R("ML"), oU1), ck, None, Op.add, arrive=MS)
+    tt(R("LX"), by(R("ML"), oUS), R("BQ"), Op.add)
+    pick("P1", 0, NP, "C1", R("LP", 0, 24), (LZ, None), arrive=P1)
+    quant("QW", 0, 128, "TW")
+    cp(R("LV"), R("LX", 0, 32))
+    mm("P4", "WM", 0, "P1", 0, NP)
+    ts(R("ZF"), R("TH8"), cSA, 0.0, Op.add, Op.is_lt)
+    pick("PV", HH, NP, "C1", R("LV", 12 * ha, 12 * ha + 12), (LZ, None))
+    tt(R("CA", NP), R("ZF"), R("ML", 1, 64, 8), Op.mult)
+    mm("P5", "QW", 0, "P1", 0, NP)
+    for b in range(4):
+        mm(banks[b], "QE", 128 * b, "PV", HH, NP, True, False)
+    for b in range(4):
+        mm(banks[b], "QE", 128 * b, "L2", 0, HH, False, True, PA)
+    for q in range(N):
+        ts(R("CA", S * q, S * (q + 1)), R("P4", S * q, S * (q + 1)), cSA, c1("TH8", q), Op.subtract, Op.is_gt)
+    act(R("YS", 0, NP), R("P5", 0, NP), Act.Copy)
+    out = [dma("s", T.y[:, 0:NP], R("YS", 0, NP))]
+    for b in range(4):
+        shifted("a", R("X2", 4 * HA + b, 4 * (HA + HH), 4), R(banks[b], 0, HH), c1("A0", AW * b + K1))
+    scan(R("CB"), R("CA"), R("CA"), Op.add, Op.max)
+    ts(R("FV"), R("LMM"), c1("CB", NP + 7), c1("PS"), Op.is_gt, Op.mult)
+    tr(R("FT"), R("FV"))
+    scan(R("FS"), R("R4"), R("FT"), Op.min)
+    run(spread("FS", 3, 32, SPQ, 4))
+    ts(R("LQ"), by(R("FS"), oLQ), -1.0, cZ, Op.mult, Op.add)
+    act(R("T2N"), by(R("ML"), oU), scale=4.0, bias=ck)
+    quant("C2", HA, HA + HH + 4, "X2")
+    for h, win, bank, arrive in ((hb, (0, HH + 16), "P2", PB), (ha, (HA, None), "P3", ())):
+        pick("OC", HH * h, HH * (h + 1), "C2", R("LQ", 12 * h, 12 * h + 12), win, arrive)
+        mm(bank, "QW", 0, "OC", HH * h, HH * (h + 1))
+        out.append(dma("s", T.oc[:, 4 * HH * h:4 * HH * (h + 1)], u8(halfof("OCc", h))))
+    act(halfof("YS", hb, NP), R("P2", 0, HH), Act.Copy)
+    out.append(dma("s", T.y[:, NP + HH * hb:NP + HH * (hb + 1)], halfof("YS", hb, NP)))
     oa = [dma("a", T.osc[4 * q:4 * q + 4, :], R("OCs", 0, NP, 1, (32 * q, 32 * q + 4))) for q in range(4)]
-    out.append(dma("s", T.y[:, NP + 192 * ha:NP + 192 * (ha + 1)], half("YS", ha, NP)))
-    cp(u32(half("OCc", hb)), by(u32(window("L2c", hb)), R("LQ", 12 * hb, 12 * hb + 12)), PB["c"])
-    mm("P3", "QW", 0, "OC", 192 * hb, 192 * (hb + 1))
-    out.append(dma("s", T.oc[:, 768 * hb:768 * (hb + 1)], u8(half("OCc", hb))))
-    ts(R("NQ", at[0], at[0] + K1), by(R("NU"), oNM), -1.0, None, Op.add)
-    cp(half("YS", hb, NP), R("P3", 0, 192))
-    out.append(dma("s", T.y[:, NP + 192 * hb:NP + 192 * (hb + 1)], half("YS", hb, NP)))
-    for q in range(1, 4):
-        cp(quad("NQ", 0, at[q], at[q] + K1), quad("NQ", q, at[0], at[0] + K1))
-    out.append(dma("s", T.nm[0:1, NP:2 * NP], R("NQ", 0, NP, 1, (0, 1))))
+    ts(R("N2"), by(R("FS"), oLQ), 1000.0, -1.0, Op.mult, Op.add)
+    tt(R("N1"), by(R("ML"), oU1), R("BQ", 0, 32), Op.subtract)
+    cp(halfof("YS", ha, NP), R("P3", 0, HH))
+    out.append(dma("s", T.y[:, NP + HH * ha:NP + HH * (ha + 1)], halfof("YS", ha, NP)))
+    tt(R("N2B", p=low), R("N2", p=low), R("T2N", p=low), Op.min)
+    ts(R("N1B", p=low), R("N1", p=low), R("CF", 4, 5, 1, low), -1.0, Op.add, Op.max)
+    tr(R("N2T", p=low), R("N2B", p=low))
+    tr(R("N1T", p=low), R("N1B", p=low))
+    oa.append(dma("a", T.nm[0:1, NP:2 * NP], R("N2T", 0, 16, 1, (0, P))))
+    out.append(dma("s", T.nm[0:1, 0:NP], R("N1T", 0, 16, 1, (0, P))))
     op("s", None, after=out)
     op("a", None, after=oa)
     op("g", None, arrive=(("sent", sent[0]),))

@@ -14,11 +14,31 @@ HH, HB, HA = NP // 2, 3 * S, 7 * S + 16
 AW = 100
 EPS, BIG, HUGE = 1e-37, 2.0 ** 80, 2.0 ** 90
 PARTS = ((4, 8), (0, 4))
-XA = (4, 5, 6, 7, 1, 2, 3)
-XV = (4, 5, 6, 7, 18, 19, 26, 27)
-VIA0, VIA1, VIA2 = (4, 5), (4, 5), (4, 5)
-SPQ = "vv"
-OWNQ = "aava"
+GROUPS = (((6, 7), (6, 7), "R1", ()), ((4, 5, 1), (4, 5), "R1", (1,)), ((2, 3), (), "R3", (2, 3)))
+XA = sum((group[0] for group in GROUPS), ())
+VIA0, VIA2 = (4, 5, 6, 7), (4, 5)
+CYC, PEC, SLOW, WAKE, LOCAL, ISSUE, REMOTE, CALL, ROW, RATE, FIRST = 0.83, 0.63, 1.25, 150, 1400, 60, 2300, 250, 7, 20, 1300
+NEARLY, YIELD, SPARE = 30, 60, 1000
+NVP, NP1, NPE, DHQ, YQ = 1, 2, 2, "vvvv", "av"
+MERGE = 1
+NEAR, AQ = 4, "aava"
+ORDER = [
+    1, 15, 0, 6, 2, 10, 3, 4, 13, 7, 11, 5, 18, 12, 16, 17, 8, 19, -42, 14, -43, 44, 9, 47, -56, 111, 20, -45, 54, 55,
+    24, -50, -48, 46, -94, 21, -57, 25, -51, 87, -110, 86, 61, 60, 26, -103, 22, -100, 27, -58, 62, 59, -112, -95, 64,
+    28, -99, 52, 66, 23, -113, -101, 63, -96, 30, 85, -106, 65, -49, 67, 29, 97, 70, 102, 68, -119, 116, -105, 69, 53,
+    71, 88, 72, 104, 73, 80, 37, -92, -91, 89, -77, 32, 74, 84, 33, 76, 75, 35, -122, 107, -90, 108, -118, 78, -120,
+    93, 79, 36, -121, -98, 81, 31, 83, 38, 115, 109, 34, 117, 114, 39, 40, 124, 41, 123, 125, 126, 127, 132, 128, 133,
+    129, -136, 134, 157, 130, -149, 135, -153, 180, -158, 181, 155, -150, 182, -159, 137, -151, 169, -160, 184, -143,
+    183, 139, -152, -154, 185, -156, 167, -138, 186, -142, 161, -140, -141, -173, 187, -170, 144, -171, 162, -174,
+    189, -168, -172, 145, 147, 188, 163, 164, 175, 148, 194, 131, 191, 146, 165, 190, 176, 192, 195, 166, 196, 193,
+    177, 178, 197, 179, -200, 198, -217, 199, 202, 204, 201, 203, 220, 205, 207, 210, 211, 212, 208, 209, 206, 221,
+    222, 213, 223, 216, 214, 215, -227, 218, -230, -231, -228, 219, -224, 232, -229, 225, 226, -233, -234, -236, 238,
+    -235, 237, -240, 239, 241, -243, 244, 245, 242, 256, 247, 255, 251, 248, 246, 249, 260, 252, 258, 257, 262, 253,
+    261, 250, 259, 263, 264, 254, 274, 265, 272, 273, 267, 266, 82, 268, 270, 279, 269, 281, 280, 278, 271, 277, 282,
+    276, 275, -355, 283, -314, 286, 287, 284, 288, 289, 285, 291, 292, 362, 290, 297, 313, 316, 293, 319, 299, 318,
+    315, 294, 317, 322, 321, 323, 320, 298, 295, 324, 300, 302, 325, 351, 301, 326, 303, 352, 327, 305, 353, 304,
+    -328, 331, -330, 329, 354, 306, 296, 333, -332, 307, 308, 334, 311, 310, 309, 335, -356, 336, 312, 338, 357, 342,
+    341, 337, 358, 344, 343, 348, 359, 339, 349, 345, 350, 347, 340, 346, 361, 360,]
 
 F, BF, I32, U16, C, SC = "float32", "bfloat16", "int32", "uint16", "float8_e4m3fn_x4", "uint8"
 SCRATCH = {}
@@ -30,30 +50,30 @@ def _sb(dtype, **kw):
 
 
 _sb(BF, T0=512, T1=512, T2=4 * NP, TW=512, TE=516, JB=128, JM=48, JQ=128, X1=4 * (OWN + K1), X2=4 * (HA + HH + 4),
-    RR=144, R4=128, DM=48, DN=48, TB1=144, TH1=144, TH0=48, D0=48, CM0=50, SN0=50, D1=144, CM1=144, SN1=144,
+    RR=144, R4=128, DM=48, TB1=150, TH1=74, TH0=48, D0=48, CM0=50, SN0=50, D1=144,
     CG=NO, CH=NO, CA=NP + 8, CB=NP + 8, LMM=128, FV=128, FT=128, FS=128, NT=2 * K1, MX=16, JK=48, PS=2)
 for _n, _w in dict(Q0=144, Q1=128, Q2=NP, QW=128, QE=512, LC=NO, WQ=128, WM=128, V0=128, C1=OWN + N * K1, PE=NP,
-                   L2=HH, PV=NP, P1=NP, C2=HA + HH + 4, OC=NP, R0=P, R1=K1, R2=S).items():
+                   L2=HH, PV=NP, P1=NP, C2=HA + HH + 4, OC=NP, R0=P, R1=2 * K1, R2=S, R3=2 * K1).items():
     _sb(C, **{_n + "c": _w})
     _sb(SC, **{_n + "s": _w})
-_sb(F, CP=1, CF=8, A0=4 * AW, DH=32, AF=2 * K1, MS=64, ML=64, YS=2 * NP, SR0=200, SS0=200)
+_sb(F, FM=150, EQ=150, SN1=150, CP=1, CF=8, A0=4 * AW, DH=32, AF=2 * K1, MS=64, ML=64, YS=2 * NP, SR0=200, SS0=200)
 _sb(I32, PI=4, CI=8, KI=2)
 _sb(U16, OU=48, OL0=2, OL1=4, OA=4, LO=16, LV=32, LE=32, LP=32, LQ=32)
 for _k in range(8):
     SCRATCH["P%d" % _k] = ("psum", [128, 512], F)
 PIECE = {}
-for _b, _d in (("K", dict(CD=16, OF=48, PY0=32, MK=16, LM=32, TA=8, TB=8, TH8=8, BQ=48, TT=8, KF=16)),
+for _b, _d in (("K", dict(CD=16, OF=48, PY0=32, MK=16, LM=32, TA=8, TB=8, TH8=8, BQ=48, TT=8, KF=16, I3=8)),
                ("WA", dict(M0=32, BS0=32, AS=32, NS=16, SE=16, SF=16, FL0=32, FT0=32, PEN=48, NI=8, SV=16,
-                           G0=128, GT0=128, PB=48, A1=48, M1=48, BS1=48, SR1=48, SS1=48, G1=96, GT1=128, LF=16)),
-               ("WB", dict(LX=48, ZF=8, N1=32, N1B=32, N1T=32, T2N=32, N2=32, N2B=32, N2T=32))):
+                           G0=128, GT0=128, PB=48, A1=48, M1=48, BS1=48, SR1=48, SS1=48, G1=96, GT1=128, LF=16, IW=8, IV=8)),
+               ("WB", dict(LX=48, ZF=8, ZE=8, N1=32, N1B=32, N1T=32, T2N=32, N2=32, N2B=32, N2T=32))):
     _at = 0
     for _n, _w in _d.items():
         PIECE[_n] = (_b, _at, _w)
         _at += _w
     _sb(F, **{_b: _at})
 
-POOL = {"v": 47, "a": 44, "p": 18, "g": 12, "d": 16}
-SEMAPHORES = (["e1", "e2", "p1", "ms", "pa", "pb", "sent", "R0c", "R0s", "R1c", "R1s", "R2c", "R2s"]
+POOL = {"v": 47, "a": 42, "p": 18, "g": 11, "d": 16}
+SEMAPHORES = (["e1", "e2", "p1", "m0", "m1", "pa", "pb", "sent"] + ["R%d%s" % (j, x) for j in range(4) for x in "cs"]
               + ["x%s%d" % (q, i) for q, n in POOL.items() for i in range(n)])
 
 
@@ -109,13 +129,17 @@ def _inner(topo, cores, r):
     return [e for e in topo.engines(src, mate) if e not in topo.engines(src, far)]
 
 
+def _hand(inner, helpers):
+    return inner // min(helpers, 2)
+
+
 def _roots_at(r, k):
     return P * (r - (r > r ^ k))
 
 
-STAGES = (("R0", VIA0, "LC", _roots_at, P, "e2", True),
-          ("R1", VIA1, "C1", lambda r, k: OWN + K1 * k, K1, "p1", False),
-          ("R2", VIA2, "L2", lambda r, k: S * (r % 4), S, "pa", False))
+STAGES = ((("R0", VIA0, "LC", _roots_at, P, "e2", True),)
+          + tuple((buf, via, "C1", lambda r, k: OWN + K1 * k, K1, "p1", False) for _, via, buf, _ in GROUPS)
+          + (("R2", VIA2, "L2", lambda r, k: S * (r % 4), S, "pa", False),))
 
 
 def _helper(g, core, T, topo):
@@ -128,17 +152,103 @@ def _helper(g, core, T, topo):
                 continue
             ks = plan[core]
             off = topo.engines(core, cores[r ^ ks[0]])
+            n = len(off) // len(ks)
             for x in "cs":
-                src, dsts = T[buf + x][:], [T[land + x][:, at(r, k):at(r, k) + w] for k in ks]
-                if x == "c":
-                    src, dsts = src.bitcast(dt.uint8), [d.bitcast(dt.uint8) for d in dsts]
-                g.wait_ge(T.sem[buf + x], len(_inner(topo, cores, r)) // (2 if shared else len(plan)))
+                def view(name, a):
+                    v = T[name + x][:, a:a + w]
+                    return v.bitcast(dt.uint8) if x == "c" else v
+                g.wait_ge(T.sem[buf + x], _hand(len(_inner(topo, cores, r)), 2 if shared else len(plan)))
                 g.remote_dma_fused([RemoteDMATransfer(
-                    dst_ids=[_dst(topo, cores[r ^ k]) for k in ks], dma_engine_mask=_mask(off), remote_sem=T.sem[sem],
-                    srcs=[src], dsts=dsts)], local_sem=T.sem.sent)
+                    dst_ids=[_dst(topo, cores[r ^ k])], dma_engine_mask=_mask(off[n * i:n * (i + 1)]), remote_sem=T.sem[sem],
+                    srcs=[view(buf, 0 if shared else w * i)], dsts=[view(land, at(r, k))]) for i, k in enumerate(ks)],
+                    local_sem=T.sem.sent)
                 sent += len(off)
     if sent:
         g.wait_ge(T.sem.sent, sent)
+
+
+def _order(ops):
+    final = {b + x: sem for b, _, _, _, _, sem, _ in STAGES for x in "cs"}
+    first = [b for b, via, _, _, _, _, _ in STAGES if via][:1]
+    feeders, succ = {}, [[] for _ in ops]
+    for i, o in enumerate(ops):
+        for sem, _, busy, again in o["feeds"]:
+            feeders.setdefault(final.get(sem, sem), set()).add(i)
+
+    def hop(sem, again):
+        return (REMOTE + CALL + again + FIRST * (sem[:2] in first)) if sem in final else 0
+
+    def after(d):
+        return LOCAL + ops[d]["dma"] if ops[d]["dma"] else SLOW * ops[d]["cost"] + WAKE
+
+    need = []
+    for i, o in enumerate(ops):
+        fed = set(j for sem, _ in o["arrive"] for j in feeders.get(sem, ()))
+        need.append(o["deps"] | o["behind"] | fed)
+        for d in o["deps"]:
+            succ[d].append((i, after(d)))
+        for d in o["behind"]:
+            succ[d].append((i, SLOW * ops[d]["cost"]))
+        for d in fed:
+            succ[d].append((i, REMOTE + max(busy + hop(sem, again) for sem, _, busy, again in ops[d]["feeds"])))
+    way = [0.0] * len(ops)
+    for i in reversed(range(len(ops))):
+        way[i] = max([lat + way[j] for j, lat in succ[i]] + [after(i)]) + ops[i]["lift"]
+    start, free, engine, land, left, order = {}, {}, {}, {}, set(range(len(ops))), []
+    ready, called = {}, [False]
+    while left:
+        best = {}
+        for i in left:
+            o = ops[i]
+            if i not in ready:
+                if not all(d in start for d in need[i]):
+                    continue
+                ready[i] = max([0] + [start[d] + after(d) for d in o["deps"]] + [land.get(s, 0) for s, _ in o["arrive"]])
+            for q, cost in [(o["q"], o["cost"])] + ([(o["alt"][0], o["alt"][2])] if o["alt"] else []):
+                best.setdefault(q, []).append((max(ready[i], free.get(q, 0)), i, cost))
+        q = min(best, key=lambda q: (min(best[q])[0], q != "a"))
+        now = min(best[q])[0]
+        rank = {i: way[i] - (SPARE if q == "v" and ops[i]["alt"] else 0) for _, i, _ in best[q]}
+        cands = sorted(best[q], key=lambda c: -rank[c[1]])
+        for t, i, cost in cands:
+            if t > now + NEARLY:
+                continue
+            if any(rank[j] > rank[i] and t + SLOW * cost - u > YIELD and u - t < rank[j] - rank[i]
+                   and not ops[j]["alt"] for u, j, _ in cands if u > t):
+                continue
+            break
+        else:
+            t, i, cost = min(c for c in cands if c[0] > now + NEARLY)
+            free[q] = t - NEARLY
+            continue
+        o = ops[i]
+        if q != o["q"]:
+            o["q"], o["fn"], o["cost"] = o["alt"]
+        start[i] = t
+        free[q] = t + (cost if o["dma"] or o["feeds"] else SLOW * cost)
+        for sem, engines, busy, again in o["feeds"]:
+            at = t + REMOTE + FIRST * (not called[0])
+            for e in engines:
+                engine[e] = max(engine.get(e, 0), at) + busy
+            end = max(engine[e] for e in engines) + hop(sem, again)
+            land[final.get(sem, sem)] = max(land.get(final.get(sem, sem), 0), end)
+        called[0] = called[0] or bool(o["feeds"])
+        left.remove(i)
+        order.append(i)
+    at = {i: n for n, i in enumerate(order)}
+    return [dict(ops[i], deps=sorted((at[d] for d in ops[i]["deps"]), reverse=True)) for i in order]
+
+
+def _given(ops, order):
+    at = {abs(i): n for n, i in enumerate(order)}
+    assert len(at) == len(ops) and all(at[d] < at[i] for i, o in enumerate(ops) for d in o["deps"] | o["behind"])
+    out = []
+    for i in order:
+        o = dict(ops[abs(i)], deps=sorted((at[d] for d in ops[abs(i)]["deps"]), reverse=True))
+        if i < 0:
+            o["q"], o["fn"], o["cost"] = o["alt"]
+        out.append(o)
+    return out
 
 
 def rank_program(g, core, T, topo):
@@ -154,7 +264,7 @@ def rank_program(g, core, T, topo):
         buf, at, n = PIECE[name] if name in PIECE else (name, 0, SCRATCH[name][1][1])
         b = n if b is None else b
         cols = range(512) if SCRATCH[buf][0] == "psum" else range(at + a, at + b, step)
-        return (T[buf][p[0]:p[1], at + a:at + b:step], [(buf, p[0], p[1], frozenset(cols))])
+        return (T[buf][p[0]:p[1], at + a:at + b:step], [(buf, p[0], p[1], frozenset(cols))], len(range(a, b, step)))
 
     def c1(name, j=0):
         return R(name, j, j + 1)
@@ -163,18 +273,30 @@ def rank_program(g, core, T, topo):
         return (win[0].indirect(offs[0]), win[1] + offs[1], win[1], offs[1])
 
     def u8(v):
-        return (v[0].bitcast(dt.uint8), v[1])
+        return (v[0].bitcast(dt.uint8), v[1], v[2])
 
     def u32(v):
-        return (v[0].bitcast(dt.uint32), v[1])
+        return (v[0].bitcast(dt.uint32), v[1], v[2])
 
     def ap(x):
         return x[0] if isinstance(x, tuple) else x
 
-    ops, log = [], {}
+    ops, log, lift = [], {}, [0]
 
-    def op(q, fn, reads=(), writes=(), arrive=(), dma=False, acc=False, after=()):
-        i, deps = len(ops), set(after)
+    def size(v):
+        return 16 * len(v[3][0][3]) if len(v) == 4 else v[2]
+
+    def cycles(out, ins, per=None, fixed=50):
+        if len(out) == 4:
+            return fixed + 3.5 * CYC * size(out)
+        if len(ins[0]) == 4:
+            return fixed + 1.5 * CYC * size(ins[0])
+        if per is None:
+            per = 0.5 if all(SCRATCH[v[1][0][0]][2] in (BF, U16) for v in (out,) + ins) else 1
+        return CYC * max(64, per * size(out))
+
+    def op(q, fn, reads=(), writes=(), arrive=(), dma=0, acc=False, after=(), cost=0, alt=None, feeds=(), behind=()):
+        i, deps, behind = len(ops), set(after), set(behind)
         rd = [r for x in reads if isinstance(x, tuple) for r in x[1]]
         wr = []
         for x in writes:
@@ -190,6 +312,8 @@ def rank_program(g, core, T, topo):
                     if bank:
                         hit = ops[j]["q"] != q or (k != kind) or (k and not acc)
                         hit = hit and (ops[j]["q"] != q or (q0 < p1 and p0 < q1))
+                        if acc and not hit:
+                            behind.add(j)
                     else:
                         hit = (k or kind) and q0 < p1 and p0 < q1 and not cols.isdisjoint(cs)
                     if hit:
@@ -197,79 +321,94 @@ def rank_program(g, core, T, topo):
         for kind, regs in ((0, rd), (1, wr)):
             for buf, p0, p1, cols in regs:
                 log.setdefault(buf, []).append((i, kind, p0, p1, cols))
-        ops.append(dict(q=q, fn=fn, deps=sorted(deps, reverse=True), arrive=arrive, dma=dma))
+        ops.append(dict(q=q, fn=fn, deps=deps, behind=behind, arrive=arrive, dma=dma, cost=cost, alt=alt, feeds=feeds,
+                        lift=lift[0]))
+        lift[0] = 0
         return i
 
     def ts(out, in0, s1, s2, o0, o1=None, arrive=()):
-        if s2 is None:
-            op("v", lambda: V.tensor_scalar(out[0], in0[0], ap(s1), None, o0), (in0, s1), (out,), arrive)
-        else:
-            op("v", lambda: V.tensor_scalar(out[0], in0[0], ap(s1), ap(s2), o0, o1), (in0, s1, s2), (out,), arrive)
+        more = (None, o0) if s2 is None else (ap(s2), o0, o1)
+        op("v", lambda: V.tensor_scalar(out[0], in0[0], ap(s1), *more), (in0, s1, s2), (out,), arrive,
+           cost=cycles(out, (in0,)))
 
     def tt(out, in0, in1, o, arrive=()):
-        op("v", lambda: V.tensor_tensor(out[0], in0[0], in1[0], o), (in0, in1), (out,), arrive)
+        op("v", lambda: V.tensor_tensor(out[0], in0[0], in1[0], o), (in0, in1), (out,), arrive,
+           cost=cycles(out, (in0,), 1 if SCRATCH[in0[1][0][0]][0] == "psum" else 2))
 
     def cp(out, in_, arrive=()):
-        op("v", lambda: V.tensor_copy(out[0], in_[0]), (in_,), (out,), arrive)
+        op("v", lambda: V.tensor_copy(out[0], in_[0]), (in_,), (out,), arrive, cost=cycles(out, (in_,)))
 
     def ms(out, val):
-        op("v", lambda: V.memset(out[0], val), (), (out,))
+        op("v", lambda: V.memset(out[0], val), (), (out,), cost=cycles(out, (out,)))
 
     def scan(out, reset, data, o0=Op.mult, o1=Op.add):
-        op("v", lambda: V.tensor_tensor_scan(out[0], reset[0], data[0], 0.0, o0, o1), (reset, data), (out,))
+        op("v", lambda: V.tensor_tensor_scan(out[0], reset[0], data[0], 0.0, o0, o1), (reset, data), (out,),
+           cost=cycles(out, (reset, data)))
 
     def tr(out, in_):
-        op("v", lambda: V.transpose(out[0], in_[0]), (in_,), (out,))
+        op("v", lambda: V.transpose(out[0], in_[0]), (in_,), (out,), cost=cycles(out, (in_,)))
 
     def act(out, in_, func=Act.Identity, arrive=(), acc=None, **kw):
         args = {k: ap(v) for k, v in kw.items()}
         if acc is not None:
             args["accum_out"] = acc[0]
         op("a", lambda: A.activation(out[0], in_[0], func, **args), (in_,) + tuple(kw.values()),
-           (out,) if acc is None else (out, acc), arrive)
+           (out,) if acc is None else (out, acc), arrive, cost=cycles(out, (in_,), 1, 65) + (acc is not None) * 20)
+
+    def lin(out, in_, scale=1.0, bias=0.0, arrive=(), q=None):
+        if scale == 1.0:
+            fv = (lambda: V.tensor_scalar(out[0], in_[0], ap(bias), None, Op.add)) if bias != 0.0 else (
+                lambda: V.tensor_copy(out[0], in_[0]))
+        else:
+            fv = lambda: V.tensor_scalar(out[0], in_[0], scale, ap(bias), Op.mult, Op.add)
+        fa = (lambda: A.activation(out[0], in_[0], Act.Identity, bias=ap(bias), scale=scale)) if bias != 0.0 else (
+            lambda: A.activation(out[0], in_[0], Act.Copy, scale=scale))
+        a = ("a", fa, cycles(out, (in_,), 1, 65))
+        if q == "a":
+            op("a", fa, (in_, bias), (out,), arrive, cost=a[2])
+        else:
+            op("v", fv, (in_, bias), (out,), arrive, cost=cycles(out, (in_,)), alt=None if q else a)
 
     def fill(out, n, val):
-        act(out, R("JB", 0, n), scale=0.0, bias=val)
+        lin(out, R("JB", 0, n), 0.0, val)
 
     def quant(name, a, b, tile, at=None):
         at = 4 * a if at is None else at
         o, s, i = R(name + "c", a, b), R(name + "s", a, b), R(tile, at, at + 4 * (b - a))
-        op("v", lambda: V.quantize_mx(o[0], s[0], i[0]), (i,), (o, s))
+        op("v", lambda: V.quantize_mx(o[0], s[0], i[0]), (i,), (o, s), cost=12 + 0.88 * (b - a))
 
     def mm(bank, lhs, la, rhs, a, b, start=True, stop=True, arrive=()):
         v = (R(lhs + "c", la, la + 128), R(lhs + "s", la, la + 128), R(rhs + "c", a, b), R(rhs + "s", a, b))
         o = R(bank, 0, b - a)
         op("p", lambda: PE.matmul_mx(o[0], v[0][0], v[1][0], v[2][0], v[3][0], start, stop), v, (o,), arrive,
-           acc=not start)
+           acc=not start, cost=PEC * (b - a + 16))
 
-    def pickc(dst, a, b, src, offs, win=(0, None), arrive=()):
+    def pick(dst, a, b, src, offs, win=(0, None), arrive=()):
         cp(u32(R(dst + "c", a, b)), by(u32(R(src + "c", *win)), offs), arrive)
-
-    def picks(dst, a, b, src, offs, win=(0, None), arrive=()):
         act(R(dst + "s", a, b), by(R(src + "s", *win), offs), Act.Copy, arrive)
 
-    def pick(*a, **kw):
-        pickc(*a, **kw)
-        picks(*a, **kw)
+    def width(v):
+        return v[2] * {BF: 2, SC: 1}.get(SCRATCH[v[1][0][0]][2], 4)
 
     def dma(q, out, in_, arrive=()):
         return op(q, lambda: queues[q].dma_start(ap(out), ap(in_)), (in_,), (out,) if isinstance(out, tuple) else (),
-                  arrive, dma=True)
+                  arrive, dma=8 * (ROW + width(out if isinstance(out, tuple) else in_) / RATE), cost=ISSUE)
 
     def iota(out, pattern, base=0, cm=0, whole=False):
-        if whole:
-            op("g", lambda: g.iota(out[0], pattern, base, cm), (), (out,))
-        else:
-            op("g", lambda: g.iota(out[0], pattern, base, cm, allow_small_or_imprecise_dtypes=True), (), (out,))
+        kw = {} if whole else dict(allow_small_or_imprecise_dtypes=True)
+        op("g", lambda: g.iota(out[0], pattern, base, cm, **kw), (), (out,), cost=130 + 2 * CYC * size(out),
+           behind=calls[-1:])
 
-    sent = [0]
+    sent, calls = [0], []
 
     def remote(transfers):
         sent[0] += sum(len(t[2]) for t in transfers)
-        op("g", lambda: g.remote_dma_fused([RemoteDMATransfer(
+        calls.append(op("g", lambda: g.remote_dma_fused([RemoteDMATransfer(
             dst_ids=[_dst(topo, c) for c, _ in d], dma_engine_mask=_mask(e), remote_sem=T.sem[sem],
             srcs=[s[0]], dsts=[x[0] for _, x in d]) for s, d, e, sem in transfers], local_sem=T.sem.sent),
-           [t[0] for t in transfers])
+            [t[0] for t in transfers], cost=CALL, behind=calls[-1:],
+            feeds=[(sem, e, len(d) * 128 // len(e) * (ROW + width(s) / RATE), 16 * (ROW + width(s) / RATE))
+                   for s, d, e, sem in transfers]))
 
     def direct(src, dst, cast, w, frm, to, ks, sem):
         remote([(cast(R(src, frm(k), frm(k) + w)), [(cores[me ^ k], cast(R(dst, to(k), to(k) + w)))], e, sem)
@@ -283,26 +422,17 @@ def rank_program(g, core, T, topo):
 
     both = (("c", u8), ("s", same))
 
-    def spread(name, base, w, on="va", step=1):
-        def mv(q, po, pi, n, a, b):
+    def spread(name, base, w, step):
+        for po, pi, n, a, b in ((0, 32, 32, 1, 2), (64, 96, 32, 3, 4), (32, 0, 32, 0, 1), (96, 64, 32, 2, 3),
+                                (64, 0, 64, 0, 2), (0, 64, 64, 2, 4)):
             a, b = base + w * a, base - base % step + w * b
-            o, i = R(name, a, b, step, (po, po + n)), R(name, a, b, step, (pi, pi + n))
-            if q == "v":
-                cp(o, i)
-            else:
-                act(o, i, Act.Copy)
-        return [lambda: mv(on[0], 0, 32, 32, 1, 2), lambda: mv(on[1], 64, 96, 32, 3, 4),
-                lambda: mv(on[0], 32, 0, 32, 0, 1), lambda: mv(on[1], 96, 64, 32, 2, 3),
-                lambda: mv(on[0], 64, 0, 64, 0, 2), lambda: mv(on[1], 0, 64, 64, 2, 4)]
-
-    def run(calls):
-        for c in calls:
-            c()
+            lin(R(name, a, b, step, (po, po + n)), R(name, a, b, step, (pi, pi + n)))
 
     cg, ca, c4, cs, ck, ch, c2 = (c1("CF", j) for j in range(7))
-    cPN, cOA, cBG, c64, cLM, cB, cPS, cZ, cF, cX = (c1("CD", j) for j in range(10))
-    oWQ, oV0, oWM, oG, oPN, oSV, oF, oU1, oU, oU0, oUS, oLQ = (R("OU", a, b) for a, b in (
-        (0, 8), (8, 16), (16, 24), (24, 30), (30, 33), (34, 35), (36, 38), (38, 40), (40, 42), (40, 41), (40, 43), (44, 46)))
+    cPN, cOA, cBG, c64, cLM, cB, cPS, cZ, cF, cX, cO2, cL2 = (c1("CD", j) for j in range(12))
+    oWQ, oV0, oWM, oG, oPN, oSV, oF, oU, oU0, oUS, oLQ = (R("OU", a, b) for a, b in (
+        (0, 8), (8, 16), (16, 24), (24, 30), (30, 33), (34, 35), (36, 38), (38, 40), (38, 39), (38, 41), (42, 44)))
+    oU1 = R("OU", 44, 46) if MERGE else oU
 
     def JB(n):
         return R("JB", 0, n)
@@ -310,40 +440,38 @@ def rank_program(g, core, T, topo):
     def quad(name, q, a, b):
         return R(name, a, b, 1, (32 * q, 32 * q + 32))
 
-    def shifted(q, out, in_, h):
-        if q == "v":
-            ts(out, in_, h, None, Op.add)
-        else:
-            act(out, in_, bias=h)
+    def shift(k, b):
+        return c1("DH", 8 * b + k) if k else c1("A0", AW * b + K1)
 
     def made(k):
         return K1 * XA.index(k) if k else OWN
 
-    def child(q, k, b):
-        shifted(q, R("X1", 4 * made(k) + b, 4 * (made(k) + K1), 4), R("A0", AW * b, AW * b + K1),
-                c1("DH", 8 * b + k) if k else c1("A0", AW * b + K1))
+    def children(k):
+        for b in range(4):
+            lin(R("X1", 4 * made(k) + b, 4 * (made(k) + K1), 4), R("A0", AW * b, AW * b + K1), bias=shift(k, b))
 
     dma("s", R("T0", 0, 4 * P), T.r0[:])
     dma("a", R("T0", 4 * UQ), T.u[:, 0:8])
     dma("s", R("T1", 0, 4 * K1), T.r1[:])
+    lift[0] = 9000
     dma("s", R("T2"), T.r2[:])
     iota(c1("PI"), [[0, 1]], 0, 1, True)
     iota(R("JB"), [[1, 128]])
     for j in (1, 2):
         iota(c1("PI", j), [[0, 1]], 0, 4 ** j, True)
     iota(R("JM"), [[0, 3], [1, 16]])
-    iota(R("TB1"), [[-16, 3], [1, 48]])
+    iota(R("TB1"), [[-16, 3], [1, 50]])
     ms(R("T0", 4 * P, 4 * UQ), 0.0)
     ms(R("TE"), 0.0)
     cp(R("CP"), c1("PI"))
     ms(R("T1", 4 * K1), 0.0)
     ts(R("TE", 3, 515, 4), R("JB"), R("CP"), None, Op.is_equal)
     ms(R("X1", 4 * LZ, 4 * OWN), 0.0)
-    quant("QE", 0, 128, "TE", 3)
     for a, b, v, m in ((0, 2, R("PI", 0, 3, 2), 15), (2, 5, R("PI", 0, 3), 3), (5, 7, R("PI", 0, 2), 1)):
         ts(R("CI", a, b), v, 4, m, Op.logical_shift_right, Op.bitwise_and)
     cp(R("CF", 0, 7), R("CI", 0, 7))
-    quant("QE", 128, 256, "TE", 2)
+    for b in range(4):
+        quant("QE", 128 * b, 128 * (b + 1), "TE", 3 - b)
     quant("Q0", 0, 128, "T0")
 
     eng = _share(topo, cores, me, range(N))
@@ -361,233 +489,225 @@ def rank_program(g, core, T, topo):
         src = cast(R("Q0" + x, 0, P))
         land = {k: (cores[me ^ k], cast(R("LC" + x, _roots_at(me, k), _roots_at(me, k) + P))) for k in eng}
         remote([(src, [land[k] for k in far if k not in VIA0], off, "e2")]
-               + [(src, [land[k]], on[0:3:2], "e2") for k in near]
-               + [(src, [(h, cast(R("R0" + x))) for h in _relay(topo, cores, me, VIA0)], on[half:], "R0" + x)][:len(VIA0)])
-    E2 = (("e2", 2 * (len(far) * len(off) + 2 * len(near))),)
+               + [(src, [land[k]], on[0:NEAR], "e2") for k in near]
+               + [(src, [(h, cast(R("R0" + x))) for h in _relay(topo, cores, me, VIA0)][::-1], on[half:], "R0" + x)][:len(VIA0)])
 
-    def relay(src, buf, via, w, frm):
+    def handed(via):
+        return sum(len(off) // len(ks) for k in via for ks in _relay(topo, cores, me ^ k, via).values() if k in ks)
+
+    E2 = (("e2", 2 * ((len(far) - len(VIA0)) * len(off) + handed(VIA0) + NEAR * len(near))),)
+
+    def relay(src, buf, via, w, frm, beside=()):
         plan = _relay(topo, cores, me, via)
-        n = len(on) // len(plan)
+        n = _hand(len(on), len(plan))
         for x, cast in both:
-            remote([(cast(R(src + x, frm(ks[0]), frm(ks[0]) + w)), [(h, cast(R(buf + x)))], on[n * i:n * (i + 1)], buf + x)
-                    for i, (h, ks) in enumerate(plan.items())])
+            remote([(cast(R(src + x, frm(ks[0]), frm(ks[0]) + w * len(ks))), [(h, cast(R(buf + x, 0, w * len(ks))))],
+                     (on + off)[n * i:n * (i + 1)], buf + x) for i, (h, ks) in enumerate(plan.items())]
+                   + [(cast(R(src + x, frm(k), frm(k) + w)), [(cores[me ^ k], cast(R(dst + x, at, at + w)))], off, sem)
+                      for k, dst, at, sem in beside])
 
     iota(R("NT"), [[0, 2], [1, K1]])
     iota(R("KF"), [[0, 16]], OWN)
     iota(R("X2", 4 * HH, 4 * (HH + 16)), [[0, 64]])
-    iota(R("KF", 3, 12), [[K1, 3], [0, 3]], made(1))
+    iota(R("KF", 3, 6), [[0, 3]], made(1))
+    iota(R("KF", 6, 12), [[K1, 2], [0, 3]], made(2))
     iota(R("X2", 4 * (HA + HH)), [[0, 16]])
     iota(R("JQ"), [[0, 8], [1, 4], [0, 4]])
-    dma("s", R("TW"), T.w[:], E1)
-    fill(R("OF", 14, 16), 2, float(UQ + 1))
-    act(R("OF", 0, 8), JB(8), scale=2.0, bias=float(UQ))
-    fill(R("OF", 16, 24), 8, float(UQ))
-    fill(R("RR", 0, 128), 128, 1.0)
-    fill(R("RR", 128, 144), 16, 1.0)
-    act(R("OF", 8, 14), JB(6), scale=4.0, bias=cs)
-    act(cX, ca, scale=4.0 / 3, bias=2.0 / 3)
-    act(cBG, ca, Act.Relu, scale=BIG, bias=-7 * BIG)
-    fill(R("RR", 0, 144, 48), 3, 0.0)
-    act(R("TT", 0, 2), JB(2), scale=64.0 / 3, bias=cX)
-    act(c1("CM0", 48), ca, Act.Relu, scale=24.0, bias=-168.0)
-    act(cB, cg, scale=float(K1), bias=float(ZC))
-    act(cOA, ch, scale=float(K1), bias=ck)
-    quant("QE", 256, 384, "TE", 1)
-    cp(R("OU", 0, 24), R("OF", 0, 24))
-    quant("Q1", 0, 128, "T1")
-    pick("V0", 0, 128, "Q0", oV0, (0, 128))
-    quant("QE", 384, 512, "TE", 0)
-    for b in range(4):
-        mm("P%d" % b, "QE", 128 * b, "V0", 0, 128, True, False)
-        mm("P%d" % b, "QE", 128 * b, "Q1", 0, 128, False, True)
-    ts(R("TH1"), R("TB1"), ca, -EPS, Op.is_lt, Op.mult)
-    cp(R("KI"), R("TT", 0, 2))
-    ts(R("DM"), R("JM"), ca, None, Op.is_equal)
-    ts(R("TT", 4, 6), R("KI"), 31.0, 2.0, Op.min, Op.mult)
-    ts(R("MK", 0, 12), R("JM", 0, 48, 4), 0.25, cs, Op.mult, Op.is_equal)
-    act(R("PY0"), JB(32), scale=4.0, bias=cB)
-    act(cOA, cB, scale=-1.0, bias=cOA)
-    act(cPN, ch, scale=16.0, bias=cs)
-    act(cF, c2, scale=16.0, bias=15.0)
-    small = [lambda: act(R("TH0", 0, P), R("TH1", 0, P), Act.Copy),
-             lambda: act(R("TH0", P, 2 * P), R("TH1", 48, 48 + P), bias=cBG),
-             lambda: act(R("MX"), R("DM", 0, 16), scale=-2 * HUGE, bias=HUGE),
-             lambda: act(R("OF", 24, 30, 2), JB(3), scale=4.0, bias=cs),
-             lambda: act(R("OF", 25, 30, 2), JB(3), scale=4.0, bias=cs),
-             lambda: act(R("OF", 30, 34), JB(4), scale=4.0, bias=cPN)]
-    for b in range(4):
-        act(R("A0", AW * b, AW * b + K1 + 1), R("P%d" % b, 0, K1 + 1), Act.Copy)
-        run(small[2 * b:2 * b + 2])
-    for b in range(4):
-        child(OWNQ[b], 0, b)
-    quant("Q2", 0, NP, "T2")
-    act(R("OF", 34, 36), R("CF", 5, 7), scale=16.0, bias=ca)
-    act(c1("OF", 36), ck, scale=32.0, bias=cF)
-    act(c1("OF", 37), ck, scale=32.0, bias=cF)
-    act(R("OF", 38, 40), R("TT", 4, 6), bias=1.0)
-    act(R("OF", 40, 42), R("TT", 4, 6), Act.Copy)
-    act(R("OF", 42, 44), R("CF", 0, 2), Act.Copy, scale=8.0)
-    act(R("OF", 44, 46), R("TT", 4, 6), scale=2.0, bias=-1.0)
-    act(c64, ca, scale=-1.0, bias=float(M))
-    act(cLM, ca, Act.Relu, scale=100.0, bias=-100.0 * (CAP - 1))
-    quant("C1", LZ, LZ + 128, "X1")
-    cp(R("OU", 24, 46), R("OF", 24, 46))
-    act(cLM, cLM, scale=-1.0, bias=c64)
-    act(R("DN"), R("DM"), Act.Copy, scale=-1.0)
-    fill(R("LM"), 32, cLM)
-    ha, hb = ((me ^ k0) // 4 for k0, _ in PARTS)
-    s0, s1 = 1 - 2 * (me & 1), 1 - (me & 2)
-    pa, pb = ((64 * h, 64 * h + 64) for h in (ha, hb))
-    late = [
-        lambda: act(R("CD", 6, 7, 1, pa), R("CF", 2, 3, 1, pa), scale=-float(S), bias=float(HH)),
-        lambda: act(R("CD", 6, 7, 1, pb), R("CF", 2, 3, 1, pb), scale=float(S * s1), bias=float(S * (1 + me % 4))),
-        lambda: act(cZ, ck, bias=float(HH)),
-        lambda: act(R("CD", 6, 7, 1, pb), R("CF", 5, 6, 1, pb), scale=float(S * (s0 - s1)), bias=R("CD", 6, 7, 1, pb)),
-        lambda: act(c1("PS"), ca, scale=-4.0, bias=cPS)]
-    gaps = [lambda: ts(R("TA"), JB(8), cg, -EPS, Op.is_lt, Op.mult),
-            lambda: ts(R("TB"), JB(8), cg, 4 * BIG, Op.is_equal, Op.mult),
-            lambda: ts(R("LMM"), R("JQ"), ck, cLM, Op.is_equal, Op.mult),
-            lambda: tt(R("TH8"), R("TA"), R("TB"), Op.add)]
-
-    pick("WQ", 0, 128, "Q0", oWQ, (0, NL), E1)
-    for b in range(3):
-        mm("P%d" % b, "QE", 128 * b, "Q0", NL - 128, NL, arrive=E1)
-    mm("P4", "WQ", 0, "Q0", 0, 128)
-    mm("P3", "QE", 128 * 3, "Q0", NL - 128, NL)
-    mm("P7", "WQ", 0, "C1", LZ, LZ + 128)
-    for b in range(4):
-        act(R("DH", 8 * b + 1, 8 * b + 8), R("P%d" % b, 128 - 2 * N + 3, 128, 2), Act.Copy)
-    xs = [(k, b) for k in XA for b in range(4)]
-    xv = [xs[i] for i in XV]
-    for k, b in xs:
-        if (k, b) not in xv:
-            child("a", k, b)
-
-    def more(n=1):
-        for _ in range(n):
-            if xv:
-                child("v", *xv.pop(0))
-
-    def group(ks, bank):
-        while any(k in ks for k, _ in xv):
-            more()
-        a, b = made(ks[0]), made(ks[-1]) + K1
-        quant("C1", a, b, "X1")
-        return lambda: mm(bank, "WQ", 0, "C1", a, b)
-
-    got = [len(VIA1) * len(off)]
-
-    def send(ks):
-        if ks[0] in VIA1:
-            return relay("C1", "R1", VIA1, K1, made)
-        for x, cast in both:
-            direct("C1" + x, "C1" + x, cast, K1, made, lambda k: OWN + K1 * k, ks, "p1")
-        got.append(landed(ks))
-
-    tt(R("M0"), R("P4", 0, 32), R("DM", 0, 32), Op.mult)
-    cp(R("AS"), R("P4", 0, 32))
-    scan(R("BS0"), R("RR", 0, 96, 3), R("M0"))
-    more()
-    for s in range(2):
-        ts(R("D0", P * s, P * s + P), R("AS", 0, P), c1("BS0", 16 * s + 15), None, Op.subtract)
-    more()
-    tt(R("CM0", 0, 48), R("D0"), R("TH0"), Op.is_gt)
-    more()
-    scan(R("SN0", 0, 49), R("RR", 24, 73), R("CM0", 0, 49))
-    more()
-    cp(R("OL0"), R("SN0", 23, 49, 25))
-    group(XA[:2], "P5")()
-    send(XA[:2])
-    cp(by(R("SS0"), R("OL0")), R("AS"))
-    cp(by(R("SR0"), R("OL0")), R("PY0"))
-    scan(R("NS"), R("MX"), R("SS0", 0, 16), Op.min, Op.max)
-    tt(R("SE", 0, 12), R("SR0", 0, 12), R("MK", 0, 12), Op.mult)
-    more()
-    scan(R("SF", 0, 12), R("RR", 0, 144, 12), R("SE", 0, 12))
-    more()
-    ts(R("OA", 0, 3), R("SF", 3, 12, 4), cOA, None, Op.add)
-    later = group(XA[2:5], "P6")
-    send(XA[2:4])
-    mm("P3", "WQ", 0, "LC", 0, NO, arrive=E2)
-    later()
-    more(9)
-    for a, b, o in ((0, P * me, Op.is_ge), (P * me, NO, Op.is_gt)):
-        if a < b:
-            ts(R("CG", a, b), R("P3", a, b), c1("NS", 15), None, o)
-    group(XA[5:], "P0")()
-    send(XA[4:])
     iota(R("BQ", P), [[0, P]])
     for m in range(3):
         iota(R("BQ", m, P, 3), [[K1 * (1 - 2 * (me >> i & 1)) << i, 2] for i in (2, 1, 0)], ZC + K1 * me)
     iota(R("R4"), [[0, 32], [256, 4]])
-    scan(R("CH"), R("CG"), R("CG"), Op.add, Op.max)
-    P1 = (("p1", 2 * sum(got)),)
-    act(quad("AF", 0, 0, K1), quad("P7", 0, ZC, 128), Act.Copy)
-    act(quad("AF", XA[0] // 2, 0, 192), quad("P5", XA[0] // 2, 0, 192), Act.Copy)
-    act(quad("AF", XA[2] // 2, 0, 192), quad("P6", XA[2] // 2, 0, 192), Act.Copy)
-    act(quad("AF", 0, K1, 192), quad("P6", 0, 192, 192 + K1), Act.Copy)
-    act(quad("AF", 1, 0, 192), quad("P0", 1, 0, 192), Act.Copy)
-    ts(R("FL0"), R("LM"), c1("CH", NO - 1), None, Op.is_gt)
-    gaps[0]()
-    tr(R("FT0"), R("FL0"))
-    gaps[1]()
-    ts(R("PEN"), by(R("FT0"), oPN), -1.0, BIG, Op.add, Op.mult)
+    dma("s", R("TW"), T.w[:], E1)
+    fill(R("OF", 14, 16), 2, float(UQ + 1))
+    lin(R("OF", 0, 8), JB(8), 2.0, float(UQ))
+    fill(R("OF", 16, 24), 8, float(UQ))
+    lin(R("OF", 8, 14), JB(6), 4.0, cs)
+    cp(R("OU", 0, 24), R("OF", 0, 24))
+    fill(R("RR", 0, 128), 128, 1.0)
+    fill(R("RR", 128, 144), 16, 1.0)
+    fill(R("RR", 0, 144, 48), 3, 0.0)
+    lin(cX, ca, 4.0 / 3, 2.0 / 3)
+    lin(R("TT", 0, 2), JB(2), 64.0 / 3, cX)
+    cp(R("KI"), R("TT", 0, 2))
+    ts(R("OF", 38, 40), R("KI"), 31.0, 1.0 + MERGE, Op.min, Op.mult)
+    act(cBG, ca, Act.Relu, scale=BIG, bias=-7 * BIG)
+    act(c1("CM0", 48), ca, Act.Relu, scale=24.0, bias=-168.0)
+    lin(cB, cg, float(K1), float(ZC))
+    lin(cO2, ch, float(K1), ck)
+    lin(cOA, cB, -1.0, cO2)
+    quant("Q1", 0, 128, "T1")
+    pick("V0", 0, 128, "Q0", oV0, (0, 128))
+    for b in range(4):
+        mm("P%d" % b, "QE", 128 * b, "V0", 0, 128, True, False)
+        mm("P%d" % b, "QE", 128 * b, "Q1", 0, 128, False, True)
+    for b in range(4):
+        lin(R("A0", AW * b, AW * b + K1 + 1), R("P%d" % b, 0, K1 + 1), q="a")
+    children(0)
+    quant("C1", LZ, LZ + 128, "X1")
+    for a in range(0, NP, 128):
+        quant("Q2", a, a + 128, "T2")
+    quant("QW", 0, 128, "TW")
+    pick("WM", 0, 128, "Q0", oWM, (0, 128))
+    ts(R("TH1"), R("TB1", 0, 74), ca, -EPS, Op.is_lt, Op.mult)
+    ts(R("DM"), R("JM"), ca, None, Op.is_equal)
+    ts(R("MK", 0, 12), R("JM", 0, 48, 4), 0.25, cs, Op.mult, Op.is_equal)
+    ts(R("FM"), R("TB1"), ca, 2.0, Op.not_equal, Op.mult)
+    lin(R("FM"), R("FM"), bias=-1.0)
+    fill(R("FM", 0, 150, 50), 3, 0.0)
+    fill(R("EQ", 49, 150, 50), 3, -float(S))
+    lin(R("I3", 0, 3), JB(3), 16.0, ca)
+    lin(R("I3", 4, 7), R("I3", 0, 3), 2.0, -float(S))
+    lin(R("PY0"), JB(32), 4.0, cB)
+    lin(cPN, ch, 16.0, cs)
+    lin(cF, c2, 16.0, 15.0)
+    lin(R("TH0", 0, P), R("TH1", 0, P))
+    lin(R("TH0", P, 2 * P), R("TH1", 50, 50 + P), bias=cBG)
+    lin(R("MX"), R("DM", 0, 16), -2 * HUGE, HUGE)
+    lin(R("OF", 24, 30, 2), JB(3), 4.0, cs)
+    lin(R("OF", 25, 30, 2), JB(3), 4.0, cs)
+    lin(R("OF", 30, 34), JB(4), 4.0, cPN)
+    lin(R("OF", 34, 36), R("CF", 5, 7), 16.0, ca)
+    lin(c1("OF", 36), ck, 32.0, cF)
+    lin(c1("OF", 37), ck, 32.0, cF)
+    lin(R("OF", 40, 42), R("CF", 0, 2), 4.0 * (1 + MERGE))
+    lin(R("OF", 42, 44), R("OF", 38, 40), 4.0 / (1 + MERGE), -1.0)
+    if MERGE:
+        lin(R("OF", 44, 46), R("OF", 38, 40), bias=1.0)
+    cp(R("OU", 24, 44 + 2 * MERGE), R("OF", 24, 44 + 2 * MERGE))
+    lin(c64, ca, -1.0, M - 0.5)
+    act(cL2, ca, Act.Relu, scale=100.0, bias=-100.0 * (CAP - 1))
+    lin(cLM, cL2, -1.0, c64)
+    fill(R("LM"), 32, cLM)
+    ts(R("LMM"), R("JQ"), ck, cLM, Op.is_equal, Op.mult)
+    ts(R("TA"), JB(8), cg, -EPS, Op.is_lt, Op.mult)
+    ts(R("TB"), JB(8), cg, 4 * BIG, Op.is_equal, Op.mult)
+    tt(R("TH8"), R("TA"), R("TB"), Op.add)
+    ha, hb = ((me ^ k0) // 4 for k0, _ in PARTS)
+    s0, s1 = 1 - 2 * (me & 1), 1 - (me & 2)
+    pa, pb = ((64 * h, 64 * h + 64) for h in (ha, hb))
+    lin(R("CD", 6, 7, 1, pa), R("CF", 2, 3, 1, pa), -float(S), float(HH))
+    lin(R("CD", 12, 13, 1, pb), R("CF", 2, 3, 1, pb), float(S * s1), float(S * (1 + me % 4)))
+    lin(R("CD", 6, 7, 1, pb), R("CF", 5, 6, 1, pb), float(S * (s0 - s1)), R("CD", 12, 13, 1, pb))
+    lin(c1("PS"), ca, -4.0, cPS)
+    lin(cZ, ck, bias=float(HH))
 
-    tt(R("SV"), by(R("FT0"), oSV), R("SR0", 0, 16), Op.mult)
-    tt(R("A1"), by(R("AF"), R("OA", 0, 3)), R("PEN"), Op.add)
-    act(R("JK"), R("PEN"), Act.Copy, scale=1.0 / BIG, acc=c1("NI"))
-    act(R("G0", 32, 128), by(R("SV"), oG), Act.Copy)
-    gaps[2]()
-    tt(R("M1"), R("A1"), R("DN"), Op.mult)
-    gaps[3]()
-    scan(R("BS1"), R("RR", 0, 144, 3), R("M1"))
-    fill(R("G0", 0, 32), 32, c1("NI"))
+    pick("WQ", 0, 128, "Q0", oWQ, (0, NL), E1)
+    for b in range(4):
+        mm("P%d" % b, "QE", 128 * b, "Q0", NL - 128, NL, arrive=E1)
+    mm("P4", "WQ", 0, "Q0", 0, 128)
+    mm("P7", "WQ", 0, "C1", LZ, LZ + 128)
+    lin(quad("AF", 0, 0, K1), quad("P7", 0, ZC, 128), q="a")
+    for b in range(4):
+        lin(R("DH", 8 * b + 1, 8 * b + 8), R("P%d" % b, 128 - 2 * N + 3, 128, 2), q=DHQ[b])
+    got = []
+    for (ks, via, buf, sends), bank in zip(GROUPS, ("P5", "P6", "P0")):
+        for k in ks:
+            children(k)
+        a, b = made(ks[0]), made(ks[-1]) + K1
+        quant("C1", a, b, "X1")
+        mm(bank, "WQ", 0, "C1", a, b)
+        for q in sorted(set(k // 2 for k in ks)):
+            in_q = [k for k in ks if k // 2 == q]
+            lin(quad("AF", q, K1 * (in_q[0] % 2), K1 * (in_q[-1] % 2 + 1)),
+                quad(bank, q, made(in_q[0]) - a, made(in_q[-1]) + K1 - a), q="a")
+        if via:
+            relay("C1", buf, via, K1, made, [(k, "C1", OWN + K1 * k, "p1") for k in sends])
+            got.append(handed(via) + len(off) * len(sends))
+            continue
+        for x, cast in both:
+            direct("C1" + x, "C1" + x, cast, K1, made, lambda k: OWN + K1 * k, sends, "p1")
+        got.append(landed(sends))
+    P1 = (("p1", 2 * sum(got)),)
+    tt(R("M0"), R("P4", 0, 32), R("DM", 0, 32), Op.mult)
+    cp(R("AS"), R("P4", 0, 32))
+    scan(R("BS0"), R("RR", 0, 96, 3), R("M0"))
     for s in range(2):
-        act(R("D1", 48 * s, 48 * s + 48), R("A1"), bias=c1("BS1", 16 * s + 15))
-    ts(R("D1", 96, 144), R("A1"), c1("BS1", 47), None, Op.add)
-    tr(R("GT0"), R("G0"))
-    act(R("PB"), by(R("NT"), R("OA", 0, 3)), Act.Copy)
-    tt(R("CM1"), R("D1"), R("TH1"), Op.is_gt)
-    act(R("MS", 1, 64, 2), by(R("GT0"), oF), Act.Copy)
-    scan(R("SN1"), R("RR"), R("CM1"))
-    run(spread("MS", 1, 16, "aa", 2))
-    cp(R("OL1", 0, 3), R("SN1", 47, 144, 48))
+        ts(R("D0", P * s, P * s + P), R("AS", 0, P), c1("BS0", 16 * s + 15), None, Op.subtract)
+    tt(R("CM0", 0, 48), R("D0"), R("TH0"), Op.is_gt)
+    scan(R("SN0", 0, 49), R("RR", 24, 73), R("CM0", 0, 49))
+    cp(R("OL0"), R("SN0", 23, 49, 25))
+    cp(by(R("SS0"), R("OL0")), R("AS"))
+    cp(by(R("SR0"), R("OL0")), R("PY0"))
+    scan(R("NS"), R("MX"), R("SS0", 0, 16), Op.min, Op.max)
+    tt(R("SE", 0, 12), R("SR0", 0, 12), R("MK", 0, 12), Op.mult)
+    scan(R("SF", 0, 12), R("RR", 0, 144, 12), R("SE", 0, 12))
+    ts(R("OA", 0, 3), R("SF", 3, 12, 4), cOA, None, Op.add)
+    mm("P3", "WQ", 0, "LC", 0, NO, arrive=E2)
+    for a, b, o in ((0, P * me, Op.is_ge), (P * me, NO, Op.is_gt)):
+        if a < b:
+            ts(R("CG", a, b), R("P3", a, b), c1("NS", 15), None, o)
+        else:
+            op("v", None)
+    scan(R("CH"), R("CG"), R("CG"), Op.add, Op.max)
+    ts(R("FL0"), R("LM"), c1("CH", NO - 1), 2 * BIG, Op.subtract, Op.mult)
+    tr(R("FT0"), R("FL0"))
+
+    lin(R("PEN"), by(R("AF"), R("OA", 0, 3)))
+    tt(R("A1"), by(R("FT0"), oPN), R("PEN"), Op.min)
+    tt(R("M1"), R("PEN"), R("DM"), Op.mult)
+    scan(R("BS1"), R("RR", 0, 144, 3), R("M1"))
+    act(R("JK"), by(R("FT0"), oPN), Act.Sign, acc=c1("NI"))
+    ts(R("IW", 0, 3), R("I3", 4, 7), c1("NI"), None, Op.is_ge)
+    tt(R("IV", 0, 3), R("IW", 0, 3), R("I3", 0, 3), Op.mult)
+    for s in range(3):
+        own = c1("BS1", 16 * s + 15)
+        act(R("D1", 48 * s, 48 * s + 48), R("A1"), Act.Sign, scale=-1.0, bias=own, acc=c1("EQ", 50 * s + 48))
+        ts(R("EQ", 50 * s, 50 * s + 48), R("A1"), own, None, Op.is_equal)
+    scan(R("SN1"), R("FM"), R("EQ"))
+    for s in range(3):
+        ts(c1("OL1", s), c1("SN1", 50 * s + 49), -0.5, c1("IV", s), Op.mult, Op.max)
+    lin(R("PB"), by(R("NT"), R("OA", 0, 3)))
     cp(by(R("SR1"), R("OL1", 0, 3)), R("PB"))
     cp(by(R("SS1"), R("OL1", 0, 3)), R("A1"))
-    act(R("G1"), by(R("SR1"), oG), Act.Copy)
-    run(late)
+    tt(R("SV"), by(R("FT0"), oSV), R("SR0", 0, 16), Op.min)
+    act(R("G0", 32, 128), by(R("SV"), oG), Act.Relu)
+    fill(R("G0", 0, 32), 32, c1("NI"))
+    tr(R("GT0"), R("G0"))
+    lin(R("G1"), by(R("SR1"), oG))
     at = PIECE["SS1"][1] - 16 * (me % 2)
     tr(R("GT1", 0, 32), R("WA", at, at + 32))
     tr(R("GT1", 32, 128), R("G1"))
-    cp(R("MS", 0, 64, 2), by(R("GT1"), oF))
-    run(spread("MS", 0, 16, "va", 2))
-    for p in PARTS:
-        direct("MS", "ML", same, 8, lambda k: 8 * k, lambda k: 8 * me, range(*p), "ms")
-    MS = (("ms", landed(*[range(*p) for p in PARTS])),)
-    ts(R("LE"), by(R("MS"), oU), 4.0, ck, Op.mult, Op.add)
-    tt(R("LF"), by(R("MS"), oU0), R("KF"), Op.add)
-    act(R("ML", 8 * me, 8 * me + 8), R("MS", 0, 8), Act.Copy)
-    pick("PE", HH, NP, "Q2", R("LE", 12, 24))
+    for j in range(2):
+        if MERGE:
+            lin(R("MS", 1 - j, 64, 2), by(R("GT%d" % j), oF))
+            spread("MS", 1 - j, 16, 2)
+            if j:
+                for p in PARTS:
+                    direct("MS", "ML", same, 8, lambda k: 8 * k, lambda k: 8 * me, range(*p), "m1")
+                lin(R("ML", 8 * me, 8 * me + 8), R("MS", 0, 8))
+            continue
+        lin(R("MS", 32 * j, 32 * j + 32), by(R("GT%d" % j), oF))
+        spread("MS", 32 * j, 8, 1)
+        for p in PARTS:
+            direct("MS", "ML", same, 4, lambda k: 32 * j + 4 * k, lambda k: 32 * j + 4 * me, range(*p), "m%d" % j)
+        lin(R("ML", 32 * j + 4 * me, 32 * j + 4 * me + 4), R("MS", 32 * j, 32 * j + 4))
+    M0, M1 = ((("m%d" % max(j, MERGE), landed(*[range(*p) for p in PARTS])),) for j in range(2))
+    L0, L1, S1 = (R("ML"), R("ML"), R("MS")) if MERGE else (R("ML", 0, 32), R("ML", 32, 64), R("MS", 32, 64))
+    ts(R("LE"), by(S1, oU), 4.0, ck, Op.mult, Op.add)
+    tt(R("LF"), by(S1, oU0), R("KF"), Op.add)
     cp(R("LO"), R("LF"))
     rest = [k for k in range(*PARTS[0]) if k not in VIA2]
+    PA = (("pa", 2 * (landed(rest) + handed(VIA2))),)
+    n = 12 // NPE
+    for j in range(NPE):
+        pick("PE", HH + 16 * n * j, HH + 16 * n * (j + 1), "Q2", R("LE", 12 + n * j, 12 + n * (j + 1)))
     if VIA2:
         relay("PE", "R2", VIA2, S, lambda k: S * k)
     for x, cast in both:
         direct("PE" + x, "L2" + x, cast, S, lambda k: S * k, lambda k: S * (me % 4), rest, "pa")
-    PA = (("pa", 2 * (landed(rest) + len(VIA2) * len(off))),)
-    pick("PV", 0, HH, "C1", R("LO", 0, 12), (0, OWN + K1))
     pick("PE", 0, HH, "Q2", R("LE", 0, 12))
-    for b, src in zip((0, 2, 0, 2, 1, 1, 3, 3), ("PV", "PV", "PE", "PE", "PV", "PE", "PV", "PE")):
-        mm("P%d" % b, "QE", 128 * b, src, 0, HH, src == "PV", src == "PE")
-    pick("WM", 0, 128, "Q0", oWM, (0, 128))
+    pick("PV", 0, HH, "C1", R("LO", 0, 12), (0, OWN + K1))
+    for src in ("PE", "PV"):
+        for b in (0, 2, 1, 3):
+            mm("P%d" % b, "QE", 128 * b, src, 0, HH, src == "PE", src == "PV")
 
     def two(k):
         return HB + S * k + (16 if k else 0)
 
     for b in (2, 0, 3, 1):
         for k in range(4):
-            shifted("a" if b > 1 else "v", R("X2", 4 * two(k) + b, 4 * (two(k) + S), 4), R("P%d" % b, S * k, S * (k + 1)),
-                    c1("DH", 8 * b + k) if k else c1("A0", AW * b + K1))
+            lin(R("X2", 4 * two(k) + b, 4 * (two(k) + S), 4), R("P%d" % b, S * k, S * (k + 1)), bias=shift(k, b),
+                q="a" if b > 1 else "v")
     quant("C2", HB, HA, "X2")
     for x, cast in both:
         direct("C2" + x, "C2" + x, cast, S, two, lambda k: HB - S * k, range(4), "pb")
@@ -598,54 +718,58 @@ def rank_program(g, core, T, topo):
     def halfof(name, h, base=0):
         return R(name, base + HH * h, base + HH * (h + 1))
 
-    ts(R("LP"), by(R("ML"), oU1), ck, None, Op.add, arrive=MS)
-    tt(R("LX"), by(R("ML"), oUS), R("BQ"), Op.add)
-    pick("P1", 0, NP, "C1", R("LP", 0, 24), (LZ, None), arrive=P1)
-    quant("QW", 0, 128, "TW")
-    cp(R("LV"), R("LX", 0, 32))
-    mm("P4", "WM", 0, "P1", 0, NP)
-    ts(R("ZF"), R("TH8"), cSA, 0.0, Op.add, Op.is_lt)
-    pick("PV", HH, NP, "C1", R("LV", 12 * ha, 12 * ha + 12), (LZ, None))
-    tt(R("CA", NP), R("ZF"), R("ML", 1, 64, 8), Op.mult)
+    ts(R("LP"), by(L0, oU1), ck, None, Op.add, arrive=M0)
+    tt(R("LX"), by(L1, oUS), R("BQ"), Op.add, arrive=M1)
+    n = 24 // NP1
+    for j in range(NP1):
+        pick("P1", 16 * n * j, 16 * n * (j + 1), "C1", R("LP", n * j, n * (j + 1)), (LZ, None), arrive=P1)
+        mm(("P4", "P2")[j], "WM", 0, "P1", 16 * n * j, 16 * n * (j + 1))
     mm("P5", "QW", 0, "P1", 0, NP)
+    lin(R("YS", 0, NP), R("P5", 0, NP), q="a")
+    out = [dma("s", T.y[:, 0:NP], R("YS", 0, NP))]
+    cp(R("LV"), R("LX", 0, 32))
+    n = 12 // NVP
+    for j in range(NVP):
+        pick("PV", HH + 16 * n * j, HH + 16 * n * (j + 1), "C1", R("LV", 12 * ha + n * j, 12 * ha + n * (j + 1)), (LZ, None), P1)
     for b in range(4):
         mm(banks[b], "QE", 128 * b, "PV", HH, NP, True, False)
     for b in range(4):
         mm(banks[b], "QE", 128 * b, "L2", 0, HH, False, True, PA)
-    for q in range(N):
-        ts(R("CA", S * q, S * (q + 1)), R("P4", S * q, S * (q + 1)), cSA, c1("TH8", q), Op.subtract, Op.is_gt)
-    act(R("YS", 0, NP), R("P5", 0, NP), Act.Copy)
-    out = [dma("s", T.y[:, 0:NP], R("YS", 0, NP))]
     for b in range(4):
-        shifted("a", R("X2", 4 * HA + b, 4 * (HA + HH), 4), R(banks[b], 0, HH), c1("A0", AW * b + K1))
+        lin(R("X2", 4 * HA + b, 4 * (HA + HH), 4), R(banks[b], 0, HH), bias=shift(0, b), q=AQ[b])
+    quant("C2", HA, HA + HH + 4, "X2")
+    ts(R("ZF"), R("TH8"), cSA, 0.0, Op.add, Op.is_lt)
+    lin(R("ZE"), R("ML", 1, 64, 8) if MERGE else R("ML", 0, 32, 4), 0.5, -S / 2, arrive=M0)
+    tt(R("CA", NP), R("ZF"), R("ZE"), Op.mult)
+    for q in range(N):
+        j, at = divmod(q, N // NP1)
+        ts(R("CA", S * q, S * (q + 1)), R(("P4", "P2")[j], S * at, S * (at + 1)), cSA, c1("TH8", q), Op.subtract, Op.is_gt)
     scan(R("CB"), R("CA"), R("CA"), Op.add, Op.max)
     ts(R("FV"), R("LMM"), c1("CB", NP + 7), c1("PS"), Op.is_gt, Op.mult)
     tr(R("FT"), R("FV"))
     scan(R("FS"), R("R4"), R("FT"), Op.min)
-    run(spread("FS", 3, 32, SPQ, 4))
+    spread("FS", 3, 32, 4)
     ts(R("LQ"), by(R("FS"), oLQ), -1.0, cZ, Op.mult, Op.add)
-    act(R("T2N"), by(R("ML"), oU), scale=4.0, bias=ck)
-    quant("C2", HA, HA + HH + 4, "X2")
-    for h, win, bank, arrive in ((hb, (0, HH + 16), "P2", PB), (ha, (HA, None), "P3", ())):
+    for h, win, bank, arrive, q in ((hb, (0, HH + 16), "P2", PB, YQ[0]), (ha, (HA, None), "P3", (), YQ[1])):
         pick("OC", HH * h, HH * (h + 1), "C2", R("LQ", 12 * h, 12 * h + 12), win, arrive)
         mm(bank, "QW", 0, "OC", HH * h, HH * (h + 1))
         out.append(dma("s", T.oc[:, 4 * HH * h:4 * HH * (h + 1)], u8(halfof("OCc", h))))
-    act(halfof("YS", hb, NP), R("P2", 0, HH), Act.Copy)
-    out.append(dma("s", T.y[:, NP + HH * hb:NP + HH * (hb + 1)], halfof("YS", hb, NP)))
+        lin(halfof("YS", h, NP), R(bank, 0, HH), q=q)
+        out.append(dma("s", T.y[:, NP + HH * h:NP + HH * (h + 1)], halfof("YS", h, NP)))
     oa = [dma("a", T.osc[4 * q:4 * q + 4, :], R("OCs", 0, NP, 1, (32 * q, 32 * q + 4))) for q in range(4)]
-    ts(R("N2"), by(R("FS"), oLQ), 1000.0, -1.0, Op.mult, Op.add)
-    tt(R("N1"), by(R("ML"), oU1), R("BQ", 0, 32), Op.subtract)
-    cp(halfof("YS", ha, NP), R("P3", 0, HH))
-    out.append(dma("s", T.y[:, NP + HH * ha:NP + HH * (ha + 1)], halfof("YS", ha, NP)))
-    tt(R("N2B", p=low), R("N2", p=low), R("T2N", p=low), Op.min)
+    tt(R("N1"), by(L0, oU1), R("BQ", 0, 32), Op.subtract, arrive=M0)
     ts(R("N1B", p=low), R("N1", p=low), R("CF", 4, 5, 1, low), -1.0, Op.add, Op.max)
-    tr(R("N2T", p=low), R("N2B", p=low))
     tr(R("N1T", p=low), R("N1B", p=low))
-    oa.append(dma("a", T.nm[0:1, NP:2 * NP], R("N2T", 0, 16, 1, (0, P))))
     out.append(dma("s", T.nm[0:1, 0:NP], R("N1T", 0, 16, 1, (0, P))))
+    lin(R("T2N"), by(L1, oU), 4.0, ck, arrive=M1)
+    lin(R("N2"), by(R("FS"), oLQ), 1000.0, -1.0)
+    tt(R("N2B", p=low), R("N2", p=low), R("T2N", p=low), Op.min)
+    tr(R("N2T", p=low), R("N2B", p=low))
+    out.append(dma("s", T.nm[0:1, NP:2 * NP], R("N2T", 0, 16, 1, (0, P))))
     op("s", None, after=out)
     op("a", None, after=oa)
-    op("g", None, arrive=(("sent", sent[0]),))
+    op("g", None, arrive=(("sent", sent[0]),), behind=[i for i, o in enumerate(ops) if o["q"] == "g"])
+    ops = _given(ops, ORDER) if len(ORDER) == len(ops) else _order(ops)
 
     known, at_issue, waits, needed = {q: 0 for q in queues}, [], [], set()
     for i, o in enumerate(ops):

from concourse.bass import DstId, RemoteDMATransfer
from concourse.mybir import dt, AluOpType, AxisListType, ActivationFunctionType

Op, Act = AluOpType, ActivationFunctionType
N, P, CAP, M, S = 8, 24, 12, 64, 48
UQ = 126
NL, NO = UQ + 2 * N, (N - 1) * P
K1 = 4 * P
NP = N * S
ZC = 32
LZ = (N - 1) * K1
OWN = LZ + ZC
HH, HB, HA = NP // 2, 3 * S, 7 * S + 16
AW = 100
EPS, BIG, HUGE = 1e-37, 2.0 ** 80, 2.0 ** 90
PARTS = ((4, 8), (0, 4))
GROUPS = (((6, 7), (6, 7), "R1", ()), ((4, 5, 1), (4, 5), "R1", (1,)), ((2, 3), (), "R3", (2, 3)))
XA = sum((group[0] for group in GROUPS), ())
VIA0, VIA2 = (4, 5, 6, 7), (4, 5)
CYC, PEC, SLOW, WAKE, LOCAL, ISSUE, REMOTE, CALL, ROW, RATE, FIRST = 0.83, 0.63, 1.25, 150, 1400, 60, 2300, 250, 7, 20, 1300
NEARLY, YIELD, SPARE = 30, 60, 1000
NVP, NP1, NPE, DHQ, YQ = 1, 2, 2, "vvvv", "av"
MERGE = 1
NEAR, AQ = 4, "aava"
ORDER = [
    1, 15, 0, 6, 2, 10, 3, 4, 13, 7, 11, 5, 18, 12, 16, 17, 8, 19, -42, 14, -43, 44, 9, 47, -56, 111, 20, -45, 54, 55,
    24, -50, -48, 46, -94, 21, -57, 25, -51, 87, -110, 86, 61, 60, 26, -103, 22, -100, 27, -58, 62, 59, -112, -95, 64,
    28, -99, 52, 66, 23, -113, -101, 63, -96, 30, 85, -106, 65, -49, 67, 29, 97, 70, 102, 68, -119, 116, -105, 69, 53,
    71, 88, 72, 104, 73, 80, 37, -92, -91, 89, -77, 32, 74, 84, 33, 76, 75, 35, -122, 107, -90, 108, -118, 78, -120,
    93, 79, 36, -121, -98, 81, 31, 83, 38, 115, 109, 34, 117, 114, 39, 40, 124, 41, 123, 125, 126, 127, 132, 128, 133,
    129, -136, 134, 157, 130, -149, 135, -153, 180, -158, 181, 155, -150, 182, -159, 137, -151, 169, -160, 184, -143,
    183, 139, -152, -154, 185, -156, 167, -138, 186, -142, 161, -140, -141, -173, 187, -170, 144, -171, 162, -174,
    189, -168, -172, 145, 147, 188, 163, 164, 175, 148, 194, 131, 191, 146, 165, 190, 176, 192, 195, 166, 196, 193,
    177, 178, 197, 179, -200, 198, -217, 199, 202, 204, 201, 203, 220, 205, 207, 210, 211, 212, 208, 209, 206, 221,
    222, 213, 223, 216, 214, 215, -227, 218, -230, -231, -228, 219, -224, 232, -229, 225, 226, -233, -234, -236, 238,
    -235, 237, -240, 239, 241, -243, 244, 245, 242, 256, 247, 255, 251, 248, 246, 249, 260, 252, 258, 257, 262, 253,
    261, 250, 259, 263, 264, 254, 274, 265, 272, 273, 267, 266, 82, 268, 270, 279, 269, 281, 280, 278, 271, 277, 282,
    276, 275, -355, 283, -314, 286, 287, 284, 288, 289, 285, 291, 292, 362, 290, 297, 313, 316, 293, 319, 299, 318,
    315, 294, 317, 322, 321, 323, 320, 298, 295, 324, 300, 302, 325, 351, 301, 326, 303, 352, 327, 305, 353, 304,
    -328, 331, -330, 329, 354, 306, 296, 333, -332, 307, 308, 334, 311, 310, 309, 335, -356, 336, 312, 338, 357, 342,
    341, 337, 358, 344, 343, 348, 359, 339, 349, 345, 350, 347, 340, 346, 361, 360,]

F, BF, I32, U16, C, SC = "float32", "bfloat16", "int32", "uint16", "float8_e4m3fn_x4", "uint8"
SCRATCH = {}


def _sb(dtype, **kw):
    for name, n in kw.items():
        SCRATCH[name] = ("sbuf", [128, n], dtype)


_sb(BF, T0=512, T1=512, T2=4 * NP, TW=512, TE=516, JB=128, JM=48, JQ=128, X1=4 * (OWN + K1), X2=4 * (HA + HH + 4),
    RR=144, R4=128, DM=48, TB1=150, TH1=74, TH0=48, D0=48, CM0=50, SN0=50, D1=144,
    CG=NO, CH=NO, CA=NP + 8, CB=NP + 8, LMM=128, FV=128, FT=128, FS=128, NT=2 * K1, MX=16, JK=48, PS=2)
for _n, _w in dict(Q0=144, Q1=128, Q2=NP, QW=128, QE=512, LC=NO, WQ=128, WM=128, V0=128, C1=OWN + N * K1, PE=NP,
                   L2=HH, PV=NP, P1=NP, C2=HA + HH + 4, OC=NP, R0=P, R1=2 * K1, R2=S, R3=2 * K1).items():
    _sb(C, **{_n + "c": _w})
    _sb(SC, **{_n + "s": _w})
_sb(F, FM=150, EQ=150, SN1=150, CP=1, CF=8, A0=4 * AW, DH=32, AF=2 * K1, MS=64, ML=64, YS=2 * NP, SR0=200, SS0=200)
_sb(I32, PI=4, CI=8, KI=2)
_sb(U16, OU=48, OL0=2, OL1=4, OA=4, LO=16, LV=32, LE=32, LP=32, LQ=32)
for _k in range(8):
    SCRATCH["P%d" % _k] = ("psum", [128, 512], F)
PIECE = {}
for _b, _d in (("K", dict(CD=16, OF=48, PY0=32, MK=16, LM=32, TA=8, TB=8, TH8=8, BQ=48, TT=8, KF=16, I3=8)),
               ("WA", dict(M0=32, BS0=32, AS=32, NS=16, SE=16, SF=16, FL0=32, FT0=32, PEN=48, NI=8, SV=16,
                           G0=128, GT0=128, PB=48, A1=48, M1=48, BS1=48, SR1=48, SS1=48, G1=96, GT1=128, LF=16, IW=8, IV=8)),
               ("WB", dict(LX=48, ZF=8, ZE=8, N1=32, N1B=32, N1T=32, T2N=32, N2=32, N2B=32, N2T=32))):
    _at = 0
    for _n, _w in _d.items():
        PIECE[_n] = (_b, _at, _w)
        _at += _w
    _sb(F, **{_b: _at})

POOL = {"v": 47, "a": 42, "p": 18, "g": 11, "d": 16}
SEMAPHORES = (["e1", "e2", "p1", "m0", "m1", "pa", "pb", "sent"] + ["R%d%s" % (j, x) for j in range(4) for x in "cs"]
              + ["x%s%d" % (q, i) for q, n in POOL.items() for i in range(n)])


def _mask(engines):
    m = 0
    for e in engines:
        m |= 1 << e
    return m


def _dst(topo, c):
    rid, pid, _ = topo.addr(c)
    return DstId(rid=rid, pnc=pid)


def _share(topo, cores, r, ks):
    src = cores[r]
    far = [k for k in ks if k and topo.chip(cores[r ^ k]) != topo.chip(src)]
    near = [k for k in ks if k and k not in far]
    off = topo.engines(src, cores[r ^ far[0]])
    size = {k: 1 for k in far}
    grown = True
    while grown:
        grown = False
        low = min(size.values())
        for k in far:
            if size[k] == low and sum(size.values()) + low <= len(off):
                size[k] *= 2
                grown = True
    out, at = {}, 0
    for k in sorted(far, key=lambda k: -size[k]):
        out[k] = off[at:at + size[k]]
        at += size[k]
    for k in near:
        out[k] = [e for e in topo.engines(src, cores[r ^ k]) if e not in off]
    return out


def _relay(topo, cores, r, ks):
    src = cores[r]
    free = [h for h in topo.cores_of(src) if topo.die(h) == topo.die(src) and h not in cores]
    out = {}
    for k in ks:
        can = [h for h in free if topo.may_write(h, cores[r ^ k])]
        out.setdefault(min(can, key=lambda h: len(out.get(h, ()))), []).append(k)
    return out


def _inner(topo, cores, r):
    src = cores[r]
    far = [c for c in cores if topo.chip(c) != topo.chip(src)][0]
    mate = [c for c in topo.cores_of(src) if c != src][0]
    return [e for e in topo.engines(src, mate) if e not in topo.engines(src, far)]


def _hand(inner, helpers):
    return inner // min(helpers, 2)


def _roots_at(r, k):
    return P * (r - (r > r ^ k))


STAGES = ((("R0", VIA0, "LC", _roots_at, P, "e2", True),)
          + tuple((buf, via, "C1", lambda r, k: OWN + K1 * k, K1, "p1", False) for _, via, buf, _ in GROUPS)
          + (("R2", VIA2, "L2", lambda r, k: S * (r % 4), S, "pa", False),))


def _helper(g, core, T, topo):
    cores = list(T.cores)
    sent = 0
    for r in range(N):
        for buf, via, land, at, w, sem, shared in STAGES:
            plan = _relay(topo, cores, r, via)
            if core not in plan:
                continue
            ks = plan[core]
            off = topo.engines(core, cores[r ^ ks[0]])
            n = len(off) // len(ks)
            for x in "cs":
                def view(name, a):
                    v = T[name + x][:, a:a + w]
                    return v.bitcast(dt.uint8) if x == "c" else v
                g.wait_ge(T.sem[buf + x], _hand(len(_inner(topo, cores, r)), 2 if shared else len(plan)))
                g.remote_dma_fused([RemoteDMATransfer(
                    dst_ids=[_dst(topo, cores[r ^ k])], dma_engine_mask=_mask(off[n * i:n * (i + 1)]), remote_sem=T.sem[sem],
                    srcs=[view(buf, 0 if shared else w * i)], dsts=[view(land, at(r, k))]) for i, k in enumerate(ks)],
                    local_sem=T.sem.sent)
                sent += len(off)
    if sent:
        g.wait_ge(T.sem.sent, sent)


def _order(ops):
    final = {b + x: sem for b, _, _, _, _, sem, _ in STAGES for x in "cs"}
    first = [b for b, via, _, _, _, _, _ in STAGES if via][:1]
    feeders, succ = {}, [[] for _ in ops]
    for i, o in enumerate(ops):
        for sem, _, busy, again in o["feeds"]:
            feeders.setdefault(final.get(sem, sem), set()).add(i)

    def hop(sem, again):
        return (REMOTE + CALL + again + FIRST * (sem[:2] in first)) if sem in final else 0

    def after(d):
        return LOCAL + ops[d]["dma"] if ops[d]["dma"] else SLOW * ops[d]["cost"] + WAKE

    need = []
    for i, o in enumerate(ops):
        fed = set(j for sem, _ in o["arrive"] for j in feeders.get(sem, ()))
        need.append(o["deps"] | o["behind"] | fed)
        for d in o["deps"]:
            succ[d].append((i, after(d)))
        for d in o["behind"]:
            succ[d].append((i, SLOW * ops[d]["cost"]))
        for d in fed:
            succ[d].append((i, REMOTE + max(busy + hop(sem, again) for sem, _, busy, again in ops[d]["feeds"])))
    way = [0.0] * len(ops)
    for i in reversed(range(len(ops))):
        way[i] = max([lat + way[j] for j, lat in succ[i]] + [after(i)]) + ops[i]["lift"]
    start, free, engine, land, left, order = {}, {}, {}, {}, set(range(len(ops))), []
    ready, called = {}, [False]
    while left:
        best = {}
        for i in left:
            o = ops[i]
            if i not in ready:
                if not all(d in start for d in need[i]):
                    continue
                ready[i] = max([0] + [start[d] + after(d) for d in o["deps"]] + [land.get(s, 0) for s, _ in o["arrive"]])
            for q, cost in [(o["q"], o["cost"])] + ([(o["alt"][0], o["alt"][2])] if o["alt"] else []):
                best.setdefault(q, []).append((max(ready[i], free.get(q, 0)), i, cost))
        q = min(best, key=lambda q: (min(best[q])[0], q != "a"))
        now = min(best[q])[0]
        rank = {i: way[i] - (SPARE if q == "v" and ops[i]["alt"] else 0) for _, i, _ in best[q]}
        cands = sorted(best[q], key=lambda c: -rank[c[1]])
        for t, i, cost in cands:
            if t > now + NEARLY:
                continue
            if any(rank[j] > rank[i] and t + SLOW * cost - u > YIELD and u - t < rank[j] - rank[i]
                   and not ops[j]["alt"] for u, j, _ in cands if u > t):
                continue
            break
        else:
            t, i, cost = min(c for c in cands if c[0] > now + NEARLY)
            free[q] = t - NEARLY
            continue
        o = ops[i]
        if q != o["q"]:
            o["q"], o["fn"], o["cost"] = o["alt"]
        start[i] = t
        free[q] = t + (cost if o["dma"] or o["feeds"] else SLOW * cost)
        for sem, engines, busy, again in o["feeds"]:
            at = t + REMOTE + FIRST * (not called[0])
            for e in engines:
                engine[e] = max(engine.get(e, 0), at) + busy
            end = max(engine[e] for e in engines) + hop(sem, again)
            land[final.get(sem, sem)] = max(land.get(final.get(sem, sem), 0), end)
        called[0] = called[0] or bool(o["feeds"])
        left.remove(i)
        order.append(i)
    at = {i: n for n, i in enumerate(order)}
    return [dict(ops[i], deps=sorted((at[d] for d in ops[i]["deps"]), reverse=True)) for i in order]


def _given(ops, order):
    at = {abs(i): n for n, i in enumerate(order)}
    assert len(at) == len(ops) and all(at[d] < at[i] for i, o in enumerate(ops) for d in o["deps"] | o["behind"])
    out = []
    for i in order:
        o = dict(ops[abs(i)], deps=sorted((at[d] for d in ops[abs(i)]["deps"]), reverse=True))
        if i < 0:
            o["q"], o["fn"], o["cost"] = o["alt"]
        out.append(o)
    return out


def rank_program(g, core, T, topo):
    me = T.rank_of(core)
    if me is None:
        _helper(g, core, T, topo)
        return
    cores = list(T.cores)
    V, A, PE, SY = g.vector, g.scalar, g.tensor, g.sync
    queues = {"v": V, "a": A, "p": PE, "g": g, "s": SY}

    def R(name, a=0, b=None, step=1, p=(0, 128)):
        buf, at, n = PIECE[name] if name in PIECE else (name, 0, SCRATCH[name][1][1])
        b = n if b is None else b
        cols = range(512) if SCRATCH[buf][0] == "psum" else range(at + a, at + b, step)
        return (T[buf][p[0]:p[1], at + a:at + b:step], [(buf, p[0], p[1], frozenset(cols))], len(range(a, b, step)))

    def c1(name, j=0):
        return R(name, j, j + 1)

    def by(win, offs):
        return (win[0].indirect(offs[0]), win[1] + offs[1], win[1], offs[1])

    def u8(v):
        return (v[0].bitcast(dt.uint8), v[1], v[2])

    def u32(v):
        return (v[0].bitcast(dt.uint32), v[1], v[2])

    def ap(x):
        return x[0] if isinstance(x, tuple) else x

    ops, log, lift = [], {}, [0]

    def size(v):
        return 16 * len(v[3][0][3]) if len(v) == 4 else v[2]

    def cycles(out, ins, per=None, fixed=50):
        if len(out) == 4:
            return fixed + 3.5 * CYC * size(out)
        if len(ins[0]) == 4:
            return fixed + 1.5 * CYC * size(ins[0])
        if per is None:
            per = 0.5 if all(SCRATCH[v[1][0][0]][2] in (BF, U16) for v in (out,) + ins) else 1
        return CYC * max(64, per * size(out))

    def op(q, fn, reads=(), writes=(), arrive=(), dma=0, acc=False, after=(), cost=0, alt=None, feeds=(), behind=()):
        i, deps, behind = len(ops), set(after), set(behind)
        rd = [r for x in reads if isinstance(x, tuple) for r in x[1]]
        wr = []
        for x in writes:
            if len(x) == 4:
                wr += x[2]
                rd += x[3]
            else:
                wr += x[1]
        for kind, regs in ((0, rd), (1, wr)):
            for buf, p0, p1, cols in regs:
                bank = SCRATCH[buf][0] == "psum"
                for j, k, q0, q1, cs in log.get(buf, ()):
                    if bank:
                        hit = ops[j]["q"] != q or (k != kind) or (k and not acc)
                        hit = hit and (ops[j]["q"] != q or (q0 < p1 and p0 < q1))
                        if acc and not hit:
                            behind.add(j)
                    else:
                        hit = (k or kind) and q0 < p1 and p0 < q1 and not cols.isdisjoint(cs)
                    if hit:
                        deps.add(j)
        for kind, regs in ((0, rd), (1, wr)):
            for buf, p0, p1, cols in regs:
                log.setdefault(buf, []).append((i, kind, p0, p1, cols))
        ops.append(dict(q=q, fn=fn, deps=deps, behind=behind, arrive=arrive, dma=dma, cost=cost, alt=alt, feeds=feeds,
                        lift=lift[0]))
        lift[0] = 0
        return i

    def ts(out, in0, s1, s2, o0, o1=None, arrive=()):
        more = (None, o0) if s2 is None else (ap(s2), o0, o1)
        op("v", lambda: V.tensor_scalar(out[0], in0[0], ap(s1), *more), (in0, s1, s2), (out,), arrive,
           cost=cycles(out, (in0,)))

    def tt(out, in0, in1, o, arrive=()):
        op("v", lambda: V.tensor_tensor(out[0], in0[0], in1[0], o), (in0, in1), (out,), arrive,
           cost=cycles(out, (in0,), 1 if SCRATCH[in0[1][0][0]][0] == "psum" else 2))

    def cp(out, in_, arrive=()):
        op("v", lambda: V.tensor_copy(out[0], in_[0]), (in_,), (out,), arrive, cost=cycles(out, (in_,)))

    def ms(out, val):
        op("v", lambda: V.memset(out[0], val), (), (out,), cost=cycles(out, (out,)))

    def scan(out, reset, data, o0=Op.mult, o1=Op.add):
        op("v", lambda: V.tensor_tensor_scan(out[0], reset[0], data[0], 0.0, o0, o1), (reset, data), (out,),
           cost=cycles(out, (reset, data)))

    def tr(out, in_):
        op("v", lambda: V.transpose(out[0], in_[0]), (in_,), (out,), cost=cycles(out, (in_,)))

    def act(out, in_, func=Act.Identity, arrive=(), acc=None, **kw):
        args = {k: ap(v) for k, v in kw.items()}
        if acc is not None:
            args["accum_out"] = acc[0]
        op("a", lambda: A.activation(out[0], in_[0], func, **args), (in_,) + tuple(kw.values()),
           (out,) if acc is None else (out, acc), arrive, cost=cycles(out, (in_,), 1, 65) + (acc is not None) * 20)

    def lin(out, in_, scale=1.0, bias=0.0, arrive=(), q=None):
        if scale == 1.0:
            fv = (lambda: V.tensor_scalar(out[0], in_[0], ap(bias), None, Op.add)) if bias != 0.0 else (
                lambda: V.tensor_copy(out[0], in_[0]))
        else:
            fv = lambda: V.tensor_scalar(out[0], in_[0], scale, ap(bias), Op.mult, Op.add)
        fa = (lambda: A.activation(out[0], in_[0], Act.Identity, bias=ap(bias), scale=scale)) if bias != 0.0 else (
            lambda: A.activation(out[0], in_[0], Act.Copy, scale=scale))
        a = ("a", fa, cycles(out, (in_,), 1, 65))
        if q == "a":
            op("a", fa, (in_, bias), (out,), arrive, cost=a[2])
        else:
            op("v", fv, (in_, bias), (out,), arrive, cost=cycles(out, (in_,)), alt=None if q else a)

    def fill(out, n, val):
        lin(out, R("JB", 0, n), 0.0, val)

    def quant(name, a, b, tile, at=None):
        at = 4 * a if at is None else at
        o, s, i = R(name + "c", a, b), R(name + "s", a, b), R(tile, at, at + 4 * (b - a))
        op("v", lambda: V.quantize_mx(o[0], s[0], i[0]), (i,), (o, s), cost=12 + 0.88 * (b - a))

    def mm(bank, lhs, la, rhs, a, b, start=True, stop=True, arrive=()):
        v = (R(lhs + "c", la, la + 128), R(lhs + "s", la, la + 128), R(rhs + "c", a, b), R(rhs + "s", a, b))
        o = R(bank, 0, b - a)
        op("p", lambda: PE.matmul_mx(o[0], v[0][0], v[1][0], v[2][0], v[3][0], start, stop), v, (o,), arrive,
           acc=not start, cost=PEC * (b - a + 16))

    def pick(dst, a, b, src, offs, win=(0, None), arrive=()):
        cp(u32(R(dst + "c", a, b)), by(u32(R(src + "c", *win)), offs), arrive)
        act(R(dst + "s", a, b), by(R(src + "s", *win), offs), Act.Copy, arrive)

    def width(v):
        return v[2] * {BF: 2, SC: 1}.get(SCRATCH[v[1][0][0]][2], 4)

    def dma(q, out, in_, arrive=()):
        return op(q, lambda: queues[q].dma_start(ap(out), ap(in_)), (in_,), (out,) if isinstance(out, tuple) else (),
                  arrive, dma=8 * (ROW + width(out if isinstance(out, tuple) else in_) / RATE), cost=ISSUE)

    def iota(out, pattern, base=0, cm=0, whole=False):
        kw = {} if whole else dict(allow_small_or_imprecise_dtypes=True)
        op("g", lambda: g.iota(out[0], pattern, base, cm, **kw), (), (out,), cost=130 + 2 * CYC * size(out),
           behind=calls[-1:])

    sent, calls = [0], []

    def remote(transfers):
        sent[0] += sum(len(t[2]) for t in transfers)
        calls.append(op("g", lambda: g.remote_dma_fused([RemoteDMATransfer(
            dst_ids=[_dst(topo, c) for c, _ in d], dma_engine_mask=_mask(e), remote_sem=T.sem[sem],
            srcs=[s[0]], dsts=[x[0] for _, x in d]) for s, d, e, sem in transfers], local_sem=T.sem.sent),
            [t[0] for t in transfers], cost=CALL, behind=calls[-1:],
            feeds=[(sem, e, len(d) * 128 // len(e) * (ROW + width(s) / RATE), 16 * (ROW + width(s) / RATE))
                   for s, d, e, sem in transfers]))

    def direct(src, dst, cast, w, frm, to, ks, sem):
        remote([(cast(R(src, frm(k), frm(k) + w)), [(cores[me ^ k], cast(R(dst, to(k), to(k) + w)))], e, sem)
                for k, e in _share(topo, cores, me, ks).items()])

    def landed(*parts):
        return sum(len(_share(topo, cores, me ^ k, ks)[k]) for ks in parts for k in ks if k)

    def same(v):
        return v

    both = (("c", u8), ("s", same))

    def spread(name, base, w, step):
        for po, pi, n, a, b in ((0, 32, 32, 1, 2), (64, 96, 32, 3, 4), (32, 0, 32, 0, 1), (96, 64, 32, 2, 3),
                                (64, 0, 64, 0, 2), (0, 64, 64, 2, 4)):
            a, b = base + w * a, base - base % step + w * b
            lin(R(name, a, b, step, (po, po + n)), R(name, a, b, step, (pi, pi + n)))

    cg, ca, c4, cs, ck, ch, c2 = (c1("CF", j) for j in range(7))
    cPN, cOA, cBG, c64, cLM, cB, cPS, cZ, cF, cX, cO2, cL2 = (c1("CD", j) for j in range(12))
    oWQ, oV0, oWM, oG, oPN, oSV, oF, oU, oU0, oUS, oLQ = (R("OU", a, b) for a, b in (
        (0, 8), (8, 16), (16, 24), (24, 30), (30, 33), (34, 35), (36, 38), (38, 40), (38, 39), (38, 41), (42, 44)))
    oU1 = R("OU", 44, 46) if MERGE else oU

    def JB(n):
        return R("JB", 0, n)

    def quad(name, q, a, b):
        return R(name, a, b, 1, (32 * q, 32 * q + 32))

    def shift(k, b):
        return c1("DH", 8 * b + k) if k else c1("A0", AW * b + K1)

    def made(k):
        return K1 * XA.index(k) if k else OWN

    def children(k):
        for b in range(4):
            lin(R("X1", 4 * made(k) + b, 4 * (made(k) + K1), 4), R("A0", AW * b, AW * b + K1), bias=shift(k, b))

    dma("s", R("T0", 0, 4 * P), T.r0[:])
    dma("a", R("T0", 4 * UQ), T.u[:, 0:8])
    dma("s", R("T1", 0, 4 * K1), T.r1[:])
    lift[0] = 9000
    dma("s", R("T2"), T.r2[:])
    iota(c1("PI"), [[0, 1]], 0, 1, True)
    iota(R("JB"), [[1, 128]])
    for j in (1, 2):
        iota(c1("PI", j), [[0, 1]], 0, 4 ** j, True)
    iota(R("JM"), [[0, 3], [1, 16]])
    iota(R("TB1"), [[-16, 3], [1, 50]])
    ms(R("T0", 4 * P, 4 * UQ), 0.0)
    ms(R("TE"), 0.0)
    cp(R("CP"), c1("PI"))
    ms(R("T1", 4 * K1), 0.0)
    ts(R("TE", 3, 515, 4), R("JB"), R("CP"), None, Op.is_equal)
    ms(R("X1", 4 * LZ, 4 * OWN), 0.0)
    for a, b, v, m in ((0, 2, R("PI", 0, 3, 2), 15), (2, 5, R("PI", 0, 3), 3), (5, 7, R("PI", 0, 2), 1)):
        ts(R("CI", a, b), v, 4, m, Op.logical_shift_right, Op.bitwise_and)
    cp(R("CF", 0, 7), R("CI", 0, 7))
    for b in range(4):
        quant("QE", 128 * b, 128 * (b + 1), "TE", 3 - b)
    quant("Q0", 0, 128, "T0")

    eng = _share(topo, cores, me, range(N))
    far = [k for k in eng if topo.chip(cores[me ^ k]) != topo.chip(core)]
    near = [k for k in eng if k not in far]
    off = sorted(e for k in far for e in eng[k])
    on = _inner(topo, cores, me)
    half = len(on) // 2
    for j, (x, cast) in enumerate(both):
        land = {k: (cores[me ^ k], cast(R("Q0" + x, UQ + 2 * k, UQ + 2 * k + 2))) for k in eng}
        remote([(cast(R("Q0" + x, UQ, UQ + 2)), [land[k] for k in far], off, "e1")]
               + [(cast(R("Q0" + x, UQ, UQ + 2)), [land[k]], on[2 * j:2 * j + 1], "e1") for k in near])
    E1 = (("e1", 2 * (len(far) * len(off) + len(near))),)
    for x, cast in both:
        src = cast(R("Q0" + x, 0, P))
        land = {k: (cores[me ^ k], cast(R("LC" + x, _roots_at(me, k), _roots_at(me, k) + P))) for k in eng}
        remote([(src, [land[k] for k in far if k not in VIA0], off, "e2")]
               + [(src, [land[k]], on[0:NEAR], "e2") for k in near]
               + [(src, [(h, cast(R("R0" + x))) for h in _relay(topo, cores, me, VIA0)][::-1], on[half:], "R0" + x)][:len(VIA0)])

    def handed(via):
        return sum(len(off) // len(ks) for k in via for ks in _relay(topo, cores, me ^ k, via).values() if k in ks)

    E2 = (("e2", 2 * ((len(far) - len(VIA0)) * len(off) + handed(VIA0) + NEAR * len(near))),)

    def relay(src, buf, via, w, frm, beside=()):
        plan = _relay(topo, cores, me, via)
        n = _hand(len(on), len(plan))
        for x, cast in both:
            remote([(cast(R(src + x, frm(ks[0]), frm(ks[0]) + w * len(ks))), [(h, cast(R(buf + x, 0, w * len(ks))))],
                     (on + off)[n * i:n * (i + 1)], buf + x) for i, (h, ks) in enumerate(plan.items())]
                   + [(cast(R(src + x, frm(k), frm(k) + w)), [(cores[me ^ k], cast(R(dst + x, at, at + w)))], off, sem)
                      for k, dst, at, sem in beside])

    iota(R("NT"), [[0, 2], [1, K1]])
    iota(R("KF"), [[0, 16]], OWN)
    iota(R("X2", 4 * HH, 4 * (HH + 16)), [[0, 64]])
    iota(R("KF", 3, 6), [[0, 3]], made(1))
    iota(R("KF", 6, 12), [[K1, 2], [0, 3]], made(2))
    iota(R("X2", 4 * (HA + HH)), [[0, 16]])
    iota(R("JQ"), [[0, 8], [1, 4], [0, 4]])
    iota(R("BQ", P), [[0, P]])
    for m in range(3):
        iota(R("BQ", m, P, 3), [[K1 * (1 - 2 * (me >> i & 1)) << i, 2] for i in (2, 1, 0)], ZC + K1 * me)
    iota(R("R4"), [[0, 32], [256, 4]])
    dma("s", R("TW"), T.w[:], E1)
    fill(R("OF", 14, 16), 2, float(UQ + 1))
    lin(R("OF", 0, 8), JB(8), 2.0, float(UQ))
    fill(R("OF", 16, 24), 8, float(UQ))
    lin(R("OF", 8, 14), JB(6), 4.0, cs)
    cp(R("OU", 0, 24), R("OF", 0, 24))
    fill(R("RR", 0, 128), 128, 1.0)
    fill(R("RR", 128, 144), 16, 1.0)
    fill(R("RR", 0, 144, 48), 3, 0.0)
    lin(cX, ca, 4.0 / 3, 2.0 / 3)
    lin(R("TT", 0, 2), JB(2), 64.0 / 3, cX)
    cp(R("KI"), R("TT", 0, 2))
    ts(R("OF", 38, 40), R("KI"), 31.0, 1.0 + MERGE, Op.min, Op.mult)
    act(cBG, ca, Act.Relu, scale=BIG, bias=-7 * BIG)
    act(c1("CM0", 48), ca, Act.Relu, scale=24.0, bias=-168.0)
    lin(cB, cg, float(K1), float(ZC))
    lin(cO2, ch, float(K1), ck)
    lin(cOA, cB, -1.0, cO2)
    quant("Q1", 0, 128, "T1")
    pick("V0", 0, 128, "Q0", oV0, (0, 128))
    for b in range(4):
        mm("P%d" % b, "QE", 128 * b, "V0", 0, 128, True, False)
        mm("P%d" % b, "QE", 128 * b, "Q1", 0, 128, False, True)
    for b in range(4):
        lin(R("A0", AW * b, AW * b + K1 + 1), R("P%d" % b, 0, K1 + 1), q="a")
    children(0)
    quant("C1", LZ, LZ + 128, "X1")
    for a in range(0, NP, 128):
        quant("Q2", a, a + 128, "T2")
    quant("QW", 0, 128, "TW")
    pick("WM", 0, 128, "Q0", oWM, (0, 128))
    ts(R("TH1"), R("TB1", 0, 74), ca, -EPS, Op.is_lt, Op.mult)
    ts(R("DM"), R("JM"), ca, None, Op.is_equal)
    ts(R("MK", 0, 12), R("JM", 0, 48, 4), 0.25, cs, Op.mult, Op.is_equal)
    ts(R("FM"), R("TB1"), ca, 2.0, Op.not_equal, Op.mult)
    lin(R("FM"), R("FM"), bias=-1.0)
    fill(R("FM", 0, 150, 50), 3, 0.0)
    fill(R("EQ", 49, 150, 50), 3, -float(S))
    lin(R("I3", 0, 3), JB(3), 16.0, ca)
    lin(R("I3", 4, 7), R("I3", 0, 3), 2.0, -float(S))
    lin(R("PY0"), JB(32), 4.0, cB)
    lin(cPN, ch, 16.0, cs)
    lin(cF, c2, 16.0, 15.0)
    lin(R("TH0", 0, P), R("TH1", 0, P))
    lin(R("TH0", P, 2 * P), R("TH1", 50, 50 + P), bias=cBG)
    lin(R("MX"), R("DM", 0, 16), -2 * HUGE, HUGE)
    lin(R("OF", 24, 30, 2), JB(3), 4.0, cs)
    lin(R("OF", 25, 30, 2), JB(3), 4.0, cs)
    lin(R("OF", 30, 34), JB(4), 4.0, cPN)
    lin(R("OF", 34, 36), R("CF", 5, 7), 16.0, ca)
    lin(c1("OF", 36), ck, 32.0, cF)
    lin(c1("OF", 37), ck, 32.0, cF)
    lin(R("OF", 40, 42), R("CF", 0, 2), 4.0 * (1 + MERGE))
    lin(R("OF", 42, 44), R("OF", 38, 40), 4.0 / (1 + MERGE), -1.0)
    if MERGE:
        lin(R("OF", 44, 46), R("OF", 38, 40), bias=1.0)
    cp(R("OU", 24, 44 + 2 * MERGE), R("OF", 24, 44 + 2 * MERGE))
    lin(c64, ca, -1.0, M - 0.5)
    act(cL2, ca, Act.Relu, scale=100.0, bias=-100.0 * (CAP - 1))
    lin(cLM, cL2, -1.0, c64)
    fill(R("LM"), 32, cLM)
    ts(R("LMM"), R("JQ"), ck, cLM, Op.is_equal, Op.mult)
    ts(R("TA"), JB(8), cg, -EPS, Op.is_lt, Op.mult)
    ts(R("TB"), JB(8), cg, 4 * BIG, Op.is_equal, Op.mult)
    tt(R("TH8"), R("TA"), R("TB"), Op.add)
    ha, hb = ((me ^ k0) // 4 for k0, _ in PARTS)
    s0, s1 = 1 - 2 * (me & 1), 1 - (me & 2)
    pa, pb = ((64 * h, 64 * h + 64) for h in (ha, hb))
    lin(R("CD", 6, 7, 1, pa), R("CF", 2, 3, 1, pa), -float(S), float(HH))
    lin(R("CD", 12, 13, 1, pb), R("CF", 2, 3, 1, pb), float(S * s1), float(S * (1 + me % 4)))
    lin(R("CD", 6, 7, 1, pb), R("CF", 5, 6, 1, pb), float(S * (s0 - s1)), R("CD", 12, 13, 1, pb))
    lin(c1("PS"), ca, -4.0, cPS)
    lin(cZ, ck, bias=float(HH))

    pick("WQ", 0, 128, "Q0", oWQ, (0, NL), E1)
    for b in range(4):
        mm("P%d" % b, "QE", 128 * b, "Q0", NL - 128, NL, arrive=E1)
    mm("P4", "WQ", 0, "Q0", 0, 128)
    mm("P7", "WQ", 0, "C1", LZ, LZ + 128)
    lin(quad("AF", 0, 0, K1), quad("P7", 0, ZC, 128), q="a")
    for b in range(4):
        lin(R("DH", 8 * b + 1, 8 * b + 8), R("P%d" % b, 128 - 2 * N + 3, 128, 2), q=DHQ[b])
    got = []
    for (ks, via, buf, sends), bank in zip(GROUPS, ("P5", "P6", "P0")):
        for k in ks:
            children(k)
        a, b = made(ks[0]), made(ks[-1]) + K1
        quant("C1", a, b, "X1")
        mm(bank, "WQ", 0, "C1", a, b)
        for q in sorted(set(k // 2 for k in ks)):
            in_q = [k for k in ks if k // 2 == q]
            lin(quad("AF", q, K1 * (in_q[0] % 2), K1 * (in_q[-1] % 2 + 1)),
                quad(bank, q, made(in_q[0]) - a, made(in_q[-1]) + K1 - a), q="a")
        if via:
            relay("C1", buf, via, K1, made, [(k, "C1", OWN + K1 * k, "p1") for k in sends])
            got.append(handed(via) + len(off) * len(sends))
            continue
        for x, cast in both:
            direct("C1" + x, "C1" + x, cast, K1, made, lambda k: OWN + K1 * k, sends, "p1")
        got.append(landed(sends))
    P1 = (("p1", 2 * sum(got)),)
    tt(R("M0"), R("P4", 0, 32), R("DM", 0, 32), Op.mult)
    cp(R("AS"), R("P4", 0, 32))
    scan(R("BS0"), R("RR", 0, 96, 3), R("M0"))
    for s in range(2):
        ts(R("D0", P * s, P * s + P), R("AS", 0, P), c1("BS0", 16 * s + 15), None, Op.subtract)
    tt(R("CM0", 0, 48), R("D0"), R("TH0"), Op.is_gt)
    scan(R("SN0", 0, 49), R("RR", 24, 73), R("CM0", 0, 49))
    cp(R("OL0"), R("SN0", 23, 49, 25))
    cp(by(R("SS0"), R("OL0")), R("AS"))
    cp(by(R("SR0"), R("OL0")), R("PY0"))
    scan(R("NS"), R("MX"), R("SS0", 0, 16), Op.min, Op.max)
    tt(R("SE", 0, 12), R("SR0", 0, 12), R("MK", 0, 12), Op.mult)
    scan(R("SF", 0, 12), R("RR", 0, 144, 12), R("SE", 0, 12))
    ts(R("OA", 0, 3), R("SF", 3, 12, 4), cOA, None, Op.add)
    mm("P3", "WQ", 0, "LC", 0, NO, arrive=E2)
    for a, b, o in ((0, P * me, Op.is_ge), (P * me, NO, Op.is_gt)):
        if a < b:
            ts(R("CG", a, b), R("P3", a, b), c1("NS", 15), None, o)
        else:
            op("v", None)
    scan(R("CH"), R("CG"), R("CG"), Op.add, Op.max)
    ts(R("FL0"), R("LM"), c1("CH", NO - 1), 2 * BIG, Op.subtract, Op.mult)
    tr(R("FT0"), R("FL0"))

    lin(R("PEN"), by(R("AF"), R("OA", 0, 3)))
    tt(R("A1"), by(R("FT0"), oPN), R("PEN"), Op.min)
    tt(R("M1"), R("PEN"), R("DM"), Op.mult)
    scan(R("BS1"), R("RR", 0, 144, 3), R("M1"))
    act(R("JK"), by(R("FT0"), oPN), Act.Sign, acc=c1("NI"))
    ts(R("IW", 0, 3), R("I3", 4, 7), c1("NI"), None, Op.is_ge)
    tt(R("IV", 0, 3), R("IW", 0, 3), R("I3", 0, 3), Op.mult)
    for s in range(3):
        own = c1("BS1", 16 * s + 15)
        act(R("D1", 48 * s, 48 * s + 48), R("A1"), Act.Sign, scale=-1.0, bias=own, acc=c1("EQ", 50 * s + 48))
        ts(R("EQ", 50 * s, 50 * s + 48), R("A1"), own, None, Op.is_equal)
    scan(R("SN1"), R("FM"), R("EQ"))
    for s in range(3):
        ts(c1("OL1", s), c1("SN1", 50 * s + 49), -0.5, c1("IV", s), Op.mult, Op.max)
    lin(R("PB"), by(R("NT"), R("OA", 0, 3)))
    cp(by(R("SR1"), R("OL1", 0, 3)), R("PB"))
    cp(by(R("SS1"), R("OL1", 0, 3)), R("A1"))
    tt(R("SV"), by(R("FT0"), oSV), R("SR0", 0, 16), Op.min)
    act(R("G0", 32, 128), by(R("SV"), oG), Act.Relu)
    fill(R("G0", 0, 32), 32, c1("NI"))
    tr(R("GT0"), R("G0"))
    lin(R("G1"), by(R("SR1"), oG))
    at = PIECE["SS1"][1] - 16 * (me % 2)
    tr(R("GT1", 0, 32), R("WA", at, at + 32))
    tr(R("GT1", 32, 128), R("G1"))
    for j in range(2):
        if MERGE:
            lin(R("MS", 1 - j, 64, 2), by(R("GT%d" % j), oF))
            spread("MS", 1 - j, 16, 2)
            if j:
                for p in PARTS:
                    direct("MS", "ML", same, 8, lambda k: 8 * k, lambda k: 8 * me, range(*p), "m1")
                lin(R("ML", 8 * me, 8 * me + 8), R("MS", 0, 8))
            continue
        lin(R("MS", 32 * j, 32 * j + 32), by(R("GT%d" % j), oF))
        spread("MS", 32 * j, 8, 1)
        for p in PARTS:
            direct("MS", "ML", same, 4, lambda k: 32 * j + 4 * k, lambda k: 32 * j + 4 * me, range(*p), "m%d" % j)
        lin(R("ML", 32 * j + 4 * me, 32 * j + 4 * me + 4), R("MS", 32 * j, 32 * j + 4))
    M0, M1 = ((("m%d" % max(j, MERGE), landed(*[range(*p) for p in PARTS])),) for j in range(2))
    L0, L1, S1 = (R("ML"), R("ML"), R("MS")) if MERGE else (R("ML", 0, 32), R("ML", 32, 64), R("MS", 32, 64))
    ts(R("LE"), by(S1, oU), 4.0, ck, Op.mult, Op.add)
    tt(R("LF"), by(S1, oU0), R("KF"), Op.add)
    cp(R("LO"), R("LF"))
    rest = [k for k in range(*PARTS[0]) if k not in VIA2]
    PA = (("pa", 2 * (landed(rest) + handed(VIA2))),)
    n = 12 // NPE
    for j in range(NPE):
        pick("PE", HH + 16 * n * j, HH + 16 * n * (j + 1), "Q2", R("LE", 12 + n * j, 12 + n * (j + 1)))
    if VIA2:
        relay("PE", "R2", VIA2, S, lambda k: S * k)
    for x, cast in both:
        direct("PE" + x, "L2" + x, cast, S, lambda k: S * k, lambda k: S * (me % 4), rest, "pa")
    pick("PE", 0, HH, "Q2", R("LE", 0, 12))
    pick("PV", 0, HH, "C1", R("LO", 0, 12), (0, OWN + K1))
    for src in ("PE", "PV"):
        for b in (0, 2, 1, 3):
            mm("P%d" % b, "QE", 128 * b, src, 0, HH, src == "PE", src == "PV")

    def two(k):
        return HB + S * k + (16 if k else 0)

    for b in (2, 0, 3, 1):
        for k in range(4):
            lin(R("X2", 4 * two(k) + b, 4 * (two(k) + S), 4), R("P%d" % b, S * k, S * (k + 1)), bias=shift(k, b),
                q="a" if b > 1 else "v")
    quant("C2", HB, HA, "X2")
    for x, cast in both:
        direct("C2" + x, "C2" + x, cast, S, two, lambda k: HB - S * k, range(4), "pb")
    PB = (("pb", 2 * landed(range(4))),)

    low, banks, cSA = (0, 32), ("P6", "P7", "P0", "P1"), c1("LX", 32)

    def halfof(name, h, base=0):
        return R(name, base + HH * h, base + HH * (h + 1))

    ts(R("LP"), by(L0, oU1), ck, None, Op.add, arrive=M0)
    tt(R("LX"), by(L1, oUS), R("BQ"), Op.add, arrive=M1)
    n = 24 // NP1
    for j in range(NP1):
        pick("P1", 16 * n * j, 16 * n * (j + 1), "C1", R("LP", n * j, n * (j + 1)), (LZ, None), arrive=P1)
        mm(("P4", "P2")[j], "WM", 0, "P1", 16 * n * j, 16 * n * (j + 1))
    mm("P5", "QW", 0, "P1", 0, NP)
    lin(R("YS", 0, NP), R("P5", 0, NP), q="a")
    out = [dma("s", T.y[:, 0:NP], R("YS", 0, NP))]
    cp(R("LV"), R("LX", 0, 32))
    n = 12 // NVP
    for j in range(NVP):
        pick("PV", HH + 16 * n * j, HH + 16 * n * (j + 1), "C1", R("LV", 12 * ha + n * j, 12 * ha + n * (j + 1)), (LZ, None), P1)
    for b in range(4):
        mm(banks[b], "QE", 128 * b, "PV", HH, NP, True, False)
    for b in range(4):
        mm(banks[b], "QE", 128 * b, "L2", 0, HH, False, True, PA)
    for b in range(4):
        lin(R("X2", 4 * HA + b, 4 * (HA + HH), 4), R(banks[b], 0, HH), bias=shift(0, b), q=AQ[b])
    quant("C2", HA, HA + HH + 4, "X2")
    ts(R("ZF"), R("TH8"), cSA, 0.0, Op.add, Op.is_lt)
    lin(R("ZE"), R("ML", 1, 64, 8) if MERGE else R("ML", 0, 32, 4), 0.5, -S / 2, arrive=M0)
    tt(R("CA", NP), R("ZF"), R("ZE"), Op.mult)
    for q in range(N):
        j, at = divmod(q, N // NP1)
        ts(R("CA", S * q, S * (q + 1)), R(("P4", "P2")[j], S * at, S * (at + 1)), cSA, c1("TH8", q), Op.subtract, Op.is_gt)
    scan(R("CB"), R("CA"), R("CA"), Op.add, Op.max)
    ts(R("FV"), R("LMM"), c1("CB", NP + 7), c1("PS"), Op.is_gt, Op.mult)
    tr(R("FT"), R("FV"))
    scan(R("FS"), R("R4"), R("FT"), Op.min)
    spread("FS", 3, 32, 4)
    ts(R("LQ"), by(R("FS"), oLQ), -1.0, cZ, Op.mult, Op.add)
    for h, win, bank, arrive, q in ((hb, (0, HH + 16), "P2", PB, YQ[0]), (ha, (HA, None), "P3", (), YQ[1])):
        pick("OC", HH * h, HH * (h + 1), "C2", R("LQ", 12 * h, 12 * h + 12), win, arrive)
        mm(bank, "QW", 0, "OC", HH * h, HH * (h + 1))
        out.append(dma("s", T.oc[:, 4 * HH * h:4 * HH * (h + 1)], u8(halfof("OCc", h))))
        lin(halfof("YS", h, NP), R(bank, 0, HH), q=q)
        out.append(dma("s", T.y[:, NP + HH * h:NP + HH * (h + 1)], halfof("YS", h, NP)))
    oa = [dma("a", T.osc[4 * q:4 * q + 4, :], R("OCs", 0, NP, 1, (32 * q, 32 * q + 4))) for q in range(4)]
    tt(R("N1"), by(L0, oU1), R("BQ", 0, 32), Op.subtract, arrive=M0)
    ts(R("N1B", p=low), R("N1", p=low), R("CF", 4, 5, 1, low), -1.0, Op.add, Op.max)
    tr(R("N1T", p=low), R("N1B", p=low))
    out.append(dma("s", T.nm[0:1, 0:NP], R("N1T", 0, 16, 1, (0, P))))
    lin(R("T2N"), by(L1, oU), 4.0, ck, arrive=M1)
    lin(R("N2"), by(R("FS"), oLQ), 1000.0, -1.0)
    tt(R("N2B", p=low), R("N2", p=low), R("T2N", p=low), Op.min)
    tr(R("N2T", p=low), R("N2B", p=low))
    out.append(dma("s", T.nm[0:1, NP:2 * NP], R("N2T", 0, 16, 1, (0, P))))
    op("s", None, after=out)
    op("a", None, after=oa)
    op("g", None, arrive=(("sent", sent[0]),), behind=[i for i, o in enumerate(ops) if o["q"] == "g"])
    ops = _given(ops, ORDER) if len(ORDER) == len(ops) else _order(ops)

    known, at_issue, waits, needed = {q: 0 for q in queues}, [], [], set()
    for i, o in enumerate(ops):
        mine = []
        for d in o["deps"]:
            if not known[o["q"]] >> d & 1:
                mine.append(d)
                known[o["q"]] |= 1 << d | at_issue[d]
        needed.update(mine)
        waits.append(mine)
        at_issue.append(known[o["q"]])
    turn, count, before, mark, seen = {q: 0 for q in POOL}, {}, {}, {}, {q: set() for q in queues}
    for i, o in enumerate(ops):
        eng = queues[o["q"]]
        for d in waits[i]:
            eng.wait_ge(T.sem[mark[d][0]], mark[d][1])
        for sem, val in o["arrive"]:
            if (sem, val) not in seen[o["q"]]:
                seen[o["q"]].add((sem, val))
                eng.wait_ge(T.sem[sem], val)
        if o["fn"] is None:
            continue
        if i not in needed:
            o["fn"]()
            continue
        pool = "d" if o["dma"] else o["q"]
        name = "x%s%d" % (pool, turn[pool] % POOL[pool])
        turn[pool] += 1
        if name in before and not at_issue[i] >> before[name] & 1:
            eng.wait_ge(T.sem[name], count[name])
        step = 16 if o["dma"] else 1
        count[name] = count.get(name, 0) + step
        before[name] = i
        mark[i] = (name, count[name])
        o["fn"]().then_inc(T.sem[name], step)
